import numpy as np
import ml_dtypes


def mxq(x, axis, fmt="e4m3"):
    dtype, down = {"e4m3": (ml_dtypes.float8_e4m3fn, 7), "e5m2": (ml_dtypes.float8_e5m2, 14)}[fmt]
    v = np.moveaxis(np.asarray(x, np.float32).astype(ml_dtypes.bfloat16).astype(np.float64), axis, -1)
    blocks = v.reshape(v.shape[:-1] + (-1, 32))
    amax = np.abs(blocks).max(-1, keepdims=True)
    byte = np.maximum(np.where(amax > 0, np.frexp(amax)[1] - 1 + 127, 0) - down, 1)
    scale = np.exp2(byte - 127.0)
    codes = (blocks / scale).astype(np.float32).astype(dtype).astype(np.float64)
    return np.moveaxis((codes * scale).reshape(v.shape), -1, axis)


WIDE = False


def mx_kscale(k):
    if not WIDE:
        return np.ones(k)
    levels = np.array([24, -24, 12, -12, 0])
    if k % 512:
        return np.exp2(np.random.permutation(np.resize(levels, k // 32))).repeat(32)
    a = np.empty((k // 512, 16))
    for p in range(k // 512):
        a[p, :8] = np.random.permutation(np.resize(levels, 8))
        for g in range(8):
            far = levels[np.abs(levels - a[p, g]) >= 10]
            a[p, g + 8] = far[np.random.randint(len(far))]
    return np.exp2(a.ravel()).repeat(32)


def f64(x):
    return np.asarray(x).astype(np.float64)


def striped(idx):
    return np.tile(idx.reshape(-1, 16).T, (8, 1)).astype(np.uint16)


def unstriped(offs):
    return offs[:16].T.reshape(-1).astype(np.int64)


E2M1 = np.array([0.0, 0.5, 1.0, 1.5, 2.0, 3.0, 4.0, 6.0, -0.0, -0.5, -1.0, -1.5, -2.0, -3.0, -4.0, -6.0])


def pack_weight(w, fmt):
    k, n = w.shape
    w = f64(np.asarray(w, np.float32).astype(ml_dtypes.bfloat16)).reshape(k // 32, 32, n)
    amax = np.abs(w).max(1)
    if fmt == "e4m3":
        byte = np.frexp(amax)[1] - 1 + 127 - 7
    else:
        mant, ex = np.frexp(amax / 6.0)
        byte = np.where(mant > 0.5, ex, ex - 1) + 127
    byte = np.clip(np.where(amax > 0, byte, 1), 1, 254)
    scaled = (w * np.exp2(127.0 - byte)[:, None, :]).reshape(k, n).astype(np.float32)
    by_word = np.ascontiguousarray(scaled.reshape(k // 512, 128, 4, n).transpose(0, 1, 3, 2))
    if fmt == "e4m3":
        words = by_word.astype(ml_dtypes.float8_e4m3fn).view(np.uint8)
    else:
        c = by_word.astype(ml_dtypes.float4_e2m1fn).view(np.uint8) & 0xF
        words = (c[..., 0::2] | (c[..., 1::2] << 4)).reshape(k // 512, 128, 2 * n)
    return np.ascontiguousarray(words), np.ascontiguousarray(byte.astype(np.uint8).reshape(k // 512, 16, n))


def unpack_weight(words, scales, fmt):
    g, _, n = scales.shape
    words = np.ascontiguousarray(words).reshape(g, 128, n, -1)
    if fmt == "e4m3":
        vals = words.view(ml_dtypes.float8_e4m3fn).astype(np.float64)
    else:
        nib = np.empty((g, 128, n, 4), np.uint8)
        nib[..., 0::2] = words & 0xF
        nib[..., 1::2] = words >> 4
        vals = E2M1[nib]
    vals = vals * np.repeat(np.exp2(scales.astype(np.float64) - 127.0), 8, axis=1)[..., None]
    return vals.transpose(0, 1, 3, 2).reshape(g * 512, n)


def pack_table4(v):
    words, scales = pack_weight(v, "e2m1")
    g, t = words.shape[0] // 2, v.shape[1]
    return np.ascontiguousarray(words.reshape(g, 2, 128, t, 2).transpose(0, 2, 3, 1, 4).reshape(g, 128, t, 4)), scales


def unpack_table4(words, scales):
    g, _, t, _ = words.shape
    return unpack_weight(words.reshape(g, 128, t, 2, 2).transpose(0, 3, 1, 2, 4).reshape(2 * g, 128, 2 * t), scales, "e2m1")


def planes(y):
    n, m = y.shape
    v = y.astype(np.float32).astype(ml_dtypes.bfloat16).astype(np.float64).reshape(n // 32, 32, m)
    top = np.abs(v).max(1)
    byte = np.clip(np.where(top > 0, np.frexp(top)[1] - 1 + 127 - 7, 1), 1, 254)
    codes = (v * np.exp2(127.0 - byte)[:, None, :]).reshape(n, m).astype(np.float32).astype(ml_dtypes.float8_e4m3fn).view(np.uint8)
    words = codes.reshape(n // 512, 128, 4, m).transpose(0, 1, 3, 2)
    return np.ascontiguousarray(words), np.ascontiguousarray(byte.astype(np.uint8).reshape(n // 512, 16, m))


def sigm(f):
    return 1.0 / (1.0 + np.exp(-np.maximum(f, -700.0)))


K, N, T, J = 1024, 512, 2048, 1024


def setup_inputs():
    n = np.random.standard_normal
    s = mx_kscale(K)[:, None]
    p_tab = pack_table4(n((K, T)) * s)
    p_wa = pack_weight(n((K, N)) / np.sqrt(2 * K) / s, "e4m3")
    p_wb = pack_weight(n((K, N)) / np.sqrt(2 * K) / s, "e2m1")
    return {
        "tab_words": p_tab[0],
        "tab_scales": p_tab[1],
        "wa_words": p_wa[0],
        "wa_scales": p_wa[1],
        "wb_words": p_wb[0],
        "wb_scales": p_wb[1],
        "wc": (n((K, N)) / np.sqrt(K) / s).astype(np.float32),
        "wgo": np.tile(np.random.uniform(0.5, 2.0, J), (128, 1)).astype(np.float32),
        "offs": striped(np.random.permutation(T)[:J]),
        "offs2": striped(np.random.permutation(T)[:J]),
    }


def reference(tab_words, tab_scales, wa_words, wa_scales, wb_words, wb_scales, wc, wgo, offs, offs2):
    idx = unstriped(offs)
    idx2 = unstriped(offs2)
    tab_ = unpack_table4(tab_words, tab_scales)[:, idx]
    tabb_ = unpack_table4(tab_words, tab_scales)[:, idx2]
    wa_ = unpack_weight(wa_words, wa_scales, "e4m3")
    wb_ = unpack_weight(wb_words, wb_scales, "e2m1")
    za = wa_.T @ tabb_ + wb_.T @ tab_
    eta = sigm(za)
    wc_ = mxq(f64(wc), 0, "e4m3")
    ms = wc_.T @ tab_
    out = np.zeros((N, T))
    out[:, idx2] = f64(wgo)[0] * (eta * ms)
    return (out,) + planes(out)

@@ -1,0 +1,286 @@
+from contextlib import ExitStack
+
+import concourse.mybir as mybir
+from concourse.masks import make_identity
+
+K, N, T, J = 1024, 512, 2048, 1024
+FLOPS = 3 * 2 * K * N * J
+
+F32 = mybir.dt.float32
+BF16 = mybir.dt.bfloat16
+I32 = mybir.dt.int32
+U32 = mybir.dt.uint32
+U16 = mybir.dt.uint16
+U8 = mybir.dt.uint8
+FP8X4 = mybir.dt.float8_e4m3fn_x4
+FP4X4 = mybir.dt.float4_e2m1fn_x4
+MULT = mybir.AluOpType.mult
+COPY = mybir.ActivationFunctionType.Copy
+SIGMOID = mybir.ActivationFunctionType.Sigmoid
+
+P = 128
+PACK = 4
+PASSES = K // (P * PACK)
+HALF = 512
+HALVES = J // HALF
+SHIFT_ROWS = 112
+CHUNKS = ((0, 512, "v"), (512, 512, "v"), (1024, 512, "s"), (1536, 256, "s"), (1792, 256, "s"))
+
+
+def tile_list_rgg_noneP_kernel(
+    tc, tab_words, tab_scales, wa_words, wa_scales, wb_words, wb_scales, wc, wgo, offs, offs2, out_0, out_1, out_2
+):
+    nc = tc.nc
+    with ExitStack() as ctx:
+        keep = ctx.enter_context(tc.tile_pool(name="keep", bufs=1))
+        ps_gate = ctx.enter_context(tc.psum_pool(name="ps_gate", bufs=2))
+        ps_msg = ctx.enter_context(tc.psum_pool(name="ps_msg", bufs=4))
+        ps_turn = ctx.enter_context(tc.psum_pool(name="ps_turn", bufs=2))
+
+        def sb(name, shape, dtype, slot_of=None):
+            return keep.tile(shape, dtype, name=name, tag=slot_of or name, align_bytes=64)
+
+        lists = [sb("offs_sb", [P, J // 16], U16), sb("offs2_sb", [P, J // 16], U16)]
+        tab_s = sb("tab_s", [P, T], U8)
+        tab_w = sb("tab_w", [P, T], U32)
+        w_s_raw = sb("w_s_raw", [P, 2 * N], U8)
+        w_s = [sb("w_s0", [P, 2 * N], U8), sb("w_s1", [P, 2 * N], U8)]
+        v_s = [[sb("v_s%d%d" % (l, a), [P, J], U8) for a in range(PASSES)] for l in range(2)]
+        wc_raw = [sb("wc_raw%d" % a, [P, PACK, N], F32) for a in range(PASSES)]
+        wa_raw = sb("wa_raw", [P, PASSES, N], I32)
+        wb_raw = sb("wb_raw", [P, PASSES, 2 * N], U8)
+        wgo_rows = sb("wgo_rows", [P, P], F32)
+        wgo_col = sb("wgo_col", [P, J // P], F32)
+        ident = sb("ident", [P, P], F32)
+
+        nc.vector.memset(tab_s[:].bitcast(I32), 0)
+        nc.vector.memset(w_s_raw[:].bitcast(I32), 0)
+        nc.vector.memset(wgo_rows[:], 0.0)
+        for plane in (v_s[0][1], v_s[1][1], w_s[1]):
+            nc.vector.memset(plane[:].bitcast(I32), 0)
+        make_identity(nc, ident[:])
+
+        def load_scale_rows(dst, src, q):
+            nc.sync.dma_start(out=dst[32 * q : 32 * q + 8, :].bitcast(I32), in_=src[:, 4 * q : 4 * q + 4, :].bitcast(I32))
+
+        def load_wc(a):
+            nc.sync.dma_start(out=wc_raw[a][:], in_=wc[512 * a : 512 * (a + 1), :].rearrange("(p i) n -> p i n", i=PACK))
+
+        nc.sync.dma_start(lists[0][:], offs)
+        nc.sync.dma_start(lists[1][:], offs2)
+        for q in range(4):
+            load_scale_rows(tab_s, tab_scales, q)
+        load_wc(0)
+        nc.sync.dma_start(out=tab_w[:].bitcast(I32), in_=tab_words[0].rearrange("p t b -> p (t b)").bitcast(I32))
+        for q in range(3):
+            load_scale_rows(w_s_raw[:, 0:N], wa_scales, q)
+            load_scale_rows(w_s_raw[:, N : 2 * N], wb_scales, q)
+        load_wc(1)
+        nc.sync.dma_start(out=wa_raw[:], in_=wa_words.rearrange("a p n i -> p a (n i)").bitcast(I32))
+        load_scale_rows(w_s_raw[:, 0:N], wa_scales, 3)
+        load_scale_rows(w_s_raw[:, N : 2 * N], wb_scales, 3)
+        nc.sync.dma_start(out=wb_raw[:].bitcast(I32), in_=wb_words.rearrange("a p c -> p a c").bitcast(I32))
+        nc.sync.dma_start(out=wgo_rows[0 : J // P, :], in_=wgo[0].rearrange("(c m) -> c m", m=P))
+
+        def shift_down(dst, src):
+            nc.sync.dma_start(out=dst[0:SHIFT_ROWS, :].bitcast(I32), in_=src[4 : 4 + SHIFT_ROWS, :].bitcast(I32))
+
+        for l in range(2):
+            nc.vector.tensor_copy(v_s[l][0][:], tab_s[:].indirect(lists[l][:]))
+            shift_down(v_s[l][1], v_s[l][0])
+
+        wgo_ps = ps_turn.tile([P, HALF], F32, name="turn_ps")
+        nc.tensor.transpose(wgo_ps[:, 0:P], wgo_rows[:], ident[:])
+        nc.scalar.copy(out=wgo_col[:], in_=wgo_ps[:, 0 : J // P])
+
+        wc16 = [sb("wc16_%d" % a, [P, N * PACK], BF16) for a in range(PASSES)]
+        wc_q = [sb("wc_q%d" % a, [P, N], U32) for a in range(PASSES)]
+        wc_s = [sb("wc_s%d" % a, [P, N], U8) for a in range(PASSES)]
+        for a in range(PASSES):
+            nc.scalar.copy(
+                out=wc16[a][:].rearrange("p (c e i) -> p c i e", e=4, i=PACK),
+                in_=wc_raw[a][:].rearrange("p i (c e) -> p c i e", e=4),
+            )
+
+        v_w = [[sb("v_w%d%d" % (l, h), [P, PASSES, 2 * HALF], U8) for h in range(HALVES)] for l in range(2)]
+
+        def gather_words(l, h, slot_of=None):
+            both = sb("both%d%d" % (l, h), [P, HALF], U32, slot_of)
+            cols = slice(h * HALF // 16, (h + 1) * HALF // 16)
+            nc.vector.tensor_copy(both[:], tab_w[:].indirect(lists[l][:, cols]))
+            return both
+
+        def part_words(l, h, both):
+            nc.vector.tensor_copy(
+                out=v_w[l][h][:].bitcast(U16), in_=both[:].bitcast(U16).rearrange("p (j d) -> p d j", d=PASSES)
+            )
+
+        def quantize_wc(a):
+            nc.vector.quantize_mx(out=wc_q[a][:].bitcast(FP8X4), scales=wc_s[a][:], in_=wc16[a][:])
+
+        wa_q = sb("wa_q", [P, PASSES, N], I32)
+        wb_q = sb("wb_q", [P, PASSES, 2 * N], U8)
+
+        g00 = gather_words(0, 0)
+        nc.vector.tensor_copy(
+            out=w_s[0][:].rearrange("p (w t m) -> p w t m", w=2, t=PACK),
+            in_=w_s_raw[:].rearrange("p (w m t) -> p w t m", w=2, t=PACK),
+        )
+        shift_down(w_s[1], w_s[0])
+        g10 = gather_words(1, 0, "w_s_raw")
+        part_words(0, 0, g00)
+        quantize_wc(0)
+        part_words(1, 0, g10)
+        quantize_wc(1)
+        nc.vector.tensor_copy(
+            out=wa_q[:].rearrange("p a (t c e) -> p a c t e", t=PACK, e=4),
+            in_=wa_raw[:].rearrange("p a (c e t) -> p a c t e", t=PACK, e=4),
+        )
+        nc.vector.tensor_copy(
+            out=wb_q[:].bitcast(U16).rearrange("p a (t m) -> p a t m", t=PACK),
+            in_=wb_raw[:].bitcast(U16).rearrange("p a (m t) -> p a t m", t=PACK),
+        )
+        g01 = gather_words(0, 1, "wc16_1")
+        part_words(0, 1, g01)
+        g11 = gather_words(1, 1, "wb_raw")
+        part_words(1, 1, g11)
+
+        pages = [sb("page0", [P, T], F32)]
+        nc.vector.memset(pages[0][:], 0.0)
+
+        msg_t = [sb("msg_t%d" % h, [P, HALF // P, N], F32) for h in range(HALVES)]
+        eta = [sb("eta%d" % t, [P, J], F32) for t in range(PACK)]
+        msg = [sb("msg%d" % t, [P, J], F32) for t in range(PACK)]
+
+        def message_rows(h):
+            for b in range(HALF // P):
+                acc = ps_msg.tile([P, N], F32, name="msg_ps")
+                j0 = h * HALF + b * P
+                for a in range(PASSES):
+                    nc.tensor.matmul_mx(
+                        out=acc[:],
+                        lhsT=v_w[0][h][:, a, 2 * b * P : 2 * (b + 1) * P].bitcast(FP4X4),
+                        lhsT_scale=v_s[0][a][:, j0 : j0 + P],
+                        rhs=wc_q[a][:].bitcast(FP8X4),
+                        rhs_scale=wc_s[a][:],
+                        start=(a == 0),
+                        stop=(a == PASSES - 1),
+                    )
+                c = j0 // P
+                nc.scalar.activation(
+                    out=msg_t[h][:, b, :].rearrange("p (t m) -> p t m", t=PACK),
+                    in_=acc[:].rearrange("p (m t) -> p t m", t=PACK),
+                    func=COPY,
+                    scale=wgo_col[:, c : c + 1],
+                )
+
+        def gate(t, h):
+            acc = ps_gate.tile([P, HALF], F32, name="gate_ps")
+            js = slice(h * HALF, (h + 1) * HALF)
+            for a in range(PASSES):
+                nc.tensor.matmul_mx(
+                    out=acc[:],
+                    lhsT=wb_q[:, a, 2 * t * P : 2 * (t + 1) * P].bitcast(FP4X4),
+                    lhsT_scale=w_s[a][:, N + t * P : N + (t + 1) * P],
+                    rhs=v_w[0][h][:, a, :].bitcast(FP4X4),
+                    rhs_scale=v_s[0][a][:, js],
+                    start=(a == 0),
+                    stop=False,
+                )
+            for a in range(PASSES):
+                nc.tensor.matmul_mx(
+                    out=acc[:],
+                    lhsT=wa_q[:, a, t * P : (t + 1) * P].bitcast(FP8X4),
+                    lhsT_scale=w_s[a][:, t * P : (t + 1) * P],
+                    rhs=v_w[1][h][:, a, :].bitcast(FP4X4),
+                    rhs_scale=v_s[1][a][:, js],
+                    start=False,
+                    stop=(a == PASSES - 1),
+                )
+            nc.scalar.activation(out=eta[t][:, js], in_=acc[:], func=SIGMOID)
+
+        def turn_message(t, h):
+            turned = ps_turn.tile([P, HALF], F32, name="turn_ps")
+            for b in range(HALF // P):
+                nc.tensor.transpose(turned[:, b * P : (b + 1) * P], msg_t[h][:, b, t * P : (t + 1) * P], ident[:])
+            nc.scalar.copy(out=msg[t][:, h * HALF : (h + 1) * HALF], in_=turned[:])
+
+        def scatter(t, j0, j1):
+            nc.vector.tensor_tensor(
+                pages[t][:].indirect(lists[1][:, j0 // 16 : j1 // 16]), eta[t][:, j0:j1], msg[t][:, j0:j1], MULT
+            )
+
+        out_rows = out_0.rearrange("(p t) c -> p t c", t=PACK)
+        high16 = [sb("high16_%d" % i, [P, 2, w], BF16) for i, (c0, w, e) in enumerate(CHUNKS)]
+        y16 = [sb("y16_%d" % i, [P, w, PACK], BF16) for i, (c0, w, e) in enumerate(CHUNKS)]
+        y_q = sb("y_q", [P, T], U32)
+        y_s = sb("y_s", [P, T], U8)
+
+        for h in range(HALVES):
+            message_rows(h)
+            gate(0, h)
+            turn_message(0, h)
+            scatter(0, h * HALF, (h + 1) * HALF)
+        for t, slot_of in ((1, "wb_raw"), (2, "wc_q0"), (3, "wc_q1")):
+            pages.append(sb("page%d" % t, [P, T], F32, slot_of))
+            nc.gpsimd.memset(pages[t][:], 0.0)
+        for t in range(1, PACK):
+            for h in range(HALVES):
+                gate(t, h)
+                turn_message(t, h)
+        low16 = sb("low16", [P, 2, T], BF16, "msg_t1")
+        for t in range(PACK):
+            if t > 0:
+                scatter(t, 0, J)
+            nc.sync.dma_start(out=out_rows[:, t, :], in_=pages[t][:])
+            if t < 2:
+                nc.scalar.copy(out=low16[:, t, :], in_=pages[t][:])
+            if t == 1:
+                for i, (c0, w, e) in enumerate(CHUNKS):
+                    nc.scalar.copy(out=y16[i][:, :, 0:2], in_=low16[:, :, c0 : c0 + w].rearrange("p t c -> p c t"))
+            if t == 2:
+                for i, (c0, w, e) in enumerate(CHUNKS):
+                    nc.scalar.copy(out=high16[i][:, 0, :], in_=pages[2][:, c0 : c0 + w])
+
+        def finish(i):
+            c0, w, e = CHUNKS[i]
+            copy = nc.vector.tensor_copy if e == "v" else nc.scalar.copy
+            copy(out=high16[i][:, 1, :], in_=pages[3][:, c0 : c0 + w])
+
+        def weave(i):
+            c0, w, e = CHUNKS[i]
+            copy = nc.vector.tensor_copy if e == "v" else nc.scalar.copy
+            copy(out=y16[i][:, :, 2:4], in_=high16[i][:].rearrange("p t c -> p c t"))
+
+        codes_out = out_1[0].rearrange("p t b -> p (t b)").bitcast(I32)
+
+        def quantize_out(i):
+            c0, w, e = CHUNKS[i]
+            nc.vector.quantize_mx(
+                out=y_q[:, c0 : c0 + w].bitcast(FP8X4),
+                scales=y_s[:, c0 : c0 + w],
+                in_=y16[i][:].rearrange("p c t -> p (c t)"),
+            )
+
+        def store_codes(c0, c1):
+            nc.sync.dma_start(out=codes_out[:, c0:c1], in_=y_q[:, c0:c1].bitcast(I32))
+
+        finish(0)
+        finish(1)
+        for i in (2, 3, 4):
+            finish(i)
+            weave(i)
+        weave(0)
+        weave(1)
+        quantize_out(0)
+        quantize_out(1)
+        store_codes(0, 1024)
+        quantize_out(2)
+        store_codes(1024, 1536)
+        quantize_out(3)
+        quantize_out(4)
+        store_codes(1536, 2048)
+        for q in range(4):
+            nc.scalar.dma_start(
+                out=out_2[0, 4 * q : 4 * q + 4, :].bitcast(I32), in_=y_s[32 * q : 32 * q + 4, :].bitcast(I32)
+            )

@@ -43,18 +43,18 @@ def tile_list_rgg_noneP_kernel(
         lists = [sb("offs_sb", [P, J // 16], U16), sb("offs2_sb", [P, J // 16], U16)]
         tab_s = sb("tab_s", [P, T], U8)
         tab_w = sb("tab_w", [P, T], U32)
-        w_s_raw = sb("w_s_raw", [P, 2 * N], U8)
+        w_s_raw = [sb("wa_s_raw", [P, N], U8), sb("wb_s_raw", [P, N], U8)]
         w_s = [sb("w_s0", [P, 2 * N], U8), sb("w_s1", [P, 2 * N], U8)]
         v_s = [[sb("v_s%d%d" % (l, a), [P, J], U8) for a in range(PASSES)] for l in range(2)]
         wc_raw = [sb("wc_raw%d" % a, [P, PACK, N], F32) for a in range(PASSES)]
         wa_raw = sb("wa_raw", [P, PASSES, N], I32)
         wb_raw = sb("wb_raw", [P, PASSES, 2 * N], U8)
         wgo_rows = sb("wgo_rows", [P, P], F32)
-        wgo_col = sb("wgo_col", [P, J // P], F32)
         ident = sb("ident", [P, P], F32)
 
         nc.vector.memset(tab_s[:].bitcast(I32), 0)
-        nc.vector.memset(w_s_raw[:].bitcast(I32), 0)
+        for raw in w_s_raw:
+            nc.vector.memset(raw[:].bitcast(I32), 0)
         nc.vector.memset(wgo_rows[:], 0.0)
         for plane in (v_s[0][1], v_s[1][1], w_s[1]):
             nc.vector.memset(plane[:].bitcast(I32), 0)
@@ -71,27 +71,25 @@ def tile_list_rgg_noneP_kernel(
         for q in range(4):
             load_scale_rows(tab_s, tab_scales, q)
         load_wc(0)
-        nc.sync.dma_start(out=tab_w[:].bitcast(I32), in_=tab_words[0].rearrange("p t b -> p (t b)").bitcast(I32))
-        for q in range(3):
-            load_scale_rows(w_s_raw[:, 0:N], wa_scales, q)
-            load_scale_rows(w_s_raw[:, N : 2 * N], wb_scales, q)
         load_wc(1)
-        nc.sync.dma_start(out=wa_raw[:], in_=wa_words.rearrange("a p n i -> p a (n i)").bitcast(I32))
-        load_scale_rows(w_s_raw[:, 0:N], wa_scales, 3)
-        load_scale_rows(w_s_raw[:, N : 2 * N], wb_scales, 3)
-        nc.sync.dma_start(out=wb_raw[:].bitcast(I32), in_=wb_words.rearrange("a p c -> p a c").bitcast(I32))
+        nc.sync.dma_start(out=tab_w[:].bitcast(I32), in_=tab_words[0].rearrange("p t b -> p (t b)").bitcast(I32))
+        for q in range(4):
+            load_scale_rows(w_s_raw[0], wa_scales, q)
         nc.sync.dma_start(out=wgo_rows[0 : J // P, :], in_=wgo[0].rearrange("(c m) -> c m", m=P))
+        nc.sync.dma_start(out=wa_raw[:], in_=wa_words.rearrange("a p n i -> p a (n i)").bitcast(I32))
+        nc.sync.dma_start(out=wb_raw[:].bitcast(I32), in_=wb_words.rearrange("a p c -> p a c").bitcast(I32))
 
         def shift_down(dst, src):
             nc.sync.dma_start(out=dst[0:SHIFT_ROWS, :].bitcast(I32), in_=src[4 : 4 + SHIFT_ROWS, :].bitcast(I32))
 
-        for l in range(2):
+        def gather_scales(l):
             nc.vector.tensor_copy(v_s[l][0][:], tab_s[:].indirect(lists[l][:]))
             shift_down(v_s[l][1], v_s[l][0])
 
-        wgo_ps = ps_turn.tile([P, HALF], F32, name="turn_ps")
-        nc.tensor.transpose(wgo_ps[:, 0:P], wgo_rows[:], ident[:])
-        nc.scalar.copy(out=wgo_col[:], in_=wgo_ps[:, 0 : J // P])
+        gather_scales(0)
+        for q in range(4):
+            load_scale_rows(w_s_raw[1], wb_scales, q)
+        gather_scales(1)
 
         wc16 = [sb("wc16_%d" % a, [P, N * PACK], BF16) for a in range(PASSES)]
         wc_q = [sb("wc_q%d" % a, [P, N], U32) for a in range(PASSES)]
@@ -102,17 +100,21 @@ def tile_list_rgg_noneP_kernel(
                 in_=wc_raw[a][:].rearrange("p i (c e) -> p c i e", e=4),
             )
 
-        v_w = [[sb("v_w%d%d" % (l, h), [P, PASSES, 2 * HALF], U8) for h in range(HALVES)] for l in range(2)]
+        wgo_col = sb("wgo_col", [P, J // P], F32, "wc_raw1")
+        wgo_ps = ps_turn.tile([P, HALF], F32, name="turn_ps")
+        nc.tensor.transpose(wgo_ps[:, 0:P], wgo_rows[:], ident[:])
+        nc.scalar.copy(out=wgo_col[:], in_=wgo_ps[:, 0 : J // P])
 
-        def gather_words(l, h, slot_of=None):
-            both = sb("both%d%d" % (l, h), [P, HALF], U32, slot_of)
+        v_w = [[None] * HALVES for l in range(2)]
+
+        def gather_words(l, h, both):
             cols = slice(h * HALF // 16, (h + 1) * HALF // 16)
-            nc.vector.tensor_copy(both[:], tab_w[:].indirect(lists[l][:, cols]))
-            return both
+            nc.vector.tensor_copy(both, tab_w[:].indirect(lists[l][:, cols]))
 
         def part_words(l, h, both):
+            v_w[l][h] = sb("v_w%d%d" % (l, h), [P, PASSES, 2 * HALF], U8)
             nc.vector.tensor_copy(
-                out=v_w[l][h][:].bitcast(U16), in_=both[:].bitcast(U16).rearrange("p (j d) -> p d j", d=PASSES)
+                out=v_w[l][h][:].bitcast(U16), in_=both.bitcast(U16).rearrange("p (j d) -> p d j", d=PASSES)
             )
 
         def quantize_wc(a):
@@ -121,17 +123,17 @@ def tile_list_rgg_noneP_kernel(
         wa_q = sb("wa_q", [P, PASSES, N], I32)
         wb_q = sb("wb_q", [P, PASSES, 2 * N], U8)
 
-        g00 = gather_words(0, 0)
-        nc.vector.tensor_copy(
-            out=w_s[0][:].rearrange("p (w t m) -> p w t m", w=2, t=PACK),
-            in_=w_s_raw[:].rearrange("p (w m t) -> p w t m", w=2, t=PACK),
-        )
-        shift_down(w_s[1], w_s[0])
-        g10 = gather_words(1, 0, "w_s_raw")
-        part_words(0, 0, g00)
         quantize_wc(0)
-        part_words(1, 0, g10)
+        first = sb("first", [P, HALF], U32, "wc16_0")
+        gather_words(0, 0, first[:])
+        part_words(0, 0, first[:])
         quantize_wc(1)
+        for w in range(2):
+            nc.vector.tensor_copy(
+                out=w_s[0][:, w * N : (w + 1) * N].rearrange("p (t m) -> p t m", t=PACK),
+                in_=w_s_raw[w][:].rearrange("p (m t) -> p t m", t=PACK),
+            )
+        shift_down(w_s[1], w_s[0])
         nc.vector.tensor_copy(
             out=wa_q[:].rearrange("p a (t c e) -> p a c t e", t=PACK, e=4),
             in_=wa_raw[:].rearrange("p a (c e t) -> p a c t e", t=PACK, e=4),
@@ -140,10 +142,14 @@ def tile_list_rgg_noneP_kernel(
             out=wb_q[:].bitcast(U16).rearrange("p a (t m) -> p a t m", t=PACK),
             in_=wb_raw[:].bitcast(U16).rearrange("p a (m t) -> p a t m", t=PACK),
         )
-        g01 = gather_words(0, 1, "wc16_1")
-        part_words(0, 1, g01)
-        g11 = gather_words(1, 1, "wb_raw")
-        part_words(1, 1, g11)
+        rest = sb("rest", [P, 3 * HALF], U32, "wb_s_raw")
+        third = [rest[:, i * HALF : (i + 1) * HALF] for i in range(3)]
+        gather_words(1, 0, third[0])
+        gather_words(0, 1, third[1])
+        part_words(1, 0, third[0])
+        part_words(0, 1, third[1])
+        gather_words(1, 1, third[2])
+        part_words(1, 1, third[2])
 
         pages = [sb("page0", [P, T], F32)]
         nc.vector.memset(pages[0][:], 0.0)
@@ -153,12 +159,12 @@ def tile_list_rgg_noneP_kernel(
         msg = [sb("msg%d" % t, [P, J], F32) for t in range(PACK)]
 
         def message_rows(h):
-            for b in range(HALF // P):
-                acc = ps_msg.tile([P, N], F32, name="msg_ps")
-                j0 = h * HALF + b * P
-                for a in range(PASSES):
+            accs = [ps_msg.tile([P, N], F32, name="msg_ps") for b in range(HALF // P)]
+            for a in range(PASSES):
+                for b in range(HALF // P):
+                    j0 = h * HALF + b * P
                     nc.tensor.matmul_mx(
-                        out=acc[:],
+                        out=accs[b][:],
                         lhsT=v_w[0][h][:, a, 2 * b * P : 2 * (b + 1) * P].bitcast(FP4X4),
                         lhsT_scale=v_s[0][a][:, j0 : j0 + P],
                         rhs=wc_q[a][:].bitcast(FP8X4),
@@ -166,10 +172,11 @@ def tile_list_rgg_noneP_kernel(
                         start=(a == 0),
                         stop=(a == PASSES - 1),
                     )
-                c = j0 // P
+            for b in range(HALF // P):
+                c = h * HALF // P + b
                 nc.scalar.activation(
                     out=msg_t[h][:, b, :].rearrange("p (t m) -> p t m", t=PACK),
-                    in_=acc[:].rearrange("p (m t) -> p t m", t=PACK),
+                    in_=accs[b][:].rearrange("p (m t) -> p t m", t=PACK),
                     func=COPY,
                     scale=wgo_col[:, c : c + 1],
                 )
@@ -211,26 +218,36 @@ def tile_list_rgg_noneP_kernel(
             )
 
         out_rows = out_0.rearrange("(p t) c -> p t c", t=PACK)
-        high16 = [sb("high16_%d" % i, [P, 2, w], BF16) for i, (c0, w, e) in enumerate(CHUNKS)]
         y16 = [sb("y16_%d" % i, [P, w, PACK], BF16) for i, (c0, w, e) in enumerate(CHUNKS)]
         y_q = sb("y_q", [P, T], U32)
         y_s = sb("y_s", [P, T], U8)
 
+        for t, slot_of in ((1, "wb_s_raw"), (2, "wc_q0"), (3, "wc_q1")):
+            pages.append(None)
         for h in range(HALVES):
             message_rows(h)
-            gate(0, h)
-            turn_message(0, h)
-            scatter(0, h * HALF, (h + 1) * HALF)
-        for t, slot_of in ((1, "wb_raw"), (2, "wc_q0"), (3, "wc_q1")):
-            pages.append(sb("page%d" % t, [P, T], F32, slot_of))
+            if h == 0:
+                pages[1] = sb("page1", [P, T], F32, "wb_s_raw")
+                nc.gpsimd.memset(pages[1][:], 0.0)
+            for t in range(2):
+                turn_message(t, h)
+            for t in range(2):
+                gate(t, h)
+            for t in range(2):
+                scatter(t, h * HALF, (h + 1) * HALF)
+        for t, slot_of in ((2, "wc_q0"), (3, "wc_q1")):
+            pages[t] = sb("page%d" % t, [P, T], F32, slot_of)
             nc.gpsimd.memset(pages[t][:], 0.0)
-        for t in range(1, PACK):
+        for t in range(2, PACK):
+            for h in range(HALVES):
+                turn_message(t, h)
             for h in range(HALVES):
                 gate(t, h)
-                turn_message(t, h)
-        low16 = sb("low16", [P, 2, T], BF16, "msg_t1")
+        low16 = sb("low16", [P, 2, T], BF16, "msg_t0")
+        late_slots = ("wa_q", "wb_q", "w_s0", "w_s1", "v_w11")
+        high16 = [sb("high16_%d" % i, [P, 2, w], BF16, late_slots[i]) for i, (c0, w, e) in enumerate(CHUNKS)]
         for t in range(PACK):
-            if t > 0:
+            if t > 1:
                 scatter(t, 0, J)
             nc.sync.dma_start(out=out_rows[:, t, :], in_=pages[t][:])
             if t < 2:

@@ -24,7 +24,9 @@ PASSES = K // (P * PACK)
 HALF = 512
 HALVES = J // HALF
 SHIFT_ROWS = 112
-CHUNKS = ((0, 512, "v"), (512, 512, "v"), (1024, 512, "s"), (1536, 256, "s"), (1792, 256, "s"))
+VECTOR_CHUNKS = ((0, 512), (512, 256))
+SCALAR_CHUNKS = ((768, 512), (1280, 512), (1792, 256))
+SPLIT = 768
 
 
 def tile_list_rgg_noneP_kernel(
@@ -120,9 +122,6 @@ def tile_list_rgg_noneP_kernel(
         def quantize_wc(a):
             nc.vector.quantize_mx(out=wc_q[a][:].bitcast(FP8X4), scales=wc_s[a][:], in_=wc16[a][:])
 
-        wa_q = sb("wa_q", [P, PASSES, N], I32)
-        wb_q = sb("wb_q", [P, PASSES, 2 * N], U8)
-
         quantize_wc(0)
         first = sb("first", [P, HALF], U32, "wc16_0")
         gather_words(0, 0, first[:])
@@ -134,21 +133,23 @@ def tile_list_rgg_noneP_kernel(
                 in_=w_s_raw[w][:].rearrange("p (m t) -> p t m", t=PACK),
             )
         shift_down(w_s[1], w_s[0])
+        wa_q = sb("wa_q", [P, PASSES, N], I32, "wb_s_raw")
         nc.vector.tensor_copy(
             out=wa_q[:].rearrange("p a (t c e) -> p a c t e", t=PACK, e=4),
             in_=wa_raw[:].rearrange("p a (c e t) -> p a c t e", t=PACK, e=4),
         )
+        wb_q = sb("wb_q", [P, PASSES, 2 * N], U8, "wa_raw")
         nc.vector.tensor_copy(
             out=wb_q[:].bitcast(U16).rearrange("p a (t m) -> p a t m", t=PACK),
             in_=wb_raw[:].bitcast(U16).rearrange("p a (m t) -> p a t m", t=PACK),
         )
-        rest = sb("rest", [P, 3 * HALF], U32, "wb_s_raw")
+        rest = sb("rest", [P, 3 * HALF], U32, "wb_raw")
         third = [rest[:, i * HALF : (i + 1) * HALF] for i in range(3)]
         gather_words(1, 0, third[0])
         gather_words(0, 1, third[1])
         part_words(1, 0, third[0])
-        part_words(0, 1, third[1])
         gather_words(1, 1, third[2])
+        part_words(0, 1, third[1])
         part_words(1, 1, third[2])
 
         pages = [sb("page0", [P, T], F32)]
@@ -218,16 +219,15 @@ def tile_list_rgg_noneP_kernel(
             )
 
         out_rows = out_0.rearrange("(p t) c -> p t c", t=PACK)
-        y16 = [sb("y16_%d" % i, [P, w, PACK], BF16) for i, (c0, w, e) in enumerate(CHUNKS)]
+        y16 = {c0: sb("y16_%d" % c0, [P, w, PACK], BF16) for c0, w in VECTOR_CHUNKS + SCALAR_CHUNKS}
         y_q = sb("y_q", [P, T], U32)
         y_s = sb("y_s", [P, T], U8)
 
-        for t, slot_of in ((1, "wb_s_raw"), (2, "wc_q0"), (3, "wc_q1")):
-            pages.append(None)
+        pages.extend([None] * 3)
         for h in range(HALVES):
             message_rows(h)
             if h == 0:
-                pages[1] = sb("page1", [P, T], F32, "wb_s_raw")
+                pages[1] = sb("page1", [P, T], F32, "wb_raw")
                 nc.gpsimd.memset(pages[1][:], 0.0)
             for t in range(2):
                 turn_message(t, h)
@@ -243,60 +243,55 @@ def tile_list_rgg_noneP_kernel(
                 turn_message(t, h)
             for h in range(HALVES):
                 gate(t, h)
-        low16 = sb("low16", [P, 2, T], BF16, "msg_t0")
-        late_slots = ("wa_q", "wb_q", "w_s0", "w_s1", "v_w11")
-        high16 = [sb("high16_%d" % i, [P, 2, w], BF16, late_slots[i]) for i, (c0, w, e) in enumerate(CHUNKS)]
+        low_v = sb("low_v", [P, 2, SPLIT], BF16, "msg_t0")
+        low_s = sb("low_s", [P, 3, T - SPLIT], BF16, "msg_t1")
+        high16 = {
+            c0: sb("high16_%d" % c0, [P, 2, w], BF16, slot_of)
+            for (c0, w), slot_of in zip(VECTOR_CHUNKS, ("w_s0", "w_s1"))
+        }
         for t in range(PACK):
             if t > 1:
                 scatter(t, 0, J)
             nc.sync.dma_start(out=out_rows[:, t, :], in_=pages[t][:])
             if t < 2:
-                nc.scalar.copy(out=low16[:, t, :], in_=pages[t][:])
+                nc.scalar.copy(out=low_v[:, t, :], in_=pages[t][:, 0:SPLIT])
+                nc.scalar.copy(out=low_s[:, t, :], in_=pages[t][:, SPLIT:T])
             if t == 1:
-                for i, (c0, w, e) in enumerate(CHUNKS):
-                    nc.scalar.copy(out=y16[i][:, :, 0:2], in_=low16[:, :, c0 : c0 + w].rearrange("p t c -> p c t"))
+                for c0, w in VECTOR_CHUNKS:
+                    nc.scalar.copy(out=y16[c0][:, :, 0:2], in_=low_v[:, :, c0 : c0 + w].rearrange("p t c -> p c t"))
             if t == 2:
-                for i, (c0, w, e) in enumerate(CHUNKS):
-                    nc.scalar.copy(out=high16[i][:, 0, :], in_=pages[2][:, c0 : c0 + w])
-
-        def finish(i):
-            c0, w, e = CHUNKS[i]
-            copy = nc.vector.tensor_copy if e == "v" else nc.scalar.copy
-            copy(out=high16[i][:, 1, :], in_=pages[3][:, c0 : c0 + w])
-
-        def weave(i):
-            c0, w, e = CHUNKS[i]
-            copy = nc.vector.tensor_copy if e == "v" else nc.scalar.copy
-            copy(out=y16[i][:, :, 2:4], in_=high16[i][:].rearrange("p t c -> p c t"))
+                nc.scalar.copy(out=low_s[:, 2, :], in_=pages[2][:, SPLIT:T])
+                for c0, w in VECTOR_CHUNKS:
+                    nc.scalar.copy(out=high16[c0][:, 0, :], in_=pages[2][:, c0 : c0 + w])
+                for c0, w in SCALAR_CHUNKS:
+                    nc.scalar.copy(out=y16[c0][:, :, 0:3], in_=low_s[:, :, c0 - SPLIT : c0 - SPLIT + w].rearrange("p t c -> p c t"))
 
         codes_out = out_1[0].rearrange("p t b -> p (t b)").bitcast(I32)
 
-        def quantize_out(i):
-            c0, w, e = CHUNKS[i]
+        def quantize_out(c0, w):
             nc.vector.quantize_mx(
                 out=y_q[:, c0 : c0 + w].bitcast(FP8X4),
                 scales=y_s[:, c0 : c0 + w],
-                in_=y16[i][:].rearrange("p c t -> p (c t)"),
+                in_=y16[c0][:].rearrange("p c t -> p (c t)"),
             )
 
         def store_codes(c0, c1):
             nc.sync.dma_start(out=codes_out[:, c0:c1], in_=y_q[:, c0:c1].bitcast(I32))
 
-        finish(0)
-        finish(1)
-        for i in (2, 3, 4):
-            finish(i)
-            weave(i)
-        weave(0)
-        weave(1)
-        quantize_out(0)
-        quantize_out(1)
-        store_codes(0, 1024)
-        quantize_out(2)
-        store_codes(1024, 1536)
-        quantize_out(3)
-        quantize_out(4)
-        store_codes(1536, 2048)
+        for c0, w in SCALAR_CHUNKS:
+            nc.scalar.copy(out=y16[c0][:, :, 3], in_=pages[3][:, c0 : c0 + w])
+        for c0, w in VECTOR_CHUNKS:
+            nc.vector.tensor_copy(out=high16[c0][:, 1, :], in_=pages[3][:, c0 : c0 + w])
+        for c0, w in VECTOR_CHUNKS:
+            nc.vector.tensor_copy(out=y16[c0][:, :, 2:4], in_=high16[c0][:].rearrange("p t c -> p c t"))
+        for c0, w in VECTOR_CHUNKS:
+            quantize_out(c0, w)
+        store_codes(0, SPLIT)
+        for c0, w in SCALAR_CHUNKS[:-1]:
+            quantize_out(c0, w)
+        store_codes(SPLIT, SCALAR_CHUNKS[-1][0])
+        quantize_out(*SCALAR_CHUNKS[-1])
+        store_codes(SCALAR_CHUNKS[-1][0], T)
         for q in range(4):
             nc.scalar.dma_start(
                 out=out_2[0, 4 * q : 4 * q + 4, :].bitcast(I32), in_=y_s[32 * q : 32 * q + 4, :].bitcast(I32)

@@ -102,10 +102,10 @@ def tile_list_rgg_noneP_kernel(
                 in_=wc_raw[a][:].rearrange("p i (c e) -> p c i e", e=4),
             )
 
-        wgo_col = sb("wgo_col", [P, J // P], F32, "wc_raw1")
+        wgo_col = [sb("wgo_col0", [P, HALF // P], F32, "wc_raw1"), None]
         wgo_ps = ps_turn.tile([P, HALF], F32, name="turn_ps")
         nc.tensor.transpose(wgo_ps[:, 0:P], wgo_rows[:], ident[:])
-        nc.scalar.copy(out=wgo_col[:], in_=wgo_ps[:, 0 : J // P])
+        nc.scalar.copy(out=wgo_col[0][:], in_=wgo_ps[:, 0 : HALF // P])
 
         v_w = [[None] * HALVES for l in range(2)]
 
@@ -113,8 +113,8 @@ def tile_list_rgg_noneP_kernel(
             cols = slice(h * HALF // 16, (h + 1) * HALF // 16)
             nc.vector.tensor_copy(both, tab_w[:].indirect(lists[l][:, cols]))
 
-        def part_words(l, h, both):
-            v_w[l][h] = sb("v_w%d%d" % (l, h), [P, PASSES, 2 * HALF], U8)
+        def part_words(l, h, both, slot_of=None):
+            v_w[l][h] = sb("v_w%d%d" % (l, h), [P, PASSES, 2 * HALF], U8, slot_of)
             nc.vector.tensor_copy(
                 out=v_w[l][h][:].bitcast(U16), in_=both.bitcast(U16).rearrange("p (j d) -> p d j", d=PASSES)
             )
@@ -126,7 +126,12 @@ def tile_list_rgg_noneP_kernel(
         first = sb("first", [P, HALF], U32, "wc16_0")
         gather_words(0, 0, first[:])
         part_words(0, 0, first[:])
+        wgo_col[1] = sb("wgo_col1", [P, HALF // P], F32, "wc16_0")
+        nc.scalar.copy(out=wgo_col[1][:], in_=wgo_ps[:, HALF // P : J // P])
         quantize_wc(1)
+        second = sb("second", [P, HALF], U32, "wc16_1")
+        gather_words(1, 0, second[:])
+        part_words(1, 0, second[:])
         for w in range(2):
             nc.vector.tensor_copy(
                 out=w_s[0][:, w * N : (w + 1) * N].rearrange("p (t m) -> p t m", t=PACK),
@@ -143,14 +148,10 @@ def tile_list_rgg_noneP_kernel(
             out=wb_q[:].bitcast(U16).rearrange("p a (t m) -> p a t m", t=PACK),
             in_=wb_raw[:].bitcast(U16).rearrange("p a (m t) -> p a t m", t=PACK),
         )
-        rest = sb("rest", [P, 3 * HALF], U32, "wb_raw")
-        third = [rest[:, i * HALF : (i + 1) * HALF] for i in range(3)]
-        gather_words(1, 0, third[0])
-        gather_words(0, 1, third[1])
-        part_words(1, 0, third[0])
-        gather_words(1, 1, third[2])
-        part_words(0, 1, third[1])
-        part_words(1, 1, third[2])
+        rest = sb("rest", [P, 2 * HALF], U32, "wb_raw")
+        for l in range(2):
+            gather_words(l, 1, rest[:, l * HALF : (l + 1) * HALF])
+        part_words(1, 1, rest[:, HALF : 2 * HALF])
 
         pages = [sb("page0", [P, T], F32)]
         nc.vector.memset(pages[0][:], 0.0)
@@ -174,12 +175,11 @@ def tile_list_rgg_noneP_kernel(
                         stop=(a == PASSES - 1),
                     )
             for b in range(HALF // P):
-                c = h * HALF // P + b
                 nc.scalar.activation(
                     out=msg_t[h][:, b, :].rearrange("p (t m) -> p t m", t=PACK),
                     in_=accs[b][:].rearrange("p (m t) -> p t m", t=PACK),
                     func=COPY,
-                    scale=wgo_col[:, c : c + 1],
+                    scale=wgo_col[h][:, b : b + 1],
                 )
 
         def gate(t, h):
@@ -195,7 +195,6 @@ def tile_list_rgg_noneP_kernel(
                     start=(a == 0),
                     stop=False,
                 )
-            for a in range(PASSES):
                 nc.tensor.matmul_mx(
                     out=acc[:],
                     lhsT=wa_q[:, a, t * P : (t + 1) * P].bitcast(FP8X4),
@@ -227,6 +226,7 @@ def tile_list_rgg_noneP_kernel(
         for h in range(HALVES):
             message_rows(h)
             if h == 0:
+                part_words(0, 1, rest[:, 0:HALF], "wc_raw1")
                 pages[1] = sb("page1", [P, T], F32, "wb_raw")
                 nc.gpsimd.memset(pages[1][:], 0.0)
             for t in range(2):

@@ -23,7 +23,6 @@ PACK = 4
 PASSES = K // (P * PACK)
 HALF = 512
 HALVES = J // HALF
-SHIFT_ROWS = 112
 VECTOR_CHUNKS = ((0, 512), (512, 256))
 SCALAR_CHUNKS = ((768, 512), (1280, 512), (1792, 256))
 SPLIT = 768
@@ -42,58 +41,63 @@ def tile_list_rgg_noneP_kernel(
         def sb(name, shape, dtype, slot_of=None):
             return keep.tile(shape, dtype, name=name, tag=slot_of or name, align_bytes=64)
 
+        arena = ctx.enter_context(tc.tile_pool(name="arena", bufs=1))
+
+        def at(name, shape, dtype, offset):
+            return arena.tile(shape, dtype, name=name, tag=name, align_bytes=64, offset=offset)
+
         lists = [sb("offs_sb", [P, J // 16], U16), sb("offs2_sb", [P, J // 16], U16)]
-        tab_s = sb("tab_s", [P, T], U8)
+        wc16 = [at("wc16_%d" % a, [P, N * PACK], BF16, 4096 * a) for a in range(PASSES)]
+        tab_s = at("tab_s", [P, T], U8, 8192)
+        wb_raw = at("wb_raw", [P, PASSES, 2 * N], U8, 10240)
+        wbs_raw = at("wbs_raw", [P, PASSES, N], U8, 12288)
+        was_raw = at("was_raw", [P, PASSES, N], U8, 13312)
         tab_w = sb("tab_w", [P, T], U32)
-        w_s_raw = [sb("wa_s_raw", [P, N], U8), sb("wb_s_raw", [P, N], U8)]
-        w_s = [sb("w_s0", [P, 2 * N], U8), sb("w_s1", [P, 2 * N], U8)]
-        v_s = [[sb("v_s%d%d" % (l, a), [P, J], U8) for a in range(PASSES)] for l in range(2)]
+        v_s = [sb("v_s%d" % a, [P, 2, J], U8) for a in range(PASSES)]
         wc_raw = [sb("wc_raw%d" % a, [P, PACK, N], F32) for a in range(PASSES)]
         wa_raw = sb("wa_raw", [P, PASSES, N], I32)
-        wb_raw = sb("wb_raw", [P, PASSES, 2 * N], U8)
-        wgo_rows = sb("wgo_rows", [P, P], F32)
-        ident = sb("ident", [P, P], F32)
+        wgo_col = [sb("wgo_col%d" % h, [P, HALF // P], F32) for h in range(HALVES)]
+        pages = [sb("page0", [P, T], F32)]
 
         nc.vector.memset(tab_s[:].bitcast(I32), 0)
-        for raw in w_s_raw:
-            nc.vector.memset(raw[:].bitcast(I32), 0)
-        nc.vector.memset(wgo_rows[:], 0.0)
-        for plane in (v_s[0][1], v_s[1][1], w_s[1]):
-            nc.vector.memset(plane[:].bitcast(I32), 0)
-        make_identity(nc, ident[:])
+        nc.gpsimd.memset(was_raw[:].bitcast(I32), 0)
+        nc.gpsimd.memset(wbs_raw[:].bitcast(I32), 0)
+        nc.gpsimd.memset(v_s[1][96:P].bitcast(I32), 0)
+        nc.vector.memset(pages[0][:], 0.0)
 
-        def load_scale_rows(dst, src, q):
-            nc.sync.dma_start(out=dst[32 * q : 32 * q + 8, :].bitcast(I32), in_=src[:, 4 * q : 4 * q + 4, :].bitcast(I32))
+        def load_weight_scales(queue, dst, src):
+            for q in range(4):
+                queue.dma_start(
+                    out=dst[32 * q : 32 * q + 4].bitcast(I32),
+                    in_=src[:, 4 * q : 4 * q + 4, :].rearrange("a r n -> r a n").bitcast(I32),
+                )
 
         def load_wc(a):
             nc.sync.dma_start(out=wc_raw[a][:], in_=wc[512 * a : 512 * (a + 1), :].rearrange("(p i) n -> p i n", i=PACK))
 
         nc.sync.dma_start(lists[0][:], offs)
         nc.sync.dma_start(lists[1][:], offs2)
-        for q in range(4):
-            load_scale_rows(tab_s, tab_scales, q)
+        by_row = tab_scales.rearrange("a (q r) t -> r q a t", r=4)
+        for r in range(4):
+            nc.sync.dma_start(out=tab_s[r:P:16, :].bitcast(I32), in_=by_row[r].bitcast(I32))
         load_wc(0)
-        load_wc(1)
         nc.sync.dma_start(out=tab_w[:].bitcast(I32), in_=tab_words[0].rearrange("p t b -> p (t b)").bitcast(I32))
-        for q in range(4):
-            load_scale_rows(w_s_raw[0], wa_scales, q)
-        nc.sync.dma_start(out=wgo_rows[0 : J // P, :], in_=wgo[0].rearrange("(c m) -> c m", m=P))
+        load_wc(1)
+        load_weight_scales(nc.sync, wbs_raw, wb_scales)
         nc.sync.dma_start(out=wa_raw[:], in_=wa_words.rearrange("a p n i -> p a (n i)").bitcast(I32))
         nc.sync.dma_start(out=wb_raw[:].bitcast(I32), in_=wb_words.rearrange("a p c -> p a c").bitcast(I32))
+        load_weight_scales(nc.sync, was_raw, wa_scales)
+        with nc.allow_non_contiguous_dma(reason="one edge weight for each partition"):
+            for h in range(HALVES):
+                nc.sync.dma_start(out=wgo_col[h][:], in_=wgo[0, h * HALF : (h + 1) * HALF].rearrange("(b p) -> p b", p=P))
 
-        def shift_down(dst, src):
-            nc.sync.dma_start(out=dst[0:SHIFT_ROWS, :].bitcast(I32), in_=src[4 : 4 + SHIFT_ROWS, :].bitcast(I32))
+        for l in range(2):
+            nc.vector.tensor_copy(v_s[0][:, l, :], tab_s[:].indirect(lists[l][:]))
+        nc.gpsimd.dma_start(out=v_s[1][0 : P - 16].bitcast(I32), in_=v_s[0][16:P].bitcast(I32))
 
-        def gather_scales(l):
-            nc.vector.tensor_copy(v_s[l][0][:], tab_s[:].indirect(lists[l][:]))
-            shift_down(v_s[l][1], v_s[l][0])
+        ident = at("ident", [P, P], F32, 9216)
+        make_identity(nc, ident[:])
 
-        gather_scales(0)
-        for q in range(4):
-            load_scale_rows(w_s_raw[1], wb_scales, q)
-        gather_scales(1)
-
-        wc16 = [sb("wc16_%d" % a, [P, N * PACK], BF16) for a in range(PASSES)]
         wc_q = [sb("wc_q%d" % a, [P, N], U32) for a in range(PASSES)]
         wc_s = [sb("wc_s%d" % a, [P, N], U8) for a in range(PASSES)]
         for a in range(PASSES):
@@ -101,11 +105,6 @@ def tile_list_rgg_noneP_kernel(
                 out=wc16[a][:].rearrange("p (c e i) -> p c i e", e=4, i=PACK),
                 in_=wc_raw[a][:].rearrange("p i (c e) -> p c i e", e=4),
             )
-
-        wgo_col = [sb("wgo_col0", [P, HALF // P], F32, "wc_raw1"), None]
-        wgo_ps = ps_turn.tile([P, HALF], F32, name="turn_ps")
-        nc.tensor.transpose(wgo_ps[:, 0:P], wgo_rows[:], ident[:])
-        nc.scalar.copy(out=wgo_col[0][:], in_=wgo_ps[:, 0 : HALF // P])
 
         v_w = [[None] * HALVES for l in range(2)]
 
@@ -122,39 +121,36 @@ def tile_list_rgg_noneP_kernel(
         def quantize_wc(a):
             nc.vector.quantize_mx(out=wc_q[a][:].bitcast(FP8X4), scales=wc_s[a][:], in_=wc16[a][:])
 
-        quantize_wc(0)
-        first = sb("first", [P, HALF], U32, "wc16_0")
-        gather_words(0, 0, first[:])
-        part_words(0, 0, first[:])
-        wgo_col[1] = sb("wgo_col1", [P, HALF // P], F32, "wc16_0")
-        nc.scalar.copy(out=wgo_col[1][:], in_=wgo_ps[:, HALF // P : J // P])
-        quantize_wc(1)
-        second = sb("second", [P, HALF], U32, "wc16_1")
-        gather_words(1, 0, second[:])
-        part_words(1, 0, second[:])
-        for w in range(2):
+        def deal_scales(dst, src):
             nc.vector.tensor_copy(
-                out=w_s[0][:, w * N : (w + 1) * N].rearrange("p (t m) -> p t m", t=PACK),
-                in_=w_s_raw[w][:].rearrange("p (m t) -> p t m", t=PACK),
+                out=dst[:].rearrange("p a (t m) -> p a t m", t=PACK), in_=src[:].rearrange("p a (m t) -> p a t m", t=PACK)
             )
-        shift_down(w_s[1], w_s[0])
-        wa_q = sb("wa_q", [P, PASSES, N], I32, "wb_s_raw")
-        nc.vector.tensor_copy(
-            out=wa_q[:].rearrange("p a (t c e) -> p a c t e", t=PACK, e=4),
-            in_=wa_raw[:].rearrange("p a (c e t) -> p a c t e", t=PACK, e=4),
-        )
-        wb_q = sb("wb_q", [P, PASSES, 2 * N], U8, "wa_raw")
+
+        first = sb("first", [P, 2 * HALF], U32)
+        for l in range(2):
+            gather_words(l, 0, first[:, l * HALF : (l + 1) * HALF])
+        for l in range(2):
+            part_words(l, 0, first[:, l * HALF : (l + 1) * HALF])
+        quantize_wc(0)
+        quantize_wc(1)
+        wb_q = at("wb_q", [P, PASSES, 2 * N], U8, 4160)
         nc.vector.tensor_copy(
             out=wb_q[:].bitcast(U16).rearrange("p a (t m) -> p a t m", t=PACK),
             in_=wb_raw[:].bitcast(U16).rearrange("p a (m t) -> p a t m", t=PACK),
         )
-        rest = sb("rest", [P, 2 * HALF], U32, "wb_raw")
+        wa_q = at("wa_q", [P, PASSES, N], I32, 64)
+        nc.vector.tensor_copy(
+            out=wa_q[:].rearrange("p a (t c e) -> p a c t e", t=PACK, e=4),
+            in_=wa_raw[:].rearrange("p a (c e t) -> p a c t e", t=PACK, e=4),
+        )
+        wb_s = at("wb_s", [P, PASSES, N], U8, 6208)
+        deal_scales(wb_s, wbs_raw)
+        wa_s = at("wa_s", [P, PASSES, N], U8, 7232)
+        deal_scales(wa_s, was_raw)
+        rest = at("rest", [P, 2 * HALF], U32, 10240)
         for l in range(2):
             gather_words(l, 1, rest[:, l * HALF : (l + 1) * HALF])
         part_words(1, 1, rest[:, HALF : 2 * HALF])
-
-        pages = [sb("page0", [P, T], F32)]
-        nc.vector.memset(pages[0][:], 0.0)
 
         msg_t = [sb("msg_t%d" % h, [P, HALF // P, N], F32) for h in range(HALVES)]
         eta = [sb("eta%d" % t, [P, J], F32) for t in range(PACK)]
@@ -168,7 +164,7 @@ def tile_list_rgg_noneP_kernel(
                     nc.tensor.matmul_mx(
                         out=accs[b][:],
                         lhsT=v_w[0][h][:, a, 2 * b * P : 2 * (b + 1) * P].bitcast(FP4X4),
-                        lhsT_scale=v_s[0][a][:, j0 : j0 + P],
+                        lhsT_scale=v_s[a][:, 0, j0 : j0 + P],
                         rhs=wc_q[a][:].bitcast(FP8X4),
                         rhs_scale=wc_s[a][:],
                         start=(a == 0),
@@ -189,18 +185,18 @@ def tile_list_rgg_noneP_kernel(
                 nc.tensor.matmul_mx(
                     out=acc[:],
                     lhsT=wb_q[:, a, 2 * t * P : 2 * (t + 1) * P].bitcast(FP4X4),
-                    lhsT_scale=w_s[a][:, N + t * P : N + (t + 1) * P],
+                    lhsT_scale=wb_s[:, a, t * P : (t + 1) * P],
                     rhs=v_w[0][h][:, a, :].bitcast(FP4X4),
-                    rhs_scale=v_s[0][a][:, js],
+                    rhs_scale=v_s[a][:, 0, js],
                     start=(a == 0),
                     stop=False,
                 )
                 nc.tensor.matmul_mx(
                     out=acc[:],
                     lhsT=wa_q[:, a, t * P : (t + 1) * P].bitcast(FP8X4),
-                    lhsT_scale=w_s[a][:, t * P : (t + 1) * P],
+                    lhsT_scale=wa_s[:, a, t * P : (t + 1) * P],
                     rhs=v_w[1][h][:, a, :].bitcast(FP4X4),
-                    rhs_scale=v_s[1][a][:, js],
+                    rhs_scale=v_s[a][:, 1, js],
                     start=False,
                     stop=(a == PASSES - 1),
                 )
@@ -226,13 +222,13 @@ def tile_list_rgg_noneP_kernel(
         for h in range(HALVES):
             message_rows(h)
             if h == 0:
-                part_words(0, 1, rest[:, 0:HALF], "wc_raw1")
-                pages[1] = sb("page1", [P, T], F32, "wb_raw")
+                part_words(0, 1, rest[:, 0:HALF], "wgo_col0")
+                pages[1] = at("page1", [P, T], F32, 10240)
                 nc.gpsimd.memset(pages[1][:], 0.0)
             for t in range(2):
-                turn_message(t, h)
-            for t in range(2):
                 gate(t, h)
+            for t in range(2):
+                turn_message(t, h)
             for t in range(2):
                 scatter(t, h * HALF, (h + 1) * HALF)
         for t, slot_of in ((2, "wc_q0"), (3, "wc_q1")):
@@ -246,8 +242,8 @@ def tile_list_rgg_noneP_kernel(
         low_v = sb("low_v", [P, 2, SPLIT], BF16, "msg_t0")
         low_s = sb("low_s", [P, 3, T - SPLIT], BF16, "msg_t1")
         high16 = {
-            c0: sb("high16_%d" % c0, [P, 2, w], BF16, slot_of)
-            for (c0, w), slot_of in zip(VECTOR_CHUNKS, ("w_s0", "w_s1"))
+            c0: at("high16_%d" % c0, [P, 2, w], BF16, offset)
+            for (c0, w), offset in zip(VECTOR_CHUNKS, (4160, 6208))
         }
         for t in range(PACK):
             if t > 1:

@@ -34,9 +34,10 @@ def tile_list_rgg_noneP_kernel(
     nc = tc.nc
     with ExitStack() as ctx:
         keep = ctx.enter_context(tc.tile_pool(name="keep", bufs=1))
-        ps_gate = ctx.enter_context(tc.psum_pool(name="ps_gate", bufs=2))
-        ps_msg = ctx.enter_context(tc.psum_pool(name="ps_msg", bufs=4))
-        ps_turn = ctx.enter_context(tc.psum_pool(name="ps_turn", bufs=2))
+        psum = ctx.enter_context(tc.psum_pool(name="psum", bufs=1))
+
+        def bank(name, number):
+            return psum.tile([P, HALF], F32, name=name, tag=name, offset=2048 * number)
 
         def sb(name, shape, dtype, slot_of=None):
             return keep.tile(shape, dtype, name=name, tag=slot_of or name, align_bytes=64)
@@ -47,58 +48,68 @@ def tile_list_rgg_noneP_kernel(
             return arena.tile(shape, dtype, name=name, tag=name, align_bytes=64, offset=offset)
 
         lists = [sb("offs_sb", [P, J // 16], U16), sb("offs2_sb", [P, J // 16], U16)]
-        wc16 = [at("wc16_%d" % a, [P, N * PACK], BF16, 4096 * a) for a in range(PASSES)]
-        tab_s = at("tab_s", [P, T], U8, 8192)
-        wb_raw = at("wb_raw", [P, PASSES, 2 * N], U8, 10240)
-        wbs_raw = at("wbs_raw", [P, PASSES, N], U8, 12288)
-        was_raw = at("was_raw", [P, PASSES, N], U8, 13312)
+        wc16 = [at("wc16_%d" % a, [P, N * PACK], BF16, 4096 * (a + 1)) for a in range(PASSES)]
+        tab_s = at("tab_s", [P, T], U8, 36864)
+        wb_raw = at("wb_raw", [P, PASSES, 2 * N], U8, 38848)
+        ws_raw = at("ws_raw", [P, 2 * N], U8, 2176)
+        w_s = at("w_s", [P, PASSES, 2, N], U8, 45056)
         tab_w = sb("tab_w", [P, T], U32)
-        v_s = [sb("v_s%d" % a, [P, 2, J], U8) for a in range(PASSES)]
+        picked_s = sb("picked_s", [P, 2, J], U8)
         wc_raw = [sb("wc_raw%d" % a, [P, PACK, N], F32) for a in range(PASSES)]
-        wa_raw = sb("wa_raw", [P, PASSES, N], I32)
-        wgo_col = [sb("wgo_col%d" % h, [P, HALF // P], F32) for h in range(HALVES)]
-        pages = [sb("page0", [P, T], F32)]
+        wa_raw = at("wa_raw", [P, PASSES, N], I32, 32832)
+        wgo_rows = sb("wgo_rows", [P, P], F32)
+        wgo_col = sb("wgo_col", [P, J // P], F32)
+        pages = [sb("page%d" % t, [P, T], F32) for t in range(2)]
 
-        nc.vector.memset(tab_s[:].bitcast(I32), 0)
-        nc.gpsimd.memset(was_raw[:].bitcast(I32), 0)
-        nc.gpsimd.memset(wbs_raw[:].bitcast(I32), 0)
-        nc.gpsimd.memset(v_s[1][96:P].bitcast(I32), 0)
-        nc.vector.memset(pages[0][:], 0.0)
+        nc.gpsimd.memset(wgo_rows[:], 0.0)
+        warm = sb("warm", [P, 8], F32)
+        nc.scalar.activation(out=warm[:, 0:1], in_=wgo_rows[:, 0:1], func=SIGMOID)
+        for rows in (tab_s, ws_raw):
+            nc.gpsimd.memset(rows[32:64].bitcast(I32), 0)
+            nc.gpsimd.memset(rows[64:P].bitcast(I32), 0)
+        v_s = sb("v_s", [P, PASSES, 2, J], U8)
+        ident = sb("ident", [P, P], F32)
+        make_identity(nc, ident[:])
+        for planes in (v_s, w_s):
+            nc.gpsimd.memset(planes[:].bitcast(I32), 0)
+        for page in pages:
+            nc.gpsimd.memset(page[:], 0.0)
 
-        def load_weight_scales(queue, dst, src):
+        def load_scale_rows(dst, src):
+            for a in range(PASSES):
+                nc.sync.dma_start(out=dst[a:32:2].bitcast(I32), in_=src[a].bitcast(I32))
+
+        def spread_scale_rows(queue, planes, rows):
             for q in range(4):
                 queue.dma_start(
-                    out=dst[32 * q : 32 * q + 4].bitcast(I32),
-                    in_=src[:, 4 * q : 4 * q + 4, :].rearrange("a r n -> r a n").bitcast(I32),
+                    out=planes[32 * q : 32 * q + 4].rearrange("p a l c -> p a (l c)").bitcast(I32),
+                    in_=rows[8 * q : 8 * q + 8].rearrange("p l c -> p (l c)").bitcast(I32),
                 )
 
         def load_wc(a):
             nc.sync.dma_start(out=wc_raw[a][:], in_=wc[512 * a : 512 * (a + 1), :].rearrange("(p i) n -> p i n", i=PACK))
 
         nc.sync.dma_start(lists[0][:], offs)
+        load_scale_rows(tab_s[:], tab_scales)
         nc.sync.dma_start(lists[1][:], offs2)
-        by_row = tab_scales.rearrange("a (q r) t -> r q a t", r=4)
-        for r in range(4):
-            nc.sync.dma_start(out=tab_s[r:P:16, :].bitcast(I32), in_=by_row[r].bitcast(I32))
         load_wc(0)
         nc.sync.dma_start(out=tab_w[:].bitcast(I32), in_=tab_words[0].rearrange("p t b -> p (t b)").bitcast(I32))
+        nc.sync.dma_start(out=wgo_rows[0 : J // P, :], in_=wgo[0].rearrange("(c m) -> c m", m=P))
+        load_scale_rows(ws_raw[:, 0:N], wa_scales)
+        load_scale_rows(ws_raw[:, N : 2 * N], wb_scales)
         load_wc(1)
-        load_weight_scales(nc.sync, wbs_raw, wb_scales)
-        nc.sync.dma_start(out=wa_raw[:], in_=wa_words.rearrange("a p n i -> p a (n i)").bitcast(I32))
-        nc.sync.dma_start(out=wb_raw[:].bitcast(I32), in_=wb_words.rearrange("a p c -> p a c").bitcast(I32))
-        load_weight_scales(nc.sync, was_raw, wa_scales)
-        with nc.allow_non_contiguous_dma(reason="one edge weight for each partition"):
-            for h in range(HALVES):
-                nc.sync.dma_start(out=wgo_col[h][:], in_=wgo[0, h * HALF : (h + 1) * HALF].rearrange("(b p) -> p b", p=P))
 
         for l in range(2):
-            nc.vector.tensor_copy(v_s[0][:, l, :], tab_s[:].indirect(lists[l][:]))
-        nc.gpsimd.dma_start(out=v_s[1][0 : P - 16].bitcast(I32), in_=v_s[0][16:P].bitcast(I32))
+            nc.vector.tensor_copy(picked_s[:, l, :], tab_s[:].indirect(lists[l][:]))
+        spread_scale_rows(nc.sync, v_s, picked_s)
+        nc.sync.dma_start(out=wa_raw[:], in_=wa_words.rearrange("a p n i -> p a (n i)").bitcast(I32))
+        nc.sync.dma_start(out=wb_raw[:].bitcast(I32), in_=wb_words.rearrange("a p c -> p a c").bitcast(I32))
 
-        ident = at("ident", [P, P], F32, 9216)
-        make_identity(nc, ident[:])
+        wgo_ps = bank("wgo_ps", 7)
+        nc.tensor.transpose(wgo_ps[:, 0:P], wgo_rows[:], ident[:])
+        nc.scalar.copy(out=wgo_col[:], in_=wgo_ps[:, 0 : J // P])
 
-        wc_q = [sb("wc_q%d" % a, [P, N], U32) for a in range(PASSES)]
+        wc_q = [at("wc_q0", [P, N], U32, 17344), at("wc_q1", [P, N], U32, 49152)]
         wc_s = [sb("wc_s%d" % a, [P, N], U8) for a in range(PASSES)]
         for a in range(PASSES):
             nc.scalar.copy(
@@ -112,8 +123,8 @@ def tile_list_rgg_noneP_kernel(
             cols = slice(h * HALF // 16, (h + 1) * HALF // 16)
             nc.vector.tensor_copy(both, tab_w[:].indirect(lists[l][:, cols]))
 
-        def part_words(l, h, both, slot_of=None):
-            v_w[l][h] = sb("v_w%d%d" % (l, h), [P, PASSES, 2 * HALF], U8, slot_of)
+        def part_words(l, h, both, offset):
+            v_w[l][h] = at("v_w%d%d" % (l, h), [P, PASSES, 2 * HALF], U8, offset)
             nc.vector.tensor_copy(
                 out=v_w[l][h][:].bitcast(U16), in_=both.bitcast(U16).rearrange("p (j d) -> p d j", d=PASSES)
             )
@@ -123,87 +134,89 @@ def tile_list_rgg_noneP_kernel(
 
         def deal_scales(dst, src):
             nc.vector.tensor_copy(
-                out=dst[:].rearrange("p a (t m) -> p a t m", t=PACK), in_=src[:].rearrange("p a (m t) -> p a t m", t=PACK)
+                out=dst[:].rearrange("p a (t m) -> p a t m", t=PACK), in_=src[:].rearrange("p (a m t) -> p a t m", a=2, t=PACK)
             )
 
-        first = sb("first", [P, 2 * HALF], U32)
-        for l in range(2):
-            gather_words(l, 0, first[:, l * HALF : (l + 1) * HALF])
-        for l in range(2):
-            part_words(l, 0, first[:, l * HALF : (l + 1) * HALF])
+        first = at("first", [P, HALF], U32, 128)
+        gather_words(0, 0, first[:])
         quantize_wc(0)
+        part_words(0, 0, first[:], 14400)
+        ws_dealt = at("ws_dealt", [P, 2, N], U8, 128)
+        deal_scales(ws_dealt, ws_raw)
+        spread_scale_rows(nc.sync, w_s, ws_dealt)
+        second = at("second", [P, HALF], U32, 2176)
+        gather_words(1, 0, second[:])
         quantize_wc(1)
-        wb_q = at("wb_q", [P, PASSES, 2 * N], U8, 4160)
+        part_words(1, 0, second[:], 10368)
+        wb_q = at("wb_q", [P, PASSES, 2 * N], U8, 8320)
         nc.vector.tensor_copy(
             out=wb_q[:].bitcast(U16).rearrange("p a (t m) -> p a t m", t=PACK),
             in_=wb_raw[:].bitcast(U16).rearrange("p a (m t) -> p a t m", t=PACK),
         )
-        wa_q = at("wa_q", [P, PASSES, N], I32, 64)
+        wa_q = at("wa_q", [P, PASSES, N], I32, 4224)
         nc.vector.tensor_copy(
             out=wa_q[:].rearrange("p a (t c e) -> p a c t e", t=PACK, e=4),
             in_=wa_raw[:].rearrange("p a (c e t) -> p a c t e", t=PACK, e=4),
         )
-        wb_s = at("wb_s", [P, PASSES, N], U8, 6208)
-        deal_scales(wb_s, wbs_raw)
-        wa_s = at("wa_s", [P, PASSES, N], U8, 7232)
-        deal_scales(wa_s, was_raw)
-        rest = at("rest", [P, 2 * HALF], U32, 10240)
+        rest = at("rest", [P, 2 * HALF], U32, 36800)
         for l in range(2):
             gather_words(l, 1, rest[:, l * HALF : (l + 1) * HALF])
-        part_words(1, 1, rest[:, HALF : 2 * HALF])
+        for l in range(2):
+            part_words(l, 1, rest[:, l * HALF : (l + 1) * HALF], 57344 + 2048 * l)
 
         msg_t = [sb("msg_t%d" % h, [P, HALF // P, N], F32) for h in range(HALVES)]
         eta = [sb("eta%d" % t, [P, J], F32) for t in range(PACK)]
         msg = [sb("msg%d" % t, [P, J], F32) for t in range(PACK)]
 
         def message_rows(h):
-            accs = [ps_msg.tile([P, N], F32, name="msg_ps") for b in range(HALF // P)]
-            for a in range(PASSES):
-                for b in range(HALF // P):
-                    j0 = h * HALF + b * P
-                    nc.tensor.matmul_mx(
-                        out=accs[b][:],
-                        lhsT=v_w[0][h][:, a, 2 * b * P : 2 * (b + 1) * P].bitcast(FP4X4),
-                        lhsT_scale=v_s[a][:, 0, j0 : j0 + P],
-                        rhs=wc_q[a][:].bitcast(FP8X4),
-                        rhs_scale=wc_s[a][:],
-                        start=(a == 0),
-                        stop=(a == PASSES - 1),
-                    )
+            accs = [bank("msg_ps%d%d" % (h, b), 4 * h + b) for b in range(HALF // P)]
+            blocks = range(HALF // P)
+            order = [(a, b) for a in range(PASSES) for b in blocks] if h == 0 else [(a, b) for b in blocks for a in range(PASSES)]
+            for a, b in order:
+                j0 = h * HALF + b * P
+                nc.tensor.matmul_mx(
+                    out=accs[b][:],
+                    lhsT=v_w[0][h][:, a, 2 * b * P : 2 * (b + 1) * P].bitcast(FP4X4),
+                    lhsT_scale=v_s[:, a, 0, j0 : j0 + P],
+                    rhs=wc_q[a][:].bitcast(FP8X4),
+                    rhs_scale=wc_s[a][:],
+                    start=(a == 0),
+                    stop=(a == PASSES - 1),
+                )
             for b in range(HALF // P):
                 nc.scalar.activation(
                     out=msg_t[h][:, b, :].rearrange("p (t m) -> p t m", t=PACK),
                     in_=accs[b][:].rearrange("p (m t) -> p t m", t=PACK),
                     func=COPY,
-                    scale=wgo_col[h][:, b : b + 1],
+                    scale=wgo_col[:, 4 * h + b : 4 * h + b + 1],
                 )
 
-        def gate(t, h):
-            acc = ps_gate.tile([P, HALF], F32, name="gate_ps")
+        def gate(t, h, number):
+            acc = bank("gate_ps%d%d" % (t, h), number)
             js = slice(h * HALF, (h + 1) * HALF)
             for a in range(PASSES):
                 nc.tensor.matmul_mx(
                     out=acc[:],
                     lhsT=wb_q[:, a, 2 * t * P : 2 * (t + 1) * P].bitcast(FP4X4),
-                    lhsT_scale=wb_s[:, a, t * P : (t + 1) * P],
+                    lhsT_scale=w_s[:, a, 1, t * P : (t + 1) * P],
                     rhs=v_w[0][h][:, a, :].bitcast(FP4X4),
-                    rhs_scale=v_s[a][:, 0, js],
+                    rhs_scale=v_s[:, a, 0, js],
                     start=(a == 0),
                     stop=False,
                 )
                 nc.tensor.matmul_mx(
                     out=acc[:],
                     lhsT=wa_q[:, a, t * P : (t + 1) * P].bitcast(FP8X4),
-                    lhsT_scale=wa_s[:, a, t * P : (t + 1) * P],
+                    lhsT_scale=w_s[:, a, 0, t * P : (t + 1) * P],
                     rhs=v_w[1][h][:, a, :].bitcast(FP4X4),
-                    rhs_scale=v_s[a][:, 1, js],
+                    rhs_scale=v_s[:, a, 1, js],
                     start=False,
                     stop=(a == PASSES - 1),
                 )
             nc.scalar.activation(out=eta[t][:, js], in_=acc[:], func=SIGMOID)
 
-        def turn_message(t, h):
-            turned = ps_turn.tile([P, HALF], F32, name="turn_ps")
+        def turn_message(t, h, number):
+            turned = bank("turn_ps%d%d" % (t, h), number)
             for b in range(HALF // P):
                 nc.tensor.transpose(turned[:, b * P : (b + 1) * P], msg_t[h][:, b, t * P : (t + 1) * P], ident[:])
             nc.scalar.copy(out=msg[t][:, h * HALF : (h + 1) * HALF], in_=turned[:])
@@ -218,32 +231,31 @@ def tile_list_rgg_noneP_kernel(
         y_q = sb("y_q", [P, T], U32)
         y_s = sb("y_s", [P, T], U8)
 
-        pages.extend([None] * 3)
+        pages.extend([None] * 2)
         for h in range(HALVES):
             message_rows(h)
-            if h == 0:
-                part_words(0, 1, rest[:, 0:HALF], "wgo_col0")
-                pages[1] = at("page1", [P, T], F32, 10240)
-                nc.gpsimd.memset(pages[1][:], 0.0)
             for t in range(2):
-                gate(t, h)
-            for t in range(2):
-                turn_message(t, h)
+                if h == 0:
+                    gate(t, h, 4 + 2 * t)
+                    turn_message(t, h, 5 + 2 * t)
+                else:
+                    gate(t, h, 4 if t == 0 else 0)
+                    turn_message(t, h, t)
             for t in range(2):
                 scatter(t, h * HALF, (h + 1) * HALF)
-        for t, slot_of in ((2, "wc_q0"), (3, "wc_q1")):
-            pages[t] = sb("page%d" % t, [P, T], F32, slot_of)
+        for t, offset in ((2, 17408), (3, 49152)):
+            pages[t] = at("page%d" % t, [P, T], F32, offset)
             nc.gpsimd.memset(pages[t][:], 0.0)
         for t in range(2, PACK):
             for h in range(HALVES):
-                turn_message(t, h)
+                turn_message(t, h, (7, 5)[h] if t == 2 else (1, 5)[h])
             for h in range(HALVES):
-                gate(t, h)
+                gate(t, h, (4, 6)[h] if t == 2 else (0, 7)[h])
         low_v = sb("low_v", [P, 2, SPLIT], BF16, "msg_t0")
         low_s = sb("low_s", [P, 3, T - SPLIT], BF16, "msg_t1")
         high16 = {
             c0: at("high16_%d" % c0, [P, 2, w], BF16, offset)
-            for (c0, w), offset in zip(VECTOR_CHUNKS, (4160, 6208))
+            for (c0, w), offset in zip(VECTOR_CHUNKS, (8320, 45056))
         }
         for t in range(PACK):
             if t > 1:

@@ -49,61 +49,56 @@ def tile_list_rgg_noneP_kernel(
 
         lists = [sb("offs_sb", [P, J // 16], U16), sb("offs2_sb", [P, J // 16], U16)]
         wc16 = [at("wc16_%d" % a, [P, N * PACK], BF16, 4096 * (a + 1)) for a in range(PASSES)]
-        tab_s = at("tab_s", [P, T], U8, 36864)
-        wb_raw = at("wb_raw", [P, PASSES, 2 * N], U8, 38848)
-        ws_raw = at("ws_raw", [P, 2 * N], U8, 2176)
-        w_s = at("w_s", [P, PASSES, 2, N], U8, 45056)
+        tab_s = sb("tab_s", [P, T], U8)
+        wa_raw = at("wa_raw", [P, PASSES, N], I32, 32768)
+        was_raw = at("was_raw", [P, PASSES, N], U8, 36864)
+        wbs_raw = at("wbs_raw", [P, PASSES, N], U8, 37888)
+        wb_raw = at("wb_raw", [P, PASSES, 2 * N], U8, 38912)
         tab_w = sb("tab_w", [P, T], U32)
-        picked_s = sb("picked_s", [P, 2, J], U8)
+        v_s = [sb("v_s%d" % a, [P, 2, J], U8) for a in range(PASSES)]
         wc_raw = [sb("wc_raw%d" % a, [P, PACK, N], F32) for a in range(PASSES)]
-        wa_raw = at("wa_raw", [P, PASSES, N], I32, 32832)
         wgo_rows = sb("wgo_rows", [P, P], F32)
         wgo_col = sb("wgo_col", [P, J // P], F32)
-        pages = [sb("page%d" % t, [P, T], F32) for t in range(2)]
+        pages = [sb("page0", [P, T], F32)]
 
+        nc.vector.memset(tab_s[:].bitcast(I32), 0)
         nc.gpsimd.memset(wgo_rows[:], 0.0)
         warm = sb("warm", [P, 8], F32)
         nc.scalar.activation(out=warm[:, 0:1], in_=wgo_rows[:, 0:1], func=SIGMOID)
-        for rows in (tab_s, ws_raw):
-            nc.gpsimd.memset(rows[32:64].bitcast(I32), 0)
-            nc.gpsimd.memset(rows[64:P].bitcast(I32), 0)
-        v_s = sb("v_s", [P, PASSES, 2, J], U8)
         ident = sb("ident", [P, P], F32)
         make_identity(nc, ident[:])
-        for planes in (v_s, w_s):
-            nc.gpsimd.memset(planes[:].bitcast(I32), 0)
-        for page in pages:
-            nc.gpsimd.memset(page[:], 0.0)
+        for raw in (wbs_raw, was_raw):
+            nc.vector.memset(raw[:].bitcast(I32), 0)
+        nc.vector.memset(v_s[1][96:P].bitcast(I32), 0)
+        nc.vector.memset(pages[0][:], 0.0)
 
-        def load_scale_rows(dst, src):
-            for a in range(PASSES):
-                nc.sync.dma_start(out=dst[a:32:2].bitcast(I32), in_=src[a].bitcast(I32))
-
-        def spread_scale_rows(queue, planes, rows):
+        def load_weight_scales(dst, src):
             for q in range(4):
-                queue.dma_start(
-                    out=planes[32 * q : 32 * q + 4].rearrange("p a l c -> p a (l c)").bitcast(I32),
-                    in_=rows[8 * q : 8 * q + 8].rearrange("p l c -> p (l c)").bitcast(I32),
+                nc.sync.dma_start(
+                    out=dst[32 * q : 32 * q + 4].bitcast(I32),
+                    in_=src[:, 4 * q : 4 * q + 4, :].rearrange("a r n -> r a n").bitcast(I32),
                 )
 
         def load_wc(a):
             nc.sync.dma_start(out=wc_raw[a][:], in_=wc[512 * a : 512 * (a + 1), :].rearrange("(p i) n -> p i n", i=PACK))
 
         nc.sync.dma_start(lists[0][:], offs)
-        load_scale_rows(tab_s[:], tab_scales)
         nc.sync.dma_start(lists[1][:], offs2)
+        by_row = tab_scales.rearrange("a (q r) t -> r q a t", r=4)
+        for r in range(4):
+            nc.sync.dma_start(out=tab_s[r:P:16, :].bitcast(I32), in_=by_row[r].bitcast(I32))
         load_wc(0)
         nc.sync.dma_start(out=tab_w[:].bitcast(I32), in_=tab_words[0].rearrange("p t b -> p (t b)").bitcast(I32))
         nc.sync.dma_start(out=wgo_rows[0 : J // P, :], in_=wgo[0].rearrange("(c m) -> c m", m=P))
-        load_scale_rows(ws_raw[:, 0:N], wa_scales)
-        load_scale_rows(ws_raw[:, N : 2 * N], wb_scales)
         load_wc(1)
-
-        for l in range(2):
-            nc.vector.tensor_copy(picked_s[:, l, :], tab_s[:].indirect(lists[l][:]))
-        spread_scale_rows(nc.sync, v_s, picked_s)
+        load_weight_scales(wbs_raw, wb_scales)
         nc.sync.dma_start(out=wa_raw[:], in_=wa_words.rearrange("a p n i -> p a (n i)").bitcast(I32))
         nc.sync.dma_start(out=wb_raw[:].bitcast(I32), in_=wb_words.rearrange("a p c -> p a c").bitcast(I32))
+        load_weight_scales(was_raw, wa_scales)
+
+        for l in range(2):
+            nc.vector.tensor_copy(v_s[0][:, l, :], tab_s[:].indirect(lists[l][:]))
+        nc.gpsimd.dma_start(out=v_s[1][0 : P - 16].bitcast(I32), in_=v_s[0][16:P].bitcast(I32))
 
         wgo_ps = bank("wgo_ps", 7)
         nc.tensor.transpose(wgo_ps[:, 0:P], wgo_rows[:], ident[:])
@@ -134,17 +129,14 @@ def tile_list_rgg_noneP_kernel(
 
         def deal_scales(dst, src):
             nc.vector.tensor_copy(
-                out=dst[:].rearrange("p a (t m) -> p a t m", t=PACK), in_=src[:].rearrange("p (a m t) -> p a t m", a=2, t=PACK)
+                out=dst[:].rearrange("p a (t m) -> p a t m", t=PACK), in_=src[:].rearrange("p a (m t) -> p a t m", t=PACK)
             )
 
         first = at("first", [P, HALF], U32, 128)
         gather_words(0, 0, first[:])
         quantize_wc(0)
         part_words(0, 0, first[:], 14400)
-        ws_dealt = at("ws_dealt", [P, 2, N], U8, 128)
-        deal_scales(ws_dealt, ws_raw)
-        spread_scale_rows(nc.sync, w_s, ws_dealt)
-        second = at("second", [P, HALF], U32, 2176)
+        second = at("second", [P, HALF], U32, 2112)
         gather_words(1, 0, second[:])
         quantize_wc(1)
         part_words(1, 0, second[:], 10368)
@@ -158,7 +150,11 @@ def tile_list_rgg_noneP_kernel(
             out=wa_q[:].rearrange("p a (t c e) -> p a c t e", t=PACK, e=4),
             in_=wa_raw[:].rearrange("p a (c e t) -> p a c t e", t=PACK, e=4),
         )
-        rest = at("rest", [P, 2 * HALF], U32, 36800)
+        wb_s = at("wb_s", [P, PASSES, N], U8, 3136)
+        deal_scales(wb_s, wbs_raw)
+        wa_s = at("wa_s", [P, PASSES, N], U8, 2112)
+        deal_scales(wa_s, was_raw)
+        rest = at("rest", [P, 2 * HALF], U32, 35840)
         for l in range(2):
             gather_words(l, 1, rest[:, l * HALF : (l + 1) * HALF])
         for l in range(2):
@@ -177,7 +173,7 @@ def tile_list_rgg_noneP_kernel(
                 nc.tensor.matmul_mx(
                     out=accs[b][:],
                     lhsT=v_w[0][h][:, a, 2 * b * P : 2 * (b + 1) * P].bitcast(FP4X4),
-                    lhsT_scale=v_s[:, a, 0, j0 : j0 + P],
+                    lhsT_scale=v_s[a][:, 0, j0 : j0 + P],
                     rhs=wc_q[a][:].bitcast(FP8X4),
                     rhs_scale=wc_s[a][:],
                     start=(a == 0),
@@ -198,18 +194,18 @@ def tile_list_rgg_noneP_kernel(
                 nc.tensor.matmul_mx(
                     out=acc[:],
                     lhsT=wb_q[:, a, 2 * t * P : 2 * (t + 1) * P].bitcast(FP4X4),
-                    lhsT_scale=w_s[:, a, 1, t * P : (t + 1) * P],
+                    lhsT_scale=wb_s[:, a, t * P : (t + 1) * P],
                     rhs=v_w[0][h][:, a, :].bitcast(FP4X4),
-                    rhs_scale=v_s[:, a, 0, js],
+                    rhs_scale=v_s[a][:, 0, js],
                     start=(a == 0),
                     stop=False,
                 )
                 nc.tensor.matmul_mx(
                     out=acc[:],
                     lhsT=wa_q[:, a, t * P : (t + 1) * P].bitcast(FP8X4),
-                    lhsT_scale=w_s[:, a, 0, t * P : (t + 1) * P],
+                    lhsT_scale=wa_s[:, a, t * P : (t + 1) * P],
                     rhs=v_w[1][h][:, a, :].bitcast(FP4X4),
-                    rhs_scale=v_s[:, a, 1, js],
+                    rhs_scale=v_s[a][:, 1, js],
                     start=False,
                     stop=(a == PASSES - 1),
                 )
@@ -231,7 +227,8 @@ def tile_list_rgg_noneP_kernel(
         y_q = sb("y_q", [P, T], U32)
         y_s = sb("y_s", [P, T], U8)
 
-        pages.extend([None] * 2)
+        pages.extend([at("page1", [P, T], F32, 35840), None, None])
+        nc.gpsimd.memset(pages[1][:], 0.0)
         for h in range(HALVES):
             message_rows(h)
             for t in range(2):
@@ -255,7 +252,7 @@ def tile_list_rgg_noneP_kernel(
         low_s = sb("low_s", [P, 3, T - SPLIT], BF16, "msg_t1")
         high16 = {
             c0: at("high16_%d" % c0, [P, 2, w], BF16, offset)
-            for (c0, w), offset in zip(VECTOR_CHUNKS, (8320, 45056))
+            for (c0, w), offset in zip(VECTOR_CHUNKS, (8320, 2112))
         }
         for t in range(PACK):
             if t > 1:

@@ -292,12 +292,9 @@ def tile_list_rgg_noneP_kernel(
         for c0, w in VECTOR_CHUNKS:
             quantize_out(c0, w)
         store_codes(0, SPLIT)
-        for c0, w in SCALAR_CHUNKS[:-1]:
+        for c0, w in SCALAR_CHUNKS:
             quantize_out(c0, w)
-        store_codes(SPLIT, SCALAR_CHUNKS[-1][0])
-        quantize_out(*SCALAR_CHUNKS[-1])
-        store_codes(SCALAR_CHUNKS[-1][0], T)
-        for q in range(4):
-            nc.scalar.dma_start(
-                out=out_2[0, 4 * q : 4 * q + 4, :].bitcast(I32), in_=y_s[32 * q : 32 * q + 4, :].bitcast(I32)
-            )
+            store_codes(c0, c0 + w)
+        scale_rows = out_2[0].rearrange("(q r) t -> r q t", r=4).bitcast(I32)
+        for r in range(4):
+            nc.scalar.dma_start(out=scale_rows[r], in_=y_s[r:P:32, :].bitcast(I32))

@@ -23,9 +23,10 @@ PACK = 4
 PASSES = K // (P * PACK)
 HALF = 512
 HALVES = J // HALF
-VECTOR_CHUNKS = ((0, 512), (512, 256))
-SCALAR_CHUNKS = ((768, 512), (1280, 512), (1792, 256))
-SPLIT = 768
+VECTOR_COLS = 256
+PAIRED_CHUNKS = ((256, 512), (768, 512))
+SCALAR_CHUNKS = ((1280, 512), (1792, 256))
+SPLIT = 1280
 
 
 def tile_list_rgg_noneP_kernel(
@@ -51,9 +52,9 @@ def tile_list_rgg_noneP_kernel(
         wc16 = [at("wc16_%d" % a, [P, N * PACK], BF16, 4096 * (a + 1)) for a in range(PASSES)]
         tab_s = sb("tab_s", [P, T], U8)
         wa_raw = at("wa_raw", [P, PASSES, N], I32, 32768)
-        was_raw = at("was_raw", [P, PASSES, N], U8, 36864)
-        wbs_raw = at("wbs_raw", [P, PASSES, N], U8, 37888)
-        wb_raw = at("wb_raw", [P, PASSES, 2 * N], U8, 38912)
+        wb_raw = at("wb_raw", [P, PASSES, 2 * N], U8, 36864)
+        ws_raw = sb("ws_raw", [P, 2 * N], U8)
+        w_s = at("w_s", [P, PASSES, 2, N], U8, 45056)
         tab_w = sb("tab_w", [P, T], U32)
         v_s = [sb("v_s%d" % a, [P, 2, J], U8) for a in range(PASSES)]
         wc_raw = [sb("wc_raw%d" % a, [P, PACK, N], F32) for a in range(PASSES)]
@@ -67,17 +68,15 @@ def tile_list_rgg_noneP_kernel(
         nc.scalar.activation(out=warm[:, 0:1], in_=wgo_rows[:, 0:1], func=SIGMOID)
         ident = sb("ident", [P, P], F32)
         make_identity(nc, ident[:])
-        for raw in (wbs_raw, was_raw):
-            nc.vector.memset(raw[:].bitcast(I32), 0)
-        nc.vector.memset(v_s[1][96:P].bitcast(I32), 0)
-        nc.vector.memset(pages[0][:], 0.0)
+        nc.gpsimd.memset(v_s[1][96:P].bitcast(I32), 0)
+        nc.gpsimd.memset(ws_raw[32:64].bitcast(I32), 0)
+        nc.gpsimd.memset(ws_raw[64:P].bitcast(I32), 0)
+        nc.gpsimd.memset(w_s[:].bitcast(I32), 0)
+        nc.gpsimd.memset(pages[0][:], 0.0)
 
         def load_weight_scales(dst, src):
-            for q in range(4):
-                nc.sync.dma_start(
-                    out=dst[32 * q : 32 * q + 4].bitcast(I32),
-                    in_=src[:, 4 * q : 4 * q + 4, :].rearrange("a r n -> r a n").bitcast(I32),
-                )
+            for a in range(PASSES):
+                nc.sync.dma_start(out=dst[a:32:2].bitcast(I32), in_=src[a].bitcast(I32))
 
         def load_wc(a):
             nc.sync.dma_start(out=wc_raw[a][:], in_=wc[512 * a : 512 * (a + 1), :].rearrange("(p i) n -> p i n", i=PACK))
@@ -90,11 +89,11 @@ def tile_list_rgg_noneP_kernel(
         load_wc(0)
         nc.sync.dma_start(out=tab_w[:].bitcast(I32), in_=tab_words[0].rearrange("p t b -> p (t b)").bitcast(I32))
         nc.sync.dma_start(out=wgo_rows[0 : J // P, :], in_=wgo[0].rearrange("(c m) -> c m", m=P))
+        load_weight_scales(ws_raw[:, 0:N], wa_scales)
+        load_weight_scales(ws_raw[:, N : 2 * N], wb_scales)
         load_wc(1)
-        load_weight_scales(wbs_raw, wb_scales)
         nc.sync.dma_start(out=wa_raw[:], in_=wa_words.rearrange("a p n i -> p a (n i)").bitcast(I32))
         nc.sync.dma_start(out=wb_raw[:].bitcast(I32), in_=wb_words.rearrange("a p c -> p a c").bitcast(I32))
-        load_weight_scales(was_raw, wa_scales)
 
         for l in range(2):
             nc.vector.tensor_copy(v_s[0][:, l, :], tab_s[:].indirect(lists[l][:]))
@@ -127,10 +126,6 @@ def tile_list_rgg_noneP_kernel(
         def quantize_wc(a):
             nc.vector.quantize_mx(out=wc_q[a][:].bitcast(FP8X4), scales=wc_s[a][:], in_=wc16[a][:])
 
-        def deal_scales(dst, src):
-            nc.vector.tensor_copy(
-                out=dst[:].rearrange("p a (t m) -> p a t m", t=PACK), in_=src[:].rearrange("p a (m t) -> p a t m", t=PACK)
-            )
 
         first = at("first", [P, HALF], U32, 128)
         gather_words(0, 0, first[:])
@@ -138,6 +133,16 @@ def tile_list_rgg_noneP_kernel(
         part_words(0, 0, first[:], 14400)
         second = at("second", [P, HALF], U32, 2112)
         gather_words(1, 0, second[:])
+        ws_dealt = at("ws_dealt", [P, 2 * N], U8, 128)
+        nc.vector.tensor_copy(
+            out=ws_dealt[:].rearrange("p (w t m) -> p w t m", w=2, t=PACK),
+            in_=ws_raw[:].rearrange("p (w m t) -> p w t m", w=2, t=PACK),
+        )
+        for q in range(4):
+            nc.sync.dma_start(
+                out=w_s[32 * q : 32 * q + 4].rearrange("p a w n -> p a (w n)").bitcast(I32),
+                in_=ws_dealt[8 * q : 8 * q + 8].bitcast(I32),
+            )
         quantize_wc(1)
         part_words(1, 0, second[:], 10368)
         wb_q = at("wb_q", [P, PASSES, 2 * N], U8, 8320)
@@ -150,10 +155,6 @@ def tile_list_rgg_noneP_kernel(
             out=wa_q[:].rearrange("p a (t c e) -> p a c t e", t=PACK, e=4),
             in_=wa_raw[:].rearrange("p a (c e t) -> p a c t e", t=PACK, e=4),
         )
-        wb_s = at("wb_s", [P, PASSES, N], U8, 3136)
-        deal_scales(wb_s, wbs_raw)
-        wa_s = at("wa_s", [P, PASSES, N], U8, 2112)
-        deal_scales(wa_s, was_raw)
         rest = at("rest", [P, 2 * HALF], U32, 35840)
         for l in range(2):
             gather_words(l, 1, rest[:, l * HALF : (l + 1) * HALF])
@@ -194,7 +195,7 @@ def tile_list_rgg_noneP_kernel(
                 nc.tensor.matmul_mx(
                     out=acc[:],
                     lhsT=wb_q[:, a, 2 * t * P : 2 * (t + 1) * P].bitcast(FP4X4),
-                    lhsT_scale=wb_s[:, a, t * P : (t + 1) * P],
+                    lhsT_scale=w_s[:, a, 1, t * P : (t + 1) * P],
                     rhs=v_w[0][h][:, a, :].bitcast(FP4X4),
                     rhs_scale=v_s[a][:, 0, js],
                     start=(a == 0),
@@ -203,7 +204,7 @@ def tile_list_rgg_noneP_kernel(
                 nc.tensor.matmul_mx(
                     out=acc[:],
                     lhsT=wa_q[:, a, t * P : (t + 1) * P].bitcast(FP8X4),
-                    lhsT_scale=wa_s[:, a, t * P : (t + 1) * P],
+                    lhsT_scale=w_s[:, a, 0, t * P : (t + 1) * P],
                     rhs=v_w[1][h][:, a, :].bitcast(FP4X4),
                     rhs_scale=v_s[a][:, 1, js],
                     start=False,
@@ -223,7 +224,7 @@ def tile_list_rgg_noneP_kernel(
             )
 
         out_rows = out_0.rearrange("(p t) c -> p t c", t=PACK)
-        y16 = {c0: sb("y16_%d" % c0, [P, w, PACK], BF16) for c0, w in VECTOR_CHUNKS + SCALAR_CHUNKS}
+        y16 = {c0: sb("y16_%d" % c0, [P, w, PACK], BF16) for c0, w in ((0, VECTOR_COLS),) + PAIRED_CHUNKS + SCALAR_CHUNKS}
         y_q = sb("y_q", [P, T], U32)
         y_s = sb("y_s", [P, T], U8)
 
@@ -248,26 +249,29 @@ def tile_list_rgg_noneP_kernel(
                 turn_message(t, h, (7, 5)[h] if t == 2 else (1, 5)[h])
             for h in range(HALVES):
                 gate(t, h, (4, 6)[h] if t == 2 else (0, 7)[h])
-        low_v = sb("low_v", [P, 2, SPLIT], BF16, "msg_t0")
+        low_v = sb("low_v", [P, 2, VECTOR_COLS], BF16, "msg_t0")
         low_s = sb("low_s", [P, 3, T - SPLIT], BF16, "msg_t1")
-        high16 = {
-            c0: at("high16_%d" % c0, [P, 2, w], BF16, offset)
-            for (c0, w), offset in zip(VECTOR_CHUNKS, (8320, 2112))
-        }
+        high16 = at("high16", [P, 2, VECTOR_COLS], BF16, 45056)
+        pairs = {c0: at("pairs%d" % c0, [P, 2, w, 2], BF16, offset) for (c0, w), offset in zip(PAIRED_CHUNKS, (4224, 8320))}
+
+        def round_into_pairs(t, c0, w):
+            nc.scalar.copy(out=pairs[c0][:, t // 2, :, t % 2], in_=pages[t][:, c0 : c0 + w])
+
         for t in range(PACK):
             if t > 1:
                 scatter(t, 0, J)
             nc.sync.dma_start(out=out_rows[:, t, :], in_=pages[t][:])
             if t < 2:
-                nc.scalar.copy(out=low_v[:, t, :], in_=pages[t][:, 0:SPLIT])
-                nc.scalar.copy(out=low_s[:, t, :], in_=pages[t][:, SPLIT:T])
+                nc.scalar.copy(out=low_v[:, t, :], in_=pages[t][:, 0:VECTOR_COLS])
             if t == 1:
-                for c0, w in VECTOR_CHUNKS:
-                    nc.scalar.copy(out=y16[c0][:, :, 0:2], in_=low_v[:, :, c0 : c0 + w].rearrange("p t c -> p c t"))
+                nc.scalar.copy(out=y16[0][:, :, 0:2], in_=low_v[:].rearrange("p t c -> p c t"))
             if t == 2:
-                nc.scalar.copy(out=low_s[:, 2, :], in_=pages[2][:, SPLIT:T])
-                for c0, w in VECTOR_CHUNKS:
-                    nc.scalar.copy(out=high16[c0][:, 0, :], in_=pages[2][:, c0 : c0 + w])
+                nc.scalar.copy(out=high16[:, 0, :], in_=pages[2][:, 0:VECTOR_COLS])
+            if t < 3:
+                nc.scalar.copy(out=low_s[:, t, :], in_=pages[t][:, SPLIT:T])
+                for c0, w in PAIRED_CHUNKS:
+                    round_into_pairs(t, c0, w)
+            if t == 2:
                 for c0, w in SCALAR_CHUNKS:
                     nc.scalar.copy(out=y16[c0][:, :, 0:3], in_=low_s[:, :, c0 - SPLIT : c0 - SPLIT + w].rearrange("p t c -> p c t"))
 
@@ -283,15 +287,22 @@ def tile_list_rgg_noneP_kernel(
         def store_codes(c0, c1):
             nc.sync.dma_start(out=codes_out[:, c0:c1], in_=y_q[:, c0:c1].bitcast(I32))
 
+        for c0, w in PAIRED_CHUNKS:
+            round_into_pairs(3, c0, w)
         for c0, w in SCALAR_CHUNKS:
             nc.scalar.copy(out=y16[c0][:, :, 3], in_=pages[3][:, c0 : c0 + w])
-        for c0, w in VECTOR_CHUNKS:
-            nc.vector.tensor_copy(out=high16[c0][:, 1, :], in_=pages[3][:, c0 : c0 + w])
-        for c0, w in VECTOR_CHUNKS:
-            nc.vector.tensor_copy(out=y16[c0][:, :, 2:4], in_=high16[c0][:].rearrange("p t c -> p c t"))
-        for c0, w in VECTOR_CHUNKS:
+        nc.vector.tensor_copy(out=high16[:, 1, :], in_=pages[3][:, 0:VECTOR_COLS])
+        nc.vector.tensor_copy(out=y16[0][:, :, 2:4], in_=high16[:].rearrange("p t c -> p c t"))
+        for c0, w in PAIRED_CHUNKS:
+            nc.vector.tensor_copy(
+                out=y16[c0][:].rearrange("p c t -> p (c t)").bitcast(I32).rearrange("p (c r) -> p c r", r=2),
+                in_=pairs[c0][:].rearrange("p r c e -> p (r c e)").bitcast(I32).rearrange("p (r c) -> p c r", r=2),
+            )
+            if c0 == VECTOR_COLS:
+                quantize_out(0, VECTOR_COLS)
+        for c0, w in PAIRED_CHUNKS:
             quantize_out(c0, w)
-        store_codes(0, SPLIT)
+            store_codes(0 if c0 == VECTOR_COLS else c0, c0 + w)
         for c0, w in SCALAR_CHUNKS:
             quantize_out(c0, w)
             store_codes(c0, c0 + w)

@@ -23,10 +23,29 @@ PACK = 4
 PASSES = K // (P * PACK)
 HALF = 512
 HALVES = J // HALF
+BLOCKS = HALF // P
+SOURCE, TARGET = 0, 1
+
 VECTOR_COLS = 256
 PAIRED_CHUNKS = ((256, 512), (768, 512))
 SCALAR_CHUNKS = ((1280, 512), (1792, 256))
-SPLIT = 1280
+SCALAR_START = SCALAR_CHUNKS[0][0]
+
+WC16_AT = (4096, 8192)
+SOURCE_PICK_AT = 128
+TARGET_PICK_AT = 2112
+WA_DEALT_AT = 4224
+WB_DEALT_AT = 8320
+TARGET_PARTED_AT = 10368
+SOURCE_PARTED_AT = 14400
+WC_CODES_AT = (17344, 49152)
+LATE_PAGES_AT = (17408, 49152)
+WA_RAW_AT = 32768
+WB_RAW_AT = 36864
+LATE_PICKS_AT = 36864
+PAGE1_AT = LATE_PICKS_AT
+W_PLANES_AT = 45056
+LATE_PARTED_AT = (57344, 59392)
 
 
 def tile_list_rgg_noneP_kernel(
@@ -49,12 +68,12 @@ def tile_list_rgg_noneP_kernel(
             return arena.tile(shape, dtype, name=name, tag=name, align_bytes=64, offset=offset)
 
         lists = [sb("offs_sb", [P, J // 16], U16), sb("offs2_sb", [P, J // 16], U16)]
-        wc16 = [at("wc16_%d" % a, [P, N * PACK], BF16, 4096 * (a + 1)) for a in range(PASSES)]
+        wc16 = [at("wc16_%d" % a, [P, N * PACK], BF16, WC16_AT[a]) for a in range(PASSES)]
         tab_s = sb("tab_s", [P, T], U8)
-        wa_raw = at("wa_raw", [P, PASSES, N], I32, 32768)
-        wb_raw = at("wb_raw", [P, PASSES, 2 * N], U8, 36864)
+        wa_raw = at("wa_raw", [P, PASSES, N], I32, WA_RAW_AT)
+        wb_raw = at("wb_raw", [P, PASSES, 2 * N], U8, WB_RAW_AT)
         ws_raw = sb("ws_raw", [P, 2 * N], U8)
-        w_s = at("w_s", [P, PASSES, 2, N], U8, 45056)
+        w_s = at("w_s", [P, PASSES, 2, N], U8, W_PLANES_AT)
         tab_w = sb("tab_w", [P, T], U32)
         v_s = [sb("v_s%d" % a, [P, 2, J], U8) for a in range(PASSES)]
         wc_raw = [sb("wc_raw%d" % a, [P, PACK, N], F32) for a in range(PASSES)]
@@ -81,8 +100,8 @@ def tile_list_rgg_noneP_kernel(
         def load_wc(a):
             nc.sync.dma_start(out=wc_raw[a][:], in_=wc[512 * a : 512 * (a + 1), :].rearrange("(p i) n -> p i n", i=PACK))
 
-        nc.sync.dma_start(lists[0][:], offs)
-        nc.sync.dma_start(lists[1][:], offs2)
+        nc.sync.dma_start(lists[SOURCE][:], offs)
+        nc.sync.dma_start(lists[TARGET][:], offs2)
         by_row = tab_scales.rearrange("a (q r) t -> r q a t", r=4)
         for r in range(4):
             nc.sync.dma_start(out=tab_s[r:P:16, :].bitcast(I32), in_=by_row[r].bitcast(I32))
@@ -95,7 +114,7 @@ def tile_list_rgg_noneP_kernel(
         nc.sync.dma_start(out=wa_raw[:], in_=wa_words.rearrange("a p n i -> p a (n i)").bitcast(I32))
         nc.sync.dma_start(out=wb_raw[:].bitcast(I32), in_=wb_words.rearrange("a p c -> p a c").bitcast(I32))
 
-        for l in range(2):
+        for l in (SOURCE, TARGET):
             nc.vector.tensor_copy(v_s[0][:, l, :], tab_s[:].indirect(lists[l][:]))
         nc.gpsimd.dma_start(out=v_s[1][0 : P - 16].bitcast(I32), in_=v_s[0][16:P].bitcast(I32))
 
@@ -103,7 +122,7 @@ def tile_list_rgg_noneP_kernel(
         nc.tensor.transpose(wgo_ps[:, 0:P], wgo_rows[:], ident[:])
         nc.scalar.copy(out=wgo_col[:], in_=wgo_ps[:, 0 : J // P])
 
-        wc_q = [at("wc_q0", [P, N], U32, 17344), at("wc_q1", [P, N], U32, 49152)]
+        wc_q = [at("wc_q%d" % a, [P, N], U32, WC_CODES_AT[a]) for a in range(PASSES)]
         wc_s = [sb("wc_s%d" % a, [P, N], U8) for a in range(PASSES)]
         for a in range(PASSES):
             nc.scalar.copy(
@@ -111,29 +130,28 @@ def tile_list_rgg_noneP_kernel(
                 in_=wc_raw[a][:].rearrange("p i (c e) -> p c i e", e=4),
             )
 
-        v_w = [[None] * HALVES for l in range(2)]
+        v_w = [[None] * HALVES for l in (SOURCE, TARGET)]
 
-        def gather_words(l, h, both):
+        def gather_words(l, h, picked):
             cols = slice(h * HALF // 16, (h + 1) * HALF // 16)
-            nc.vector.tensor_copy(both, tab_w[:].indirect(lists[l][:, cols]))
+            nc.vector.tensor_copy(picked, tab_w[:].indirect(lists[l][:, cols]))
 
-        def part_words(l, h, both, offset):
+        def part_words(l, h, picked, offset):
             v_w[l][h] = at("v_w%d%d" % (l, h), [P, PASSES, 2 * HALF], U8, offset)
             nc.vector.tensor_copy(
-                out=v_w[l][h][:].bitcast(U16), in_=both.bitcast(U16).rearrange("p (j d) -> p d j", d=PASSES)
+                out=v_w[l][h][:].bitcast(U16), in_=picked.bitcast(U16).rearrange("p (j d) -> p d j", d=PASSES)
             )
 
         def quantize_wc(a):
             nc.vector.quantize_mx(out=wc_q[a][:].bitcast(FP8X4), scales=wc_s[a][:], in_=wc16[a][:])
 
-
-        first = at("first", [P, HALF], U32, 128)
-        gather_words(0, 0, first[:])
+        source_pick = at("source_pick", [P, HALF], U32, SOURCE_PICK_AT)
+        gather_words(SOURCE, 0, source_pick[:])
         quantize_wc(0)
-        part_words(0, 0, first[:], 14400)
-        second = at("second", [P, HALF], U32, 2112)
-        gather_words(1, 0, second[:])
-        ws_dealt = at("ws_dealt", [P, 2 * N], U8, 128)
+        part_words(SOURCE, 0, source_pick[:], SOURCE_PARTED_AT)
+        target_pick = at("target_pick", [P, HALF], U32, TARGET_PICK_AT)
+        gather_words(TARGET, 0, target_pick[:])
+        ws_dealt = at("ws_dealt", [P, 2 * N], U8, SOURCE_PICK_AT)
         nc.vector.tensor_copy(
             out=ws_dealt[:].rearrange("p (w t m) -> p w t m", w=2, t=PACK),
             in_=ws_raw[:].rearrange("p (w m t) -> p w t m", w=2, t=PACK),
@@ -144,48 +162,50 @@ def tile_list_rgg_noneP_kernel(
                 in_=ws_dealt[8 * q : 8 * q + 8].bitcast(I32),
             )
         quantize_wc(1)
-        part_words(1, 0, second[:], 10368)
-        wb_q = at("wb_q", [P, PASSES, 2 * N], U8, 8320)
+        part_words(TARGET, 0, target_pick[:], TARGET_PARTED_AT)
+        wb_q = at("wb_q", [P, PASSES, 2 * N], U8, WB_DEALT_AT)
         nc.vector.tensor_copy(
             out=wb_q[:].bitcast(U16).rearrange("p a (t m) -> p a t m", t=PACK),
             in_=wb_raw[:].bitcast(U16).rearrange("p a (m t) -> p a t m", t=PACK),
         )
-        wa_q = at("wa_q", [P, PASSES, N], I32, 4224)
+        wa_q = at("wa_q", [P, PASSES, N], I32, WA_DEALT_AT)
         nc.vector.tensor_copy(
             out=wa_q[:].rearrange("p a (t c e) -> p a c t e", t=PACK, e=4),
             in_=wa_raw[:].rearrange("p a (c e t) -> p a c t e", t=PACK, e=4),
         )
-        rest = at("rest", [P, 2 * HALF], U32, 35840)
-        for l in range(2):
-            gather_words(l, 1, rest[:, l * HALF : (l + 1) * HALF])
-        for l in range(2):
-            part_words(l, 1, rest[:, l * HALF : (l + 1) * HALF], 57344 + 2048 * l)
+        late_picks = at("late_picks", [P, 2 * HALF], U32, LATE_PICKS_AT)
+        for l in (SOURCE, TARGET):
+            gather_words(l, 1, late_picks[:, l * HALF : (l + 1) * HALF])
+        for l in (SOURCE, TARGET):
+            part_words(l, 1, late_picks[:, l * HALF : (l + 1) * HALF], LATE_PARTED_AT[l])
 
-        msg_t = [sb("msg_t%d" % h, [P, HALF // P, N], F32) for h in range(HALVES)]
+        msg_t = [sb("msg_t%d" % h, [P, BLOCKS, N], F32) for h in range(HALVES)]
         eta = [sb("eta%d" % t, [P, J], F32) for t in range(PACK)]
         msg = [sb("msg%d" % t, [P, J], F32) for t in range(PACK)]
 
         def message_rows(h):
-            accs = [bank("msg_ps%d%d" % (h, b), 4 * h + b) for b in range(HALF // P)]
-            blocks = range(HALF // P)
-            order = [(a, b) for a in range(PASSES) for b in blocks] if h == 0 else [(a, b) for b in blocks for a in range(PASSES)]
+            accs = [bank("msg_ps%d%d" % (h, b), BLOCKS * h + b) for b in range(BLOCKS)]
+            if h == 0:
+                order = [(a, b) for a in range(PASSES) for b in range(BLOCKS)]
+            else:
+                order = [(a, b) for b in range(BLOCKS) for a in range(PASSES)]
             for a, b in order:
                 j0 = h * HALF + b * P
                 nc.tensor.matmul_mx(
                     out=accs[b][:],
-                    lhsT=v_w[0][h][:, a, 2 * b * P : 2 * (b + 1) * P].bitcast(FP4X4),
-                    lhsT_scale=v_s[a][:, 0, j0 : j0 + P],
+                    lhsT=v_w[SOURCE][h][:, a, 2 * b * P : 2 * (b + 1) * P].bitcast(FP4X4),
+                    lhsT_scale=v_s[a][:, SOURCE, j0 : j0 + P],
                     rhs=wc_q[a][:].bitcast(FP8X4),
                     rhs_scale=wc_s[a][:],
                     start=(a == 0),
                     stop=(a == PASSES - 1),
                 )
-            for b in range(HALF // P):
+            for b in range(BLOCKS):
                 nc.scalar.activation(
                     out=msg_t[h][:, b, :].rearrange("p (t m) -> p t m", t=PACK),
                     in_=accs[b][:].rearrange("p (m t) -> p t m", t=PACK),
                     func=COPY,
-                    scale=wgo_col[:, 4 * h + b : 4 * h + b + 1],
+                    scale=wgo_col[:, BLOCKS * h + b : BLOCKS * h + b + 1],
                 )
 
         def gate(t, h, number):
@@ -196,8 +216,8 @@ def tile_list_rgg_noneP_kernel(
                     out=acc[:],
                     lhsT=wb_q[:, a, 2 * t * P : 2 * (t + 1) * P].bitcast(FP4X4),
                     lhsT_scale=w_s[:, a, 1, t * P : (t + 1) * P],
-                    rhs=v_w[0][h][:, a, :].bitcast(FP4X4),
-                    rhs_scale=v_s[a][:, 0, js],
+                    rhs=v_w[SOURCE][h][:, a, :].bitcast(FP4X4),
+                    rhs_scale=v_s[a][:, SOURCE, js],
                     start=(a == 0),
                     stop=False,
                 )
@@ -205,8 +225,8 @@ def tile_list_rgg_noneP_kernel(
                     out=acc[:],
                     lhsT=wa_q[:, a, t * P : (t + 1) * P].bitcast(FP8X4),
                     lhsT_scale=w_s[:, a, 0, t * P : (t + 1) * P],
-                    rhs=v_w[1][h][:, a, :].bitcast(FP4X4),
-                    rhs_scale=v_s[a][:, 1, js],
+                    rhs=v_w[TARGET][h][:, a, :].bitcast(FP4X4),
+                    rhs_scale=v_s[a][:, TARGET, js],
                     start=False,
                     stop=(a == PASSES - 1),
                 )
@@ -214,13 +234,13 @@ def tile_list_rgg_noneP_kernel(
 
         def turn_message(t, h, number):
             turned = bank("turn_ps%d%d" % (t, h), number)
-            for b in range(HALF // P):
+            for b in range(BLOCKS):
                 nc.tensor.transpose(turned[:, b * P : (b + 1) * P], msg_t[h][:, b, t * P : (t + 1) * P], ident[:])
             nc.scalar.copy(out=msg[t][:, h * HALF : (h + 1) * HALF], in_=turned[:])
 
         def scatter(t, j0, j1):
             nc.vector.tensor_tensor(
-                pages[t][:].indirect(lists[1][:, j0 // 16 : j1 // 16]), eta[t][:, j0:j1], msg[t][:, j0:j1], MULT
+                pages[t][:].indirect(lists[TARGET][:, j0 // 16 : j1 // 16]), eta[t][:, j0:j1], msg[t][:, j0:j1], MULT
             )
 
         out_rows = out_0.rearrange("(p t) c -> p t c", t=PACK)
@@ -228,31 +248,33 @@ def tile_list_rgg_noneP_kernel(
         y_q = sb("y_q", [P, T], U32)
         y_s = sb("y_s", [P, T], U8)
 
-        pages.extend([at("page1", [P, T], F32, 35840), None, None])
+        pages.extend([at("page1", [P, T], F32, PAGE1_AT), None, None])
         nc.gpsimd.memset(pages[1][:], 0.0)
+        gate_banks = ((4, 4), (6, 0), (4, 6), (0, 7))
+        turn_banks = ((5, 0), (7, 1), (7, 5), (1, 5))
         for h in range(HALVES):
             message_rows(h)
             for t in range(2):
-                if h == 0:
-                    gate(t, h, 4 + 2 * t)
-                    turn_message(t, h, 5 + 2 * t)
-                else:
-                    gate(t, h, 4 if t == 0 else 0)
-                    turn_message(t, h, t)
+                gate(t, h, gate_banks[t][h])
+                turn_message(t, h, turn_banks[t][h])
             for t in range(2):
                 scatter(t, h * HALF, (h + 1) * HALF)
-        for t, offset in ((2, 17408), (3, 49152)):
+        for t, offset in zip((2, 3), LATE_PAGES_AT):
             pages[t] = at("page%d" % t, [P, T], F32, offset)
             nc.gpsimd.memset(pages[t][:], 0.0)
-        for t in range(2, PACK):
+        for t in (2, 3):
             for h in range(HALVES):
-                turn_message(t, h, (7, 5)[h] if t == 2 else (1, 5)[h])
+                turn_message(t, h, turn_banks[t][h])
             for h in range(HALVES):
-                gate(t, h, (4, 6)[h] if t == 2 else (0, 7)[h])
+                gate(t, h, gate_banks[t][h])
+
         low_v = sb("low_v", [P, 2, VECTOR_COLS], BF16, "msg_t0")
-        low_s = sb("low_s", [P, 3, T - SPLIT], BF16, "msg_t1")
-        high16 = at("high16", [P, 2, VECTOR_COLS], BF16, 45056)
-        pairs = {c0: at("pairs%d" % c0, [P, 2, w, 2], BF16, offset) for (c0, w), offset in zip(PAIRED_CHUNKS, (4224, 8320))}
+        low_s = sb("low_s", [P, 3, T - SCALAR_START], BF16, "msg_t1")
+        high_v = at("high_v", [P, 2, VECTOR_COLS], BF16, W_PLANES_AT)
+        pairs = {
+            c0: at("pairs%d" % c0, [P, 2, w, 2], BF16, offset)
+            for (c0, w), offset in zip(PAIRED_CHUNKS, (WA_DEALT_AT, WB_DEALT_AT))
+        }
 
         def round_into_pairs(t, c0, w):
             nc.scalar.copy(out=pairs[c0][:, t // 2, :, t % 2], in_=pages[t][:, c0 : c0 + w])
@@ -266,14 +288,15 @@ def tile_list_rgg_noneP_kernel(
             if t == 1:
                 nc.scalar.copy(out=y16[0][:, :, 0:2], in_=low_v[:].rearrange("p t c -> p c t"))
             if t == 2:
-                nc.scalar.copy(out=high16[:, 0, :], in_=pages[2][:, 0:VECTOR_COLS])
+                nc.scalar.copy(out=high_v[:, 0, :], in_=pages[2][:, 0:VECTOR_COLS])
             if t < 3:
-                nc.scalar.copy(out=low_s[:, t, :], in_=pages[t][:, SPLIT:T])
+                nc.scalar.copy(out=low_s[:, t, :], in_=pages[t][:, SCALAR_START:T])
                 for c0, w in PAIRED_CHUNKS:
                     round_into_pairs(t, c0, w)
             if t == 2:
                 for c0, w in SCALAR_CHUNKS:
-                    nc.scalar.copy(out=y16[c0][:, :, 0:3], in_=low_s[:, :, c0 - SPLIT : c0 - SPLIT + w].rearrange("p t c -> p c t"))
+                    cols = slice(c0 - SCALAR_START, c0 - SCALAR_START + w)
+                    nc.scalar.copy(out=y16[c0][:, :, 0:3], in_=low_s[:, :, cols].rearrange("p t c -> p c t"))
 
         codes_out = out_1[0].rearrange("p t b -> p (t b)").bitcast(I32)
 
@@ -291,8 +314,8 @@ def tile_list_rgg_noneP_kernel(
             round_into_pairs(3, c0, w)
         for c0, w in SCALAR_CHUNKS:
             nc.scalar.copy(out=y16[c0][:, :, 3], in_=pages[3][:, c0 : c0 + w])
-        nc.vector.tensor_copy(out=high16[:, 1, :], in_=pages[3][:, 0:VECTOR_COLS])
-        nc.vector.tensor_copy(out=y16[0][:, :, 2:4], in_=high16[:].rearrange("p t c -> p c t"))
+        nc.vector.tensor_copy(out=high_v[:, 1, :], in_=pages[3][:, 0:VECTOR_COLS])
+        nc.vector.tensor_copy(out=y16[0][:, :, 2:4], in_=high_v[:].rearrange("p t c -> p c t"))
         for c0, w in PAIRED_CHUNKS:
             nc.vector.tensor_copy(
                 out=y16[c0][:].rearrange("p c t -> p (c t)").bitcast(I32).rearrange("p (c r) -> p c r", r=2),
@@ -308,4 +331,4 @@ def tile_list_rgg_noneP_kernel(
             store_codes(c0, c0 + w)
         scale_rows = out_2[0].rearrange("(q r) t -> r q t", r=4).bitcast(I32)
         for r in range(4):
-            nc.scalar.dma_start(out=scale_rows[r], in_=y_s[r:P:32, :].bitcast(I32))
+            (nc.scalar, nc.sync)[r % 2].dma_start(out=scale_rows[r], in_=y_s[r:P:32, :].bitcast(I32))

@@ -26,10 +26,12 @@ HALVES = J // HALF
 BLOCKS = HALF // P
 SOURCE, TARGET = 0, 1
 
-VECTOR_COLS = 256
-PAIRED_CHUNKS = ((256, 512), (768, 512))
-SCALAR_CHUNKS = ((1280, 512), (1792, 256))
-SCALAR_START = SCALAR_CHUNKS[0][0]
+SCALAR_CHUNKS = ((0, 512), (512, 256))
+SCALAR_COLS = 768
+VECTOR_START, VECTOR_COLS = 768, 256
+PAIRED_CHUNKS = ((1024, 512), (1536, 512))
+PIECE = 256
+SCALE_COLS = 512
 
 WC16_AT = (4096, 8192)
 SOURCE_PICK_AT = 128
@@ -244,9 +246,10 @@ def tile_list_rgg_noneP_kernel(
             )
 
         out_rows = out_0.rearrange("(p t) c -> p t c", t=PACK)
-        y16 = {c0: sb("y16_%d" % c0, [P, w, PACK], BF16) for c0, w in ((0, VECTOR_COLS),) + PAIRED_CHUNKS + SCALAR_CHUNKS}
+        y16 = {c0: sb("y16_%d" % c0, [P, w, PACK], BF16) for c0, w in ((VECTOR_START, VECTOR_COLS),) + PAIRED_CHUNKS + SCALAR_CHUNKS}
         y_q = sb("y_q", [P, T], U32)
-        y_s = sb("y_s", [P, T], U8)
+        y_s = sb("y_s", [P, SCALE_COLS], U8)
+        vector_cols = slice(VECTOR_START, VECTOR_START + VECTOR_COLS)
 
         pages.extend([at("page1", [P, T], F32, PAGE1_AT), None, None])
         nc.gpsimd.memset(pages[1][:], 0.0)
@@ -269,7 +272,7 @@ def tile_list_rgg_noneP_kernel(
                 gate(t, h, gate_banks[t][h])
 
         low_v = sb("low_v", [P, 2, VECTOR_COLS], BF16, "msg_t0")
-        low_s = sb("low_s", [P, 3, T - SCALAR_START], BF16, "msg_t1")
+        low_s = sb("low_s", [P, 3, SCALAR_COLS], BF16, "msg_t1")
         high_v = at("high_v", [P, 2, VECTOR_COLS], BF16, W_PLANES_AT)
         pairs = {
             c0: at("pairs%d" % c0, [P, 2, w, 2], BF16, offset)
@@ -284,27 +287,28 @@ def tile_list_rgg_noneP_kernel(
                 scatter(t, 0, J)
             nc.sync.dma_start(out=out_rows[:, t, :], in_=pages[t][:])
             if t < 2:
-                nc.scalar.copy(out=low_v[:, t, :], in_=pages[t][:, 0:VECTOR_COLS])
+                nc.scalar.copy(out=low_v[:, t, :], in_=pages[t][:, vector_cols])
             if t == 1:
-                nc.scalar.copy(out=y16[0][:, :, 0:2], in_=low_v[:].rearrange("p t c -> p c t"))
+                nc.scalar.copy(out=y16[VECTOR_START][:, :, 0:2], in_=low_v[:].rearrange("p t c -> p c t"))
             if t == 2:
-                nc.scalar.copy(out=high_v[:, 0, :], in_=pages[2][:, 0:VECTOR_COLS])
+                nc.scalar.copy(out=high_v[:, 0, :], in_=pages[2][:, vector_cols])
             if t < 3:
-                nc.scalar.copy(out=low_s[:, t, :], in_=pages[t][:, SCALAR_START:T])
+                nc.scalar.copy(out=low_s[:, t, :], in_=pages[t][:, 0:SCALAR_COLS])
                 for c0, w in PAIRED_CHUNKS:
                     round_into_pairs(t, c0, w)
             if t == 2:
                 for c0, w in SCALAR_CHUNKS:
-                    cols = slice(c0 - SCALAR_START, c0 - SCALAR_START + w)
-                    nc.scalar.copy(out=y16[c0][:, :, 0:3], in_=low_s[:, :, cols].rearrange("p t c -> p c t"))
+                    nc.scalar.copy(out=y16[c0][:, :, 0:3], in_=low_s[:, :, c0 : c0 + w].rearrange("p t c -> p c t"))
 
         codes_out = out_1[0].rearrange("p t b -> p (t b)").bitcast(I32)
 
-        def quantize_out(c0, w):
+        def quantize_out(c0, piece):
+            col = c0 + piece * PIECE
+            k, first = divmod(col, SCALE_COLS)
             nc.vector.quantize_mx(
-                out=y_q[:, c0 : c0 + w].bitcast(FP8X4),
-                scales=y_s[:, c0 : c0 + w],
-                in_=y16[c0][:].rearrange("p c t -> p (c t)"),
+                out=y_q[:, col : col + PIECE].bitcast(FP8X4),
+                scales=y_s[4 * k : P, first : first + PIECE],
+                in_=y16[c0][:, piece * PIECE : (piece + 1) * PIECE, :].rearrange("p c t -> p (c t)"),
             )
 
         def store_codes(c0, c1):
@@ -314,21 +318,20 @@ def tile_list_rgg_noneP_kernel(
             round_into_pairs(3, c0, w)
         for c0, w in SCALAR_CHUNKS:
             nc.scalar.copy(out=y16[c0][:, :, 3], in_=pages[3][:, c0 : c0 + w])
-        nc.vector.tensor_copy(out=high_v[:, 1, :], in_=pages[3][:, 0:VECTOR_COLS])
-        nc.vector.tensor_copy(out=y16[0][:, :, 2:4], in_=high_v[:].rearrange("p t c -> p c t"))
+        nc.vector.tensor_copy(out=high_v[:, 1, :], in_=pages[3][:, vector_cols])
+        nc.vector.tensor_copy(out=y16[VECTOR_START][:, :, 2:4], in_=high_v[:].rearrange("p t c -> p c t"))
         for c0, w in PAIRED_CHUNKS:
             nc.vector.tensor_copy(
                 out=y16[c0][:].rearrange("p c t -> p (c t)").bitcast(I32).rearrange("p (c r) -> p c r", r=2),
                 in_=pairs[c0][:].rearrange("p r c e -> p (r c e)").bitcast(I32).rearrange("p (r c) -> p c r", r=2),
             )
-            if c0 == VECTOR_COLS:
-                quantize_out(0, VECTOR_COLS)
-        for c0, w in PAIRED_CHUNKS:
-            quantize_out(c0, w)
-            store_codes(0 if c0 == VECTOR_COLS else c0, c0 + w)
-        for c0, w in SCALAR_CHUNKS:
-            quantize_out(c0, w)
-            store_codes(c0, c0 + w)
-        scale_rows = out_2[0].rearrange("(q r) t -> r q t", r=4).bitcast(I32)
-        for r in range(4):
-            (nc.scalar, nc.sync)[r % 2].dma_start(out=scale_rows[r], in_=y_s[r:P:32, :].bitcast(I32))
+            if c0 == vector_cols.stop:
+                quantize_out(VECTOR_START, 0)
+                quantize_out(c0, 0)
+        for c0, w in PAIRED_CHUNKS + SCALAR_CHUNKS:
+            for piece in range(1 if c0 == vector_cols.stop else 0, w // PIECE):
+                quantize_out(c0, piece)
+            store_codes(VECTOR_START if c0 == vector_cols.stop else c0, c0 + w)
+        scale_rows = out_2[0].bitcast(I32).rearrange("(q r) (k c) -> q k r c", r=4, k=T // SCALE_COLS)
+        for q in range(4):
+            (nc.scalar, nc.sync)[q % 2].dma_start(out=scale_rows[q], in_=y_s[32 * q : 32 * q + 16, :].bitcast(I32))

@@ -24,6 +24,7 @@ PASSES = K // (P * PACK)
 HALF = 512
 HALVES = J // HALF
 BLOCKS = HALF // P
+WARM_PASSES = 4
 SOURCE, TARGET = 0, 1
 
 SCALAR_CHUNKS = ((0, 512), (512, 256))
@@ -33,21 +34,23 @@ PAIRED_CHUNKS = ((1024, 512), (1536, 512))
 PIECE = 256
 SCALE_COLS = 512
 
-WC16_AT = (4096, 8192)
-SOURCE_PICK_AT = 128
-TARGET_PICK_AT = 2112
-WA_DEALT_AT = 4224
-WB_DEALT_AT = 8320
+WC16_AT = (4096, 69632)
+SOURCE_PICK_AT = 0
+TARGET_PICK_AT = 2048
+LATE_SOURCE_PICK_AT = TARGET_PICK_AT
 TARGET_PARTED_AT = 10368
 SOURCE_PARTED_AT = 14400
+LATE_PARTED_AT = (68608, 59392)
+LATE_SCALES_AT = 70656
+LATE_TARGET_PICK_AT = 71680
+PAGE1_AT = 72704
 WC_CODES_AT = (17344, 49152)
 LATE_PAGES_AT = (17408, 49152)
 WA_RAW_AT = 32768
 WB_RAW_AT = 36864
-LATE_PICKS_AT = 36864
-PAGE1_AT = LATE_PICKS_AT
 W_PLANES_AT = 45056
-LATE_PARTED_AT = (57344, 59392)
+WB_DEALT_AT = 61440
+WA_DEALT_AT = 80896
 
 
 def tile_list_rgg_noneP_kernel(
@@ -77,7 +80,7 @@ def tile_list_rgg_noneP_kernel(
         ws_raw = sb("ws_raw", [P, 2 * N], U8)
         w_s = at("w_s", [P, PASSES, 2, N], U8, W_PLANES_AT)
         tab_w = sb("tab_w", [P, T], U32)
-        v_s = [sb("v_s%d" % a, [P, 2, J], U8) for a in range(PASSES)]
+        moved_s = [sb("moved_s%d" % h, [P, 2, HALF], U8) for h in range(HALVES)]
         wc_raw = [sb("wc_raw%d" % a, [P, PACK, N], F32) for a in range(PASSES)]
         wgo_rows = sb("wgo_rows", [P, P], F32)
         wgo_col = sb("wgo_col", [P, J // P], F32)
@@ -89,7 +92,8 @@ def tile_list_rgg_noneP_kernel(
         nc.scalar.activation(out=warm[:, 0:1], in_=wgo_rows[:, 0:1], func=SIGMOID)
         ident = sb("ident", [P, P], F32)
         make_identity(nc, ident[:])
-        nc.gpsimd.memset(v_s[1][96:P].bitcast(I32), 0)
+        for h in range(HALVES):
+            nc.gpsimd.memset(moved_s[h][96:P].bitcast(I32), 0)
         nc.gpsimd.memset(ws_raw[32:64].bitcast(I32), 0)
         nc.gpsimd.memset(ws_raw[64:P].bitcast(I32), 0)
         nc.gpsimd.memset(w_s[:].bitcast(I32), 0)
@@ -102,23 +106,36 @@ def tile_list_rgg_noneP_kernel(
         def load_wc(a):
             nc.sync.dma_start(out=wc_raw[a][:], in_=wc[512 * a : 512 * (a + 1), :].rearrange("(p i) n -> p i n", i=PACK))
 
+        nc.sync.dma_start(out=wb_raw[:].bitcast(I32), in_=wb_words.rearrange("a p c -> p a c").bitcast(I32))
         nc.sync.dma_start(lists[SOURCE][:], offs)
         nc.sync.dma_start(lists[TARGET][:], offs2)
         by_row = tab_scales.rearrange("a (q r) t -> r q a t", r=4)
         for r in range(4):
             nc.sync.dma_start(out=tab_s[r:P:16, :].bitcast(I32), in_=by_row[r].bitcast(I32))
-        load_wc(0)
         nc.sync.dma_start(out=tab_w[:].bitcast(I32), in_=tab_words[0].rearrange("p t b -> p (t b)").bitcast(I32))
+        load_wc(0)
         nc.sync.dma_start(out=wgo_rows[0 : J // P, :], in_=wgo[0].rearrange("(c m) -> c m", m=P))
         load_weight_scales(ws_raw[:, 0:N], wa_scales)
         load_weight_scales(ws_raw[:, N : 2 * N], wb_scales)
         load_wc(1)
         nc.sync.dma_start(out=wa_raw[:], in_=wa_words.rearrange("a p n i -> p a (n i)").bitcast(I32))
-        nc.sync.dma_start(out=wb_raw[:].bitcast(I32), in_=wb_words.rearrange("a p c -> p a c").bitcast(I32))
 
-        for l in (SOURCE, TARGET):
-            nc.vector.tensor_copy(v_s[0][:, l, :], tab_s[:].indirect(lists[l][:]))
-        nc.gpsimd.dma_start(out=v_s[1][0 : P - 16].bitcast(I32), in_=v_s[0][16:P].bitcast(I32))
+        wb_q = at("wb_q", [P, PASSES, 2 * N], U8, WB_DEALT_AT)
+        nc.vector.tensor_copy(
+            out=wb_q[:].bitcast(U16).rearrange("p a (t m) -> p a t m", t=PACK),
+            in_=wb_raw[:].bitcast(U16).rearrange("p a (m t) -> p a t m", t=PACK),
+        )
+
+        v_s = [[None] * HALVES, moved_s]
+
+        def gather_scales(h, picked, queue):
+            v_s[0][h] = picked
+            for l in (SOURCE, TARGET):
+                cols = slice(h * HALF // 16, (h + 1) * HALF // 16)
+                nc.vector.tensor_copy(picked[:, l, :], tab_s[:].indirect(lists[l][:, cols]))
+            queue.dma_start(out=moved_s[h][0 : P - 16].bitcast(I32), in_=picked[16:P].bitcast(I32))
+
+        gather_scales(0, sb("early_scales", [P, 2, HALF], U8), nc.gpsimd)
 
         wgo_ps = bank("wgo_ps", 7)
         nc.tensor.transpose(wgo_ps[:, 0:P], wgo_rows[:], ident[:])
@@ -147,12 +164,22 @@ def tile_list_rgg_noneP_kernel(
         def quantize_wc(a):
             nc.vector.quantize_mx(out=wc_q[a][:].bitcast(FP8X4), scales=wc_s[a][:], in_=wc16[a][:])
 
-        source_pick = at("source_pick", [P, HALF], U32, SOURCE_PICK_AT)
-        gather_words(SOURCE, 0, source_pick[:])
-        quantize_wc(0)
-        part_words(SOURCE, 0, source_pick[:], SOURCE_PARTED_AT)
-        target_pick = at("target_pick", [P, HALF], U32, TARGET_PICK_AT)
-        gather_words(TARGET, 0, target_pick[:])
+        picks = [at("source_pick", [P, HALF], U32, SOURCE_PICK_AT), at("target_pick", [P, HALF], U32, TARGET_PICK_AT)]
+        for l in (SOURCE, TARGET):
+            gather_words(l, 0, picks[l][:])
+        for l, offset in ((SOURCE, SOURCE_PARTED_AT), (TARGET, TARGET_PARTED_AT)):
+            part_words(l, 0, picks[l][:], offset)
+        idle = bank("warm_ps", 7)
+        for number in range(WARM_PASSES):
+            nc.tensor.matmul_mx(
+                out=idle[:],
+                lhsT=wb_q[:, 0, 0 : 2 * P].bitcast(FP4X4),
+                lhsT_scale=v_s[0][0][:, SOURCE, 0:P],
+                rhs=v_w[SOURCE][0][:, 0, :].bitcast(FP4X4),
+                rhs_scale=v_s[0][0][:, SOURCE, :],
+                start=(number == 0),
+                stop=(number == WARM_PASSES - 1),
+            )
         ws_dealt = at("ws_dealt", [P, 2 * N], U8, SOURCE_PICK_AT)
         nc.vector.tensor_copy(
             out=ws_dealt[:].rearrange("p (w t m) -> p w t m", w=2, t=PACK),
@@ -163,40 +190,36 @@ def tile_list_rgg_noneP_kernel(
                 out=w_s[32 * q : 32 * q + 4].rearrange("p a w n -> p a (w n)").bitcast(I32),
                 in_=ws_dealt[8 * q : 8 * q + 8].bitcast(I32),
             )
-        quantize_wc(1)
-        part_words(TARGET, 0, target_pick[:], TARGET_PARTED_AT)
-        wb_q = at("wb_q", [P, PASSES, 2 * N], U8, WB_DEALT_AT)
-        nc.vector.tensor_copy(
-            out=wb_q[:].bitcast(U16).rearrange("p a (t m) -> p a t m", t=PACK),
-            in_=wb_raw[:].bitcast(U16).rearrange("p a (m t) -> p a t m", t=PACK),
-        )
+        picks[SOURCE] = at("late_source_pick", [P, HALF], U32, LATE_SOURCE_PICK_AT)
+        gather_words(SOURCE, 1, picks[SOURCE][:])
+        quantize_wc(0)
         wa_q = at("wa_q", [P, PASSES, N], I32, WA_DEALT_AT)
         nc.vector.tensor_copy(
             out=wa_q[:].rearrange("p a (t c e) -> p a c t e", t=PACK, e=4),
             in_=wa_raw[:].rearrange("p a (c e t) -> p a c t e", t=PACK, e=4),
         )
-        late_picks = at("late_picks", [P, 2 * HALF], U32, LATE_PICKS_AT)
+        quantize_wc(1)
+        gather_scales(1, at("late_scales", [P, 2, HALF], U8, LATE_SCALES_AT), nc.sync)
+        picks[TARGET] = at("late_target_pick", [P, HALF], U32, LATE_TARGET_PICK_AT)
+        gather_words(TARGET, 1, picks[TARGET][:])
         for l in (SOURCE, TARGET):
-            gather_words(l, 1, late_picks[:, l * HALF : (l + 1) * HALF])
-        for l in (SOURCE, TARGET):
-            part_words(l, 1, late_picks[:, l * HALF : (l + 1) * HALF], LATE_PARTED_AT[l])
+            part_words(l, 1, picks[l][:], LATE_PARTED_AT[l])
 
         msg_t = [sb("msg_t%d" % h, [P, BLOCKS, N], F32) for h in range(HALVES)]
         eta = [sb("eta%d" % t, [P, J], F32) for t in range(PACK)]
         msg = [sb("msg%d" % t, [P, J], F32) for t in range(PACK)]
 
         def message_rows(h):
-            accs = [bank("msg_ps%d%d" % (h, b), BLOCKS * h + b) for b in range(BLOCKS)]
+            accs = [bank("msg_ps%d%d" % (h, b), ((0, 1, 2, 3), (4, 5, 3, 6))[h][b]) for b in range(BLOCKS)]
             if h == 0:
                 order = [(a, b) for a in range(PASSES) for b in range(BLOCKS)]
             else:
                 order = [(a, b) for b in range(BLOCKS) for a in range(PASSES)]
             for a, b in order:
-                j0 = h * HALF + b * P
                 nc.tensor.matmul_mx(
                     out=accs[b][:],
                     lhsT=v_w[SOURCE][h][:, a, 2 * b * P : 2 * (b + 1) * P].bitcast(FP4X4),
-                    lhsT_scale=v_s[a][:, SOURCE, j0 : j0 + P],
+                    lhsT_scale=v_s[a][h][:, SOURCE, b * P : (b + 1) * P],
                     rhs=wc_q[a][:].bitcast(FP8X4),
                     rhs_scale=wc_s[a][:],
                     start=(a == 0),
@@ -219,7 +242,7 @@ def tile_list_rgg_noneP_kernel(
                     lhsT=wb_q[:, a, 2 * t * P : 2 * (t + 1) * P].bitcast(FP4X4),
                     lhsT_scale=w_s[:, a, 1, t * P : (t + 1) * P],
                     rhs=v_w[SOURCE][h][:, a, :].bitcast(FP4X4),
-                    rhs_scale=v_s[a][:, SOURCE, js],
+                    rhs_scale=v_s[a][h][:, SOURCE, :],
                     start=(a == 0),
                     stop=False,
                 )
@@ -228,7 +251,7 @@ def tile_list_rgg_noneP_kernel(
                     lhsT=wa_q[:, a, t * P : (t + 1) * P].bitcast(FP8X4),
                     lhsT_scale=w_s[:, a, 0, t * P : (t + 1) * P],
                     rhs=v_w[TARGET][h][:, a, :].bitcast(FP4X4),
-                    rhs_scale=v_s[a][:, TARGET, js],
+                    rhs_scale=v_s[a][h][:, TARGET, :],
                     start=False,
                     stop=(a == PASSES - 1),
                 )
@@ -253,8 +276,8 @@ def tile_list_rgg_noneP_kernel(
 
         pages.extend([at("page1", [P, T], F32, PAGE1_AT), None, None])
         nc.gpsimd.memset(pages[1][:], 0.0)
-        gate_banks = ((4, 4), (6, 0), (4, 6), (0, 7))
-        turn_banks = ((5, 0), (7, 1), (7, 5), (1, 5))
+        gate_banks = ((4, 4), (3, 0), (4, 3), (0, 6))
+        turn_banks = ((5, 0), (6, 1), (6, 5), (1, 5))
         for h in range(HALVES):
             message_rows(h)
             for t in range(2):

@@ -24,7 +24,6 @@ PASSES = K // (P * PACK)
 HALF = 512
 HALVES = J // HALF
 BLOCKS = HALF // P
-WARM_PASSES = 4
 SOURCE, TARGET = 0, 1
 
 SCALAR_CHUNKS = ((0, 512), (512, 256))
@@ -169,17 +168,6 @@ def tile_list_rgg_noneP_kernel(
             gather_words(l, 0, picks[l][:])
         for l, offset in ((SOURCE, SOURCE_PARTED_AT), (TARGET, TARGET_PARTED_AT)):
             part_words(l, 0, picks[l][:], offset)
-        idle = bank("warm_ps", 7)
-        for number in range(WARM_PASSES):
-            nc.tensor.matmul_mx(
-                out=idle[:],
-                lhsT=wb_q[:, 0, 0 : 2 * P].bitcast(FP4X4),
-                lhsT_scale=v_s[0][0][:, SOURCE, 0:P],
-                rhs=v_w[SOURCE][0][:, 0, :].bitcast(FP4X4),
-                rhs_scale=v_s[0][0][:, SOURCE, :],
-                start=(number == 0),
-                stop=(number == WARM_PASSES - 1),
-            )
         ws_dealt = at("ws_dealt", [P, 2 * N], U8, SOURCE_PICK_AT)
         nc.vector.tensor_copy(
             out=ws_dealt[:].rearrange("p (w t m) -> p w t m", w=2, t=PACK),

@@ -22,9 +22,9 @@ P = 128
 PACK = 4
 PASSES = K // (P * PACK)
 HALF = 512
-HALVES = J // HALF
-BLOCKS = HALF // P
+QUARTER = 256
 SOURCE, TARGET = 0, 1
+WA, WB = 0, 1
 
 SCALAR_CHUNKS = ((0, 512), (512, 256))
 SCALAR_COLS = 768
@@ -33,23 +33,18 @@ PAIRED_CHUNKS = ((1024, 512), (1536, 512))
 PIECE = 256
 SCALE_COLS = 512
 
-WC16_AT = (4096, 69632)
-SOURCE_PICK_AT = 0
-TARGET_PICK_AT = 2048
-LATE_SOURCE_PICK_AT = TARGET_PICK_AT
-TARGET_PARTED_AT = 10368
-SOURCE_PARTED_AT = 14400
-LATE_PARTED_AT = (68608, 59392)
-LATE_SCALES_AT = 70656
-LATE_TARGET_PICK_AT = 71680
-PAGE1_AT = 72704
-WC_CODES_AT = (17344, 49152)
-LATE_PAGES_AT = (17408, 49152)
-WA_RAW_AT = 32768
-WB_RAW_AT = 36864
-W_PLANES_AT = 45056
-WB_DEALT_AT = 61440
-WA_DEALT_AT = 80896
+EARLY_PARTED_AT = (0, 2048)
+WB_RAW_AT = 1024
+WS_RAW_AT = 4096
+PAGE1_AT = 4096
+WC_RAW_AT = (12288, 22464)
+LATE_PICK_AT = (12288, 29632)
+LATE_SOURCE_PARTED_AT = 20480
+LATE_PAGES_AT = (22528, 30720)
+FIRST_ROWS_AT = (38912, 39936)
+PAIRS_AT = (41984, 54144)
+LATE_ROWS_AT = 46016
+LOW_S_AT, LOW_V_AT, HIGH_V_AT = 46080, 50688, 51712
 
 
 def tile_list_rgg_noneP_kernel(
@@ -59,243 +54,257 @@ def tile_list_rgg_noneP_kernel(
     with ExitStack() as ctx:
         keep = ctx.enter_context(tc.tile_pool(name="keep", bufs=1))
         psum = ctx.enter_context(tc.psum_pool(name="psum", bufs=1))
+        arena = ctx.enter_context(tc.tile_pool(name="arena", bufs=1))
 
         def bank(name, number):
             return psum.tile([P, HALF], F32, name=name, tag=name, offset=2048 * number)
 
-        def sb(name, shape, dtype, slot_of=None):
-            return keep.tile(shape, dtype, name=name, tag=slot_of or name, align_bytes=64)
-
-        arena = ctx.enter_context(tc.tile_pool(name="arena", bufs=1))
+        def sb(name, shape, dtype):
+            return keep.tile(shape, dtype, name=name, tag=name, align_bytes=64)
 
         def at(name, shape, dtype, offset):
             return arena.tile(shape, dtype, name=name, tag=name, align_bytes=64, offset=offset)
 
         lists = [sb("offs_sb", [P, J // 16], U16), sb("offs2_sb", [P, J // 16], U16)]
-        wc16 = [at("wc16_%d" % a, [P, N * PACK], BF16, WC16_AT[a]) for a in range(PASSES)]
         tab_s = sb("tab_s", [P, T], U8)
-        wa_raw = at("wa_raw", [P, PASSES, N], I32, WA_RAW_AT)
-        wb_raw = at("wb_raw", [P, PASSES, 2 * N], U8, WB_RAW_AT)
-        ws_raw = sb("ws_raw", [P, 2 * N], U8)
-        w_s = at("w_s", [P, PASSES, 2, N], U8, W_PLANES_AT)
         tab_w = sb("tab_w", [P, T], U32)
-        moved_s = [sb("moved_s%d" % h, [P, 2, HALF], U8) for h in range(HALVES)]
-        wc_raw = [sb("wc_raw%d" % a, [P, PACK, N], F32) for a in range(PASSES)]
+        wa_raw = sb("wa_raw", [P, PASSES, N], U32)
+        wb_raw = at("wb_raw", [P, PASSES, 2 * N], U8, WB_RAW_AT)
+        ws_raw = at("ws_raw", [P, N], U8, WS_RAW_AT)
+        w_s = sb("w_s", [P, PASSES, 2, N], U8)
+        moved_s = sb("moved_s", [P, 2, J], U8)
+        wc_raw = [at("wc_raw%d" % a, [P, PACK, N], F32, WC_RAW_AT[a]) for a in range(PASSES)]
         wgo_rows = sb("wgo_rows", [P, P], F32)
         wgo_col = sb("wgo_col", [P, J // P], F32)
-        pages = [sb("page0", [P, T], F32)]
+        pages = [sb("page0", [P, T], F32), None, None, None]
 
         nc.vector.memset(tab_s[:].bitcast(I32), 0)
+        nc.vector.memset(pages[0][:], 0.0)
         nc.gpsimd.memset(wgo_rows[:], 0.0)
+        nc.gpsimd.memset(ws_raw[64:P].bitcast(I32), 0)
         warm = sb("warm", [P, 8], F32)
         nc.scalar.activation(out=warm[:, 0:1], in_=wgo_rows[:, 0:1], func=SIGMOID)
         ident = sb("ident", [P, P], F32)
         make_identity(nc, ident[:])
-        for h in range(HALVES):
-            nc.gpsimd.memset(moved_s[h][96:P].bitcast(I32), 0)
-        nc.gpsimd.memset(ws_raw[32:64].bitcast(I32), 0)
-        nc.gpsimd.memset(ws_raw[64:P].bitcast(I32), 0)
-        nc.gpsimd.memset(w_s[:].bitcast(I32), 0)
-        nc.gpsimd.memset(pages[0][:], 0.0)
+        nc.gpsimd.memset(w_s[:].rearrange("p a w n -> p (a w n)").bitcast(I32), 0)
+        nc.gpsimd.memset(moved_s[96:P].rearrange("p l j -> p (l j)").bitcast(I32), 0)
 
-        def load_weight_scales(dst, src):
-            for a in range(PASSES):
-                nc.sync.dma_start(out=dst[a:32:2].bitcast(I32), in_=src[a].bitcast(I32))
-
-        def load_wc(a):
-            nc.sync.dma_start(out=wc_raw[a][:], in_=wc[512 * a : 512 * (a + 1), :].rearrange("(p i) n -> p i n", i=PACK))
-
-        nc.sync.dma_start(out=wb_raw[:].bitcast(I32), in_=wb_words.rearrange("a p c -> p a c").bitcast(I32))
         nc.sync.dma_start(lists[SOURCE][:], offs)
-        nc.sync.dma_start(lists[TARGET][:], offs2)
+        for w, src in ((WA, wa_scales), (WB, wb_scales)):
+            nc.sync.dma_start(out=ws_raw[w:64:2].bitcast(I32), in_=src.rearrange("a g n -> g a n").bitcast(I32))
         by_row = tab_scales.rearrange("a (q r) t -> r q a t", r=4)
         for r in range(4):
             nc.sync.dma_start(out=tab_s[r:P:16, :].bitcast(I32), in_=by_row[r].bitcast(I32))
         nc.sync.dma_start(out=tab_w[:].bitcast(I32), in_=tab_words[0].rearrange("p t b -> p (t b)").bitcast(I32))
-        load_wc(0)
+        nc.sync.dma_start(lists[TARGET][:], offs2)
+        nc.sync.dma_start(out=wb_raw[:].bitcast(I32), in_=wb_words.rearrange("a p c -> p a c").bitcast(I32))
         nc.sync.dma_start(out=wgo_rows[0 : J // P, :], in_=wgo[0].rearrange("(c m) -> c m", m=P))
-        load_weight_scales(ws_raw[:, 0:N], wa_scales)
-        load_weight_scales(ws_raw[:, N : 2 * N], wb_scales)
-        load_wc(1)
-        nc.sync.dma_start(out=wa_raw[:], in_=wa_words.rearrange("a p n i -> p a (n i)").bitcast(I32))
+        for a in range(PASSES):
+            nc.sync.dma_start(out=wc_raw[a][:], in_=wc[512 * a : 512 * (a + 1), :].rearrange("(p i) n -> p i n", i=PACK))
+        nc.sync.dma_start(out=wa_raw[:].bitcast(I32), in_=wa_words.rearrange("a p n i -> p a (n i)").bitcast(I32))
 
-        wb_q = at("wb_q", [P, PASSES, 2 * N], U8, WB_DEALT_AT)
+        ws_dealt = sb("ws_dealt", [P, N], U8)
         nc.vector.tensor_copy(
-            out=wb_q[:].bitcast(U16).rearrange("p a (t m) -> p a t m", t=PACK),
-            in_=wb_raw[:].bitcast(U16).rearrange("p a (m t) -> p a t m", t=PACK),
+            out=ws_dealt[:].rearrange("p (t m) -> p t m", t=PACK), in_=ws_raw[:].rearrange("p (m t) -> p t m", t=PACK)
         )
+        for q in range(4):
+            nc.sync.dma_start(
+                out=w_s[32 * q : 32 * q + 4].rearrange("p a w n -> p (a w) n").bitcast(I32),
+                in_=ws_dealt[16 * q : 16 * q + 16].bitcast(I32),
+            )
+        pages[1] = at("page1", [P, T], F32, PAGE1_AT)
+        nc.gpsimd.memset(pages[1][:], 0.0)
 
-        v_s = [[None] * HALVES, moved_s]
-
-        def gather_scales(h, picked, queue):
-            v_s[0][h] = picked
-            for l in (SOURCE, TARGET):
-                cols = slice(h * HALF // 16, (h + 1) * HALF // 16)
-                nc.vector.tensor_copy(picked[:, l, :], tab_s[:].indirect(lists[l][:, cols]))
-            queue.dma_start(out=moved_s[h][0 : P - 16].bitcast(I32), in_=picked[16:P].bitcast(I32))
-
-        gather_scales(0, sb("early_scales", [P, 2, HALF], U8), nc.gpsimd)
-
+        wb_q = sb("wb_q", [P, PASSES, 2 * N], U8)
+        nc.scalar.copy(
+            out=wb_q[:].bitcast(U16).rearrange("p a (t m) -> p a m t", t=PACK),
+            in_=wb_raw[:].bitcast(U16).rearrange("p a (m t) -> p a m t", t=PACK),
+        )
         wgo_ps = bank("wgo_ps", 7)
         nc.tensor.transpose(wgo_ps[:, 0:P], wgo_rows[:], ident[:])
         nc.scalar.copy(out=wgo_col[:], in_=wgo_ps[:, 0 : J // P])
-
-        wc_q = [at("wc_q%d" % a, [P, N], U32, WC_CODES_AT[a]) for a in range(PASSES)]
-        wc_s = [sb("wc_s%d" % a, [P, N], U8) for a in range(PASSES)]
+        wc16 = [sb("wc16_%d" % a, [P, N * PACK], BF16) for a in range(PASSES)]
         for a in range(PASSES):
             nc.scalar.copy(
-                out=wc16[a][:].rearrange("p (c e i) -> p c i e", e=4, i=PACK),
-                in_=wc_raw[a][:].rearrange("p i (c e) -> p c i e", e=4),
+                out=wc16[a][:].rearrange("p (t m i) -> p m i t", t=PACK, i=PACK),
+                in_=wc_raw[a][:].rearrange("p i (m t) -> p m i t", t=PACK),
             )
+        wa_q = sb("wa_q", [P, PASSES, N], U32)
+        nc.scalar.copy(
+            out=wa_q[:].rearrange("p a (t m) -> p a m t", t=PACK), in_=wa_raw[:].rearrange("p a (m t) -> p a m t", t=PACK)
+        )
 
-        v_w = [[None] * HALVES for l in (SOURCE, TARGET)]
+        picked_s = sb("picked_s", [P, 2, J], U8)
+        v_s = [picked_s, moved_s]
+        wc_q = [sb("wc_q%d" % a, [P, N], U32) for a in range(PASSES)]
+        wc_s = [sb("wc_s%d" % a, [P, N], U8) for a in range(PASSES)]
+        v_w = [[None, None], [None, None]]
+
+        def gather_scales(l):
+            nc.vector.tensor_copy(picked_s[:, l, :], tab_s[:].indirect(lists[l][:]))
 
         def gather_words(l, h, picked):
-            cols = slice(h * HALF // 16, (h + 1) * HALF // 16)
-            nc.vector.tensor_copy(picked, tab_w[:].indirect(lists[l][:, cols]))
+            nc.vector.tensor_copy(picked[:], tab_w[:].indirect(lists[l][:, h * HALF // 16 : (h + 1) * HALF // 16]))
 
-        def part_words(l, h, picked, offset):
-            v_w[l][h] = at("v_w%d%d" % (l, h), [P, PASSES, 2 * HALF], U8, offset)
+        def part_words(l, h, picked, parted):
+            v_w[l][h] = parted
             nc.vector.tensor_copy(
-                out=v_w[l][h][:].bitcast(U16), in_=picked.bitcast(U16).rearrange("p (j d) -> p d j", d=PASSES)
+                out=parted[:].bitcast(U16), in_=picked[:].bitcast(U16).rearrange("p (j d) -> p d j", d=PASSES)
             )
 
         def quantize_wc(a):
             nc.vector.quantize_mx(out=wc_q[a][:].bitcast(FP8X4), scales=wc_s[a][:], in_=wc16[a][:])
 
-        picks = [at("source_pick", [P, HALF], U32, SOURCE_PICK_AT), at("target_pick", [P, HALF], U32, TARGET_PICK_AT)]
+        picks = [sb("early_pick%d" % l, [P, HALF], U32) for l in (SOURCE, TARGET)]
         for l in (SOURCE, TARGET):
-            gather_words(l, 0, picks[l][:])
-        for l, offset in ((SOURCE, SOURCE_PARTED_AT), (TARGET, TARGET_PARTED_AT)):
-            part_words(l, 0, picks[l][:], offset)
-        ws_dealt = at("ws_dealt", [P, 2 * N], U8, SOURCE_PICK_AT)
-        nc.vector.tensor_copy(
-            out=ws_dealt[:].rearrange("p (w t m) -> p w t m", w=2, t=PACK),
-            in_=ws_raw[:].rearrange("p (w m t) -> p w t m", w=2, t=PACK),
+            gather_scales(l)
+            gather_words(l, 0, picks[l])
+        nc.sync.dma_start(
+            out=moved_s[0 : P - 16].rearrange("p l j -> p (l j)").bitcast(I32),
+            in_=picked_s[16:P].rearrange("p l j -> p (l j)").bitcast(I32),
         )
-        for q in range(4):
-            nc.sync.dma_start(
-                out=w_s[32 * q : 32 * q + 4].rearrange("p a w n -> p a (w n)").bitcast(I32),
-                in_=ws_dealt[8 * q : 8 * q + 8].bitcast(I32),
+        for l in (SOURCE, TARGET):
+            part_words(l, 0, picks[l], at("early_parted%d" % l, [P, PASSES, 2 * HALF], U8, EARLY_PARTED_AT[l]))
+        for l in (SOURCE, TARGET):
+            quantize_wc(l)
+            picks[l] = at("late_pick%d" % l, [P, HALF], U32, LATE_PICK_AT[l])
+            gather_words(l, 1, picks[l])
+        part_words(SOURCE, 1, picks[SOURCE], at("late_parted0", [P, PASSES, 2 * HALF], U8, LATE_SOURCE_PARTED_AT))
+        part_words(TARGET, 1, picks[TARGET], sb("late_parted1", [P, PASSES, 2 * HALF], U8))
+        for t, offset in zip((2, 3), LATE_PAGES_AT):
+            pages[t] = at("page%d" % t, [P, T], F32, offset)
+            nc.gpsimd.memset(pages[t][:], 0.0)
+
+        def words(l, a, j0, w):
+            h, first = divmod(j0, HALF)
+            return v_w[l][h][:, a, 2 * first : 2 * (first + w)].bitcast(FP4X4)
+
+        def message_pass(out, a, b, n0, n1, start, stop):
+            nc.tensor.matmul_mx(
+                out=out,
+                lhsT=words(SOURCE, a, b * P, P),
+                lhsT_scale=v_s[a][:, SOURCE, b * P : (b + 1) * P],
+                rhs=wc_q[a][:, n0:n1].bitcast(FP8X4),
+                rhs_scale=wc_s[a][:, n0:n1],
+                start=start,
+                stop=stop,
             )
-        picks[SOURCE] = at("late_source_pick", [P, HALF], U32, LATE_SOURCE_PICK_AT)
-        gather_words(SOURCE, 1, picks[SOURCE][:])
-        quantize_wc(0)
-        wa_q = at("wa_q", [P, PASSES, N], I32, WA_DEALT_AT)
-        nc.vector.tensor_copy(
-            out=wa_q[:].rearrange("p a (t c e) -> p a c t e", t=PACK, e=4),
-            in_=wa_raw[:].rearrange("p a (c e t) -> p a c t e", t=PACK, e=4),
-        )
-        quantize_wc(1)
-        gather_scales(1, at("late_scales", [P, 2, HALF], U8, LATE_SCALES_AT), nc.sync)
-        picks[TARGET] = at("late_target_pick", [P, HALF], U32, LATE_TARGET_PICK_AT)
-        gather_words(TARGET, 1, picks[TARGET][:])
-        for l in (SOURCE, TARGET):
-            part_words(l, 1, picks[l][:], LATE_PARTED_AT[l])
 
-        msg_t = [sb("msg_t%d" % h, [P, BLOCKS, N], F32) for h in range(HALVES)]
-        eta = [sb("eta%d" % t, [P, J], F32) for t in range(PACK)]
-        msg = [sb("msg%d" % t, [P, J], F32) for t in range(PACK)]
-
-        def message_rows(h):
-            accs = [bank("msg_ps%d%d" % (h, b), ((0, 1, 2, 3), (4, 5, 3, 6))[h][b]) for b in range(BLOCKS)]
-            if h == 0:
-                order = [(a, b) for a in range(PASSES) for b in range(BLOCKS)]
-            else:
-                order = [(a, b) for b in range(BLOCKS) for a in range(PASSES)]
-            for a, b in order:
-                nc.tensor.matmul_mx(
-                    out=accs[b][:],
-                    lhsT=v_w[SOURCE][h][:, a, 2 * b * P : 2 * (b + 1) * P].bitcast(FP4X4),
-                    lhsT_scale=v_s[a][h][:, SOURCE, b * P : (b + 1) * P],
-                    rhs=wc_q[a][:].bitcast(FP8X4),
-                    rhs_scale=wc_s[a][:],
-                    start=(a == 0),
-                    stop=(a == PASSES - 1),
-                )
-            for b in range(BLOCKS):
-                nc.scalar.activation(
-                    out=msg_t[h][:, b, :].rearrange("p (t m) -> p t m", t=PACK),
-                    in_=accs[b][:].rearrange("p (m t) -> p t m", t=PACK),
-                    func=COPY,
-                    scale=wgo_col[:, BLOCKS * h + b : BLOCKS * h + b + 1],
+        def message_pair(acc, a, b0, n0):
+            for e in range(2):
+                message_pass(
+                    acc[:, e * QUARTER : (e + 1) * QUARTER], a, b0 + e, n0, n0 + QUARTER, a == 0 and e == 0, a == 1 and e == 1
                 )
 
-        def gate(t, h, number):
-            acc = bank("gate_ps%d%d" % (t, h), number)
-            js = slice(h * HALF, (h + 1) * HALF)
+        def weigh(out, in_, b):
+            nc.scalar.activation(out=out, in_=in_, func=COPY, scale=wgo_col[:, b : b + 1])
+
+        def gate_passes(acc, w, t, j0, width):
+            l = (TARGET, SOURCE)[w]
             for a in range(PASSES):
+                if w == WB:
+                    stationary = wb_q[:, a, 2 * t * P : 2 * (t + 1) * P].bitcast(FP4X4)
+                else:
+                    stationary = wa_q[:, a, t * P : (t + 1) * P].bitcast(FP8X4)
                 nc.tensor.matmul_mx(
-                    out=acc[:],
-                    lhsT=wb_q[:, a, 2 * t * P : 2 * (t + 1) * P].bitcast(FP4X4),
-                    lhsT_scale=w_s[:, a, 1, t * P : (t + 1) * P],
-                    rhs=v_w[SOURCE][h][:, a, :].bitcast(FP4X4),
-                    rhs_scale=v_s[a][h][:, SOURCE, :],
-                    start=(a == 0),
-                    stop=False,
+                    out=acc[:, 0:width],
+                    lhsT=stationary,
+                    lhsT_scale=w_s[:, a, w, t * P : (t + 1) * P],
+                    rhs=words(l, a, j0, width),
+                    rhs_scale=v_s[a][:, l, j0 : j0 + width],
+                    start=(w == WB and a == 0),
+                    stop=(w == WA and a == PASSES - 1),
                 )
-                nc.tensor.matmul_mx(
-                    out=acc[:],
-                    lhsT=wa_q[:, a, t * P : (t + 1) * P].bitcast(FP8X4),
-                    lhsT_scale=w_s[:, a, 0, t * P : (t + 1) * P],
-                    rhs=v_w[TARGET][h][:, a, :].bitcast(FP4X4),
-                    rhs_scale=v_s[a][h][:, TARGET, :],
-                    start=False,
-                    stop=(a == PASSES - 1),
-                )
-            nc.scalar.activation(out=eta[t][:, js], in_=acc[:], func=SIGMOID)
 
-        def turn_message(t, h, number):
-            turned = bank("turn_ps%d%d" % (t, h), number)
-            for b in range(BLOCKS):
-                nc.tensor.transpose(turned[:, b * P : (b + 1) * P], msg_t[h][:, b, t * P : (t + 1) * P], ident[:])
-            nc.scalar.copy(out=msg[t][:, h * HALF : (h + 1) * HALF], in_=turned[:])
+        def gate(out, t, j0, width, number):
+            acc = bank("gate_ps%d_%d" % (t, j0), number)
+            for w in (WB, WA):
+                gate_passes(acc, w, t, j0, width)
+            nc.scalar.activation(out=out, in_=acc[:, 0:width], func=SIGMOID)
 
-        def scatter(t, j0, j1):
-            nc.vector.tensor_tensor(
-                pages[t][:].indirect(lists[TARGET][:, j0 // 16 : j1 // 16]), eta[t][:, j0:j1], msg[t][:, j0:j1], MULT
-            )
+        def turn(out, rows, name, number):
+            turned = bank(name, number)
+            for e, block in enumerate(rows):
+                nc.tensor.transpose(turned[:, e * P : (e + 1) * P], block, ident[:])
+            nc.scalar.copy(out=out, in_=turned[:, 0 : len(rows) * P])
+
+        def scatter(t, j0, j1, eta, msg):
+            nc.vector.tensor_tensor(pages[t][:].indirect(lists[TARGET][:, j0 // 16 : j1 // 16]), eta, msg, MULT)
+
+        sums = [bank("msg_ps_a", 0), bank("msg_ps_b", 1)]
+        gates = [bank("gate_ps0_0", 2), bank("gate_ps1_0", 3)]
+        for q in range(2):
+            message_pair(sums[q], 0, 2 * q, 0)
+        for t in range(2):
+            gate_passes(gates[t], WB, t, 0, QUARTER)
+        message_pair(sums[0], 1, 0, 0)
+        for t in range(2):
+            gate_passes(gates[t], WA, t, 0, QUARTER)
+        message_pair(sums[1], 1, 2, 0)
+        for t in range(2):
+            rows = at("first_rows%d" % t, [P, 2, P], F32, FIRST_ROWS_AT[t])
+            eta = sb("eta0_0", [P, QUARTER], F32) if t == 0 else at("eta1_0", [P, QUARTER], F32, FIRST_ROWS_AT[0])
+            msg = sb("msg%d_0" % t, [P, QUARTER], F32)
+            for b in range(2):
+                weigh(rows[:, b, :], sums[0][:, b * QUARTER + t * P : b * QUARTER + (t + 1) * P], b)
+            nc.scalar.activation(out=eta[:], in_=gates[t][:, 0:QUARTER], func=SIGMOID)
+            turn(msg[:], [rows[:, b, :] for b in range(2)], "turn_ps%d_0" % t, 4 + t)
+            scatter(t, 0, QUARTER, eta[:], msg[:])
+        rows = at("second_rows", [P, 2, QUARTER], F32, FIRST_ROWS_AT[1])
+        for b in range(2):
+            weigh(rows[:, b, :], sums[1][:, b * QUARTER : (b + 1) * QUARTER], 2 + b)
+        for t in range(2):
+            eta = sb("eta%d_1" % t, [P, QUARTER], F32)
+            msg = sb("msg%d_1" % t, [P, QUARTER], F32)
+            gate(eta[:], t, QUARTER, QUARTER, 2 + t)
+            turn(msg[:], [rows[:, b, t * P : (t + 1) * P] for b in range(2)], "turn_ps%d_1" % t, 6 + t)
+            scatter(t, QUARTER, HALF, eta[:], msg[:])
+        late_rows = at("late_rows", [P, 4, N], F32, LATE_ROWS_AT)
+        for b, number in enumerate((0, 4, 5, 1)):
+            acc = bank("msg_ps_late%d" % b, number)
+            for a in range(PASSES):
+                message_pass(acc[:], a, 4 + b, 0, N, a == 0, a == PASSES - 1)
+            weigh(late_rows[:, b, :], acc[:], 4 + b)
+        for t in range(2):
+            eta = sb("eta%d_2" % t, [P, HALF], F32)
+            msg = sb("msg%d_2" % t, [P, HALF], F32)
+            gate(eta[:], t, HALF, HALF, 2 + t)
+            turn(msg[:], [late_rows[:, b, t * P : (t + 1) * P] for b in range(4)], "turn_ps%d_2" % t, 6 + t)
+            scatter(t, HALF, J, eta[:], msg[:])
+        other_rows = sb("other_rows", [P, 4, QUARTER], F32)
+        for q, number in enumerate((0, 4)):
+            acc = bank("msg_ps_other%d" % q, number)
+            for a in range(PASSES):
+                message_pair(acc, a, 2 * q, QUARTER)
+            for e in range(2):
+                weigh(other_rows[:, 2 * q + e, :], acc[:, e * QUARTER : (e + 1) * QUARTER], 2 * q + e)
+        operands = {}
+        for t, gate_banks, turn_banks in ((2, (5, 1), (2, 3)), (3, (6, 7), (0, 4))):
+            eta = sb("eta%d" % t, [P, J], F32)
+            msg = sb("msg%d" % t, [P, J], F32)
+            operands[t] = (eta, msg)
+            for h in range(2):
+                gate(eta[:, h * HALF : (h + 1) * HALF], t, h * HALF, HALF, gate_banks[h])
+            first = [other_rows[:, b, (t - 2) * P : (t - 1) * P] for b in range(4)]
+            turn(msg[:, 0:HALF], first, "turn_ps%d_0" % t, turn_banks[0])
+            turn(msg[:, HALF:J], [late_rows[:, b, t * P : (t + 1) * P] for b in range(4)], "turn_ps%d_1" % t, turn_banks[1])
 
         out_rows = out_0.rearrange("(p t) c -> p t c", t=PACK)
         y16 = {c0: sb("y16_%d" % c0, [P, w, PACK], BF16) for c0, w in ((VECTOR_START, VECTOR_COLS),) + PAIRED_CHUNKS + SCALAR_CHUNKS}
         y_q = sb("y_q", [P, T], U32)
         y_s = sb("y_s", [P, SCALE_COLS], U8)
         vector_cols = slice(VECTOR_START, VECTOR_START + VECTOR_COLS)
-
-        pages.extend([at("page1", [P, T], F32, PAGE1_AT), None, None])
-        nc.gpsimd.memset(pages[1][:], 0.0)
-        gate_banks = ((4, 4), (3, 0), (4, 3), (0, 6))
-        turn_banks = ((5, 0), (6, 1), (6, 5), (1, 5))
-        for h in range(HALVES):
-            message_rows(h)
-            for t in range(2):
-                gate(t, h, gate_banks[t][h])
-                turn_message(t, h, turn_banks[t][h])
-            for t in range(2):
-                scatter(t, h * HALF, (h + 1) * HALF)
-        for t, offset in zip((2, 3), LATE_PAGES_AT):
-            pages[t] = at("page%d" % t, [P, T], F32, offset)
-            nc.gpsimd.memset(pages[t][:], 0.0)
-        for t in (2, 3):
-            for h in range(HALVES):
-                turn_message(t, h, turn_banks[t][h])
-            for h in range(HALVES):
-                gate(t, h, gate_banks[t][h])
-
-        low_v = sb("low_v", [P, 2, VECTOR_COLS], BF16, "msg_t0")
-        low_s = sb("low_s", [P, 3, SCALAR_COLS], BF16, "msg_t1")
-        high_v = at("high_v", [P, 2, VECTOR_COLS], BF16, W_PLANES_AT)
-        pairs = {
-            c0: at("pairs%d" % c0, [P, 2, w, 2], BF16, offset)
-            for (c0, w), offset in zip(PAIRED_CHUNKS, (WA_DEALT_AT, WB_DEALT_AT))
-        }
+        low_v = at("low_v", [P, 2, VECTOR_COLS], BF16, LOW_V_AT)
+        low_s = at("low_s", [P, 3, SCALAR_COLS], BF16, LOW_S_AT)
+        high_v = at("high_v", [P, 2, VECTOR_COLS], BF16, HIGH_V_AT)
+        pairs = {c0: at("pairs%d" % c0, [P, 2, w, 2], BF16, offset) for (c0, w), offset in zip(PAIRED_CHUNKS, PAIRS_AT)}
 
         def round_into_pairs(t, c0, w):
             nc.scalar.copy(out=pairs[c0][:, t // 2, :, t % 2], in_=pages[t][:, c0 : c0 + w])
 
         for t in range(PACK):
             if t > 1:
-                scatter(t, 0, J)
+                scatter(t, 0, J, operands[t][0][:], operands[t][1][:])
             nc.sync.dma_start(out=out_rows[:, t, :], in_=pages[t][:])
             if t < 2:
                 nc.scalar.copy(out=low_v[:, t, :], in_=pages[t][:, vector_cols])

@@ -33,12 +33,13 @@ PAIRED_CHUNKS = ((1024, 512), (1536, 512))
 PIECE = 256
 SCALE_COLS = 512
 
-EARLY_PARTED_AT = (0, 2048)
-WB_RAW_AT = 1024
-WS_RAW_AT = 4096
-PAGE1_AT = 4096
+EARLY_TARGET_PARTED_AT = 0
+WB_RAW_AT = 1984
+WC_SCALES_AT = 2560
+WS_RAW_AT = 58368
+PAGE1_AT = 58368
 WC_RAW_AT = (12288, 22464)
-LATE_PICK_AT = (12288, 29632)
+LATE_PICK_AT = (3968, 29632)
 LATE_SOURCE_PARTED_AT = 20480
 LATE_PAGES_AT = (22528, 30720)
 FIRST_ROWS_AT = (38912, 39936)
@@ -89,18 +90,21 @@ def tile_list_rgg_noneP_kernel(
         nc.gpsimd.memset(w_s[:].rearrange("p a w n -> p (a w n)").bitcast(I32), 0)
         nc.gpsimd.memset(moved_s[96:P].rearrange("p l j -> p (l j)").bitcast(I32), 0)
 
+        def load_wc(a):
+            nc.sync.dma_start(out=wc_raw[a][:], in_=wc[512 * a : 512 * (a + 1), :].rearrange("(p i) n -> p i n", i=PACK))
+
         nc.sync.dma_start(lists[SOURCE][:], offs)
         for w, src in ((WA, wa_scales), (WB, wb_scales)):
             nc.sync.dma_start(out=ws_raw[w:64:2].bitcast(I32), in_=src.rearrange("a g n -> g a n").bitcast(I32))
         by_row = tab_scales.rearrange("a (q r) t -> r q a t", r=4)
         for r in range(4):
             nc.sync.dma_start(out=tab_s[r:P:16, :].bitcast(I32), in_=by_row[r].bitcast(I32))
-        nc.sync.dma_start(out=tab_w[:].bitcast(I32), in_=tab_words[0].rearrange("p t b -> p (t b)").bitcast(I32))
+        load_wc(0)
         nc.sync.dma_start(lists[TARGET][:], offs2)
+        nc.sync.dma_start(out=tab_w[:].bitcast(I32), in_=tab_words[0].rearrange("p t b -> p (t b)").bitcast(I32))
         nc.sync.dma_start(out=wb_raw[:].bitcast(I32), in_=wb_words.rearrange("a p c -> p a c").bitcast(I32))
         nc.sync.dma_start(out=wgo_rows[0 : J // P, :], in_=wgo[0].rearrange("(c m) -> c m", m=P))
-        for a in range(PASSES):
-            nc.sync.dma_start(out=wc_raw[a][:], in_=wc[512 * a : 512 * (a + 1), :].rearrange("(p i) n -> p i n", i=PACK))
+        load_wc(1)
         nc.sync.dma_start(out=wa_raw[:].bitcast(I32), in_=wa_words.rearrange("a p n i -> p a (n i)").bitcast(I32))
 
         ws_dealt = sb("ws_dealt", [P, N], U8)
@@ -124,10 +128,10 @@ def tile_list_rgg_noneP_kernel(
         nc.tensor.transpose(wgo_ps[:, 0:P], wgo_rows[:], ident[:])
         nc.scalar.copy(out=wgo_col[:], in_=wgo_ps[:, 0 : J // P])
         wc16 = [sb("wc16_%d" % a, [P, N * PACK], BF16) for a in range(PASSES)]
-        for a in range(PASSES):
+        for a, t0, t1 in ((0, 0, 4), (1, 0, 2), (1, 2, 4)):
             nc.scalar.copy(
-                out=wc16[a][:].rearrange("p (t m i) -> p m i t", t=PACK, i=PACK),
-                in_=wc_raw[a][:].rearrange("p i (m t) -> p m i t", t=PACK),
+                out=wc16[a][:].rearrange("p (t m i) -> p m i t", t=PACK, i=PACK)[:, :, :, t0:t1],
+                in_=wc_raw[a][:].rearrange("p i (m t) -> p m i t", t=PACK)[:, :, :, t0:t1],
             )
         wa_q = sb("wa_q", [P, PASSES, N], U32)
         nc.scalar.copy(
@@ -137,7 +141,7 @@ def tile_list_rgg_noneP_kernel(
         picked_s = sb("picked_s", [P, 2, J], U8)
         v_s = [picked_s, moved_s]
         wc_q = [sb("wc_q%d" % a, [P, N], U32) for a in range(PASSES)]
-        wc_s = [sb("wc_s%d" % a, [P, N], U8) for a in range(PASSES)]
+        wc_s = [at("wc_s0", [P, N], U8, WC_SCALES_AT), sb("wc_s1", [P, N], U8)]
         v_w = [[None, None], [None, None]]
 
         def gather_scales(l):
@@ -152,23 +156,28 @@ def tile_list_rgg_noneP_kernel(
                 out=parted[:].bitcast(U16), in_=picked[:].bitcast(U16).rearrange("p (j d) -> p d j", d=PASSES)
             )
 
-        def quantize_wc(a):
-            nc.vector.quantize_mx(out=wc_q[a][:].bitcast(FP8X4), scales=wc_s[a][:], in_=wc16[a][:])
+        def quantize_wc(a, n0, n1):
+            nc.vector.quantize_mx(
+                out=wc_q[a][:, n0:n1].bitcast(FP8X4), scales=wc_s[a][:, n0:n1], in_=wc16[a][:, PACK * n0 : PACK * n1]
+            )
 
         picks = [sb("early_pick%d" % l, [P, HALF], U32) for l in (SOURCE, TARGET)]
         for l in (SOURCE, TARGET):
             gather_scales(l)
+        for l in (SOURCE, TARGET):
             gather_words(l, 0, picks[l])
         nc.sync.dma_start(
             out=moved_s[0 : P - 16].rearrange("p l j -> p (l j)").bitcast(I32),
             in_=picked_s[16:P].rearrange("p l j -> p (l j)").bitcast(I32),
         )
-        for l in (SOURCE, TARGET):
-            part_words(l, 0, picks[l], at("early_parted%d" % l, [P, PASSES, 2 * HALF], U8, EARLY_PARTED_AT[l]))
-        for l in (SOURCE, TARGET):
-            quantize_wc(l)
-            picks[l] = at("late_pick%d" % l, [P, HALF], U32, LATE_PICK_AT[l])
-            gather_words(l, 1, picks[l])
+        part_words(SOURCE, 0, picks[SOURCE], sb("early_parted0", [P, PASSES, 2 * HALF], U8))
+        quantize_wc(0, 0, N)
+        part_words(TARGET, 0, picks[TARGET], at("early_parted1", [P, PASSES, 2 * HALF], U8, EARLY_TARGET_PARTED_AT))
+        picks = [at("late_pick%d" % l, [P, HALF], U32, LATE_PICK_AT[l]) for l in (SOURCE, TARGET)]
+        gather_words(SOURCE, 1, picks[SOURCE])
+        quantize_wc(1, 0, N // 2)
+        gather_words(TARGET, 1, picks[TARGET])
+        quantize_wc(1, N // 2, N)
         part_words(SOURCE, 1, picks[SOURCE], at("late_parted0", [P, PASSES, 2 * HALF], U8, LATE_SOURCE_PARTED_AT))
         part_words(TARGET, 1, picks[TARGET], sb("late_parted1", [P, PASSES, 2 * HALF], U8))
         for t, offset in zip((2, 3), LATE_PAGES_AT):
@@ -237,10 +246,10 @@ def tile_list_rgg_noneP_kernel(
             message_pair(sums[q], 0, 2 * q, 0)
         for t in range(2):
             gate_passes(gates[t], WB, t, 0, QUARTER)
-        message_pair(sums[0], 1, 0, 0)
+        for q in range(2):
+            message_pair(sums[q], 1, 2 * q, 0)
         for t in range(2):
             gate_passes(gates[t], WA, t, 0, QUARTER)
-        message_pair(sums[1], 1, 2, 0)
         for t in range(2):
             rows = at("first_rows%d" % t, [P, 2, P], F32, FIRST_ROWS_AT[t])
             eta = sb("eta0_0", [P, QUARTER], F32) if t == 0 else at("eta1_0", [P, QUARTER], F32, FIRST_ROWS_AT[0])

@@ -268,35 +268,34 @@ def tile_list_rgg_noneP_kernel(
             gate(eta[:], t, QUARTER, QUARTER, 2 + t)
             turn(msg[:], [rows[:, b, t * P : (t + 1) * P] for b in range(2)], "turn_ps%d_1" % t, 6 + t)
             scatter(t, QUARTER, HALF, eta[:], msg[:])
-        late_rows = at("late_rows", [P, 4, N], F32, LATE_ROWS_AT)
-        for b, number in enumerate((0, 4, 5, 1)):
-            acc = bank("msg_ps_late%d" % b, number)
-            for a in range(PASSES):
-                message_pass(acc[:], a, 4 + b, 0, N, a == 0, a == PASSES - 1)
-            weigh(late_rows[:, b, :], acc[:], 4 + b)
+        def message_rows(rows, b0, n0, numbers):
+            for q, number in enumerate(numbers):
+                acc = bank("msg_ps%d_%d" % (b0 + 2 * q, n0), number)
+                for a in range(PASSES):
+                    message_pair(acc, a, b0 + 2 * q, n0)
+                for e in range(2):
+                    weigh(rows[:, 2 * q + e, :], acc[:, e * QUARTER : (e + 1) * QUARTER], b0 + 2 * q + e)
+
+        late_rows = at("late_rows", [P, 4, QUARTER], F32, LATE_ROWS_AT)
+        message_rows(late_rows, 4, 0, (0, 4))
         for t in range(2):
             eta = sb("eta%d_2" % t, [P, HALF], F32)
             msg = sb("msg%d_2" % t, [P, HALF], F32)
             gate(eta[:], t, HALF, HALF, 2 + t)
             turn(msg[:], [late_rows[:, b, t * P : (t + 1) * P] for b in range(4)], "turn_ps%d_2" % t, 6 + t)
             scatter(t, HALF, J, eta[:], msg[:])
-        other_rows = sb("other_rows", [P, 4, QUARTER], F32)
-        for q, number in enumerate((0, 4)):
-            acc = bank("msg_ps_other%d" % q, number)
-            for a in range(PASSES):
-                message_pair(acc, a, 2 * q, QUARTER)
-            for e in range(2):
-                weigh(other_rows[:, 2 * q + e, :], acc[:, e * QUARTER : (e + 1) * QUARTER], 2 * q + e)
+        other_rows = at("other_rows", [P, 8, QUARTER], F32, LATE_ROWS_AT)
+        message_rows(other_rows, 0, QUARTER, (5, 1, 0, 4))
         operands = {}
-        for t, gate_banks, turn_banks in ((2, (5, 1), (2, 3)), (3, (6, 7), (0, 4))):
+        for t, gate_banks, turn_banks in ((2, (2, 3), (6, 7)), (3, (5, 1), (0, 4))):
             eta = sb("eta%d" % t, [P, J], F32)
             msg = sb("msg%d" % t, [P, J], F32)
             operands[t] = (eta, msg)
             for h in range(2):
                 gate(eta[:, h * HALF : (h + 1) * HALF], t, h * HALF, HALF, gate_banks[h])
-            first = [other_rows[:, b, (t - 2) * P : (t - 1) * P] for b in range(4)]
-            turn(msg[:, 0:HALF], first, "turn_ps%d_0" % t, turn_banks[0])
-            turn(msg[:, HALF:J], [late_rows[:, b, t * P : (t + 1) * P] for b in range(4)], "turn_ps%d_1" % t, turn_banks[1])
+            for h in range(2):
+                rows = [other_rows[:, 4 * h + b, (t - 2) * P : (t - 1) * P] for b in range(4)]
+                turn(msg[:, h * HALF : (h + 1) * HALF], rows, "turn_ps%d_%d" % (t, h), turn_banks[h])
 
         out_rows = out_0.rearrange("(p t) c -> p t c", t=PACK)
         y16 = {c0: sb("y16_%d" % c0, [P, w, PACK], BF16) for c0, w in ((VECTOR_START, VECTOR_COLS),) + PAIRED_CHUNKS + SCALAR_CHUNKS}
@@ -318,7 +317,10 @@ def tile_list_rgg_noneP_kernel(
             if t < 2:
                 nc.scalar.copy(out=low_v[:, t, :], in_=pages[t][:, vector_cols])
             if t == 1:
-                nc.scalar.copy(out=y16[VECTOR_START][:, :, 0:2], in_=low_v[:].rearrange("p t c -> p c t"))
+                nc.scalar.copy(
+                    out=y16[VECTOR_START][:, :, 0:2].rearrange("p (c e) t -> p c t e", e=4),
+                    in_=low_v[:].rearrange("p t (c e) -> p c t e", e=4),
+                )
             if t == 2:
                 nc.scalar.copy(out=high_v[:, 0, :], in_=pages[2][:, vector_cols])
             if t < 3:
@@ -327,7 +329,10 @@ def tile_list_rgg_noneP_kernel(
                     round_into_pairs(t, c0, w)
             if t == 2:
                 for c0, w in SCALAR_CHUNKS:
-                    nc.scalar.copy(out=y16[c0][:, :, 0:3], in_=low_s[:, :, c0 : c0 + w].rearrange("p t c -> p c t"))
+                    nc.scalar.copy(
+                        out=y16[c0][:, :, 0:3].rearrange("p (c e) t -> p c t e", e=4),
+                        in_=low_s[:, :, c0 : c0 + w].rearrange("p t (c e) -> p c t e", e=4),
+                    )
 
         codes_out = out_1[0].rearrange("p t b -> p (t b)").bitcast(I32)
 
@@ -357,10 +362,11 @@ def tile_list_rgg_noneP_kernel(
             if c0 == vector_cols.stop:
                 quantize_out(VECTOR_START, 0)
                 quantize_out(c0, 0)
+                store_codes(VECTOR_START, c0 + PIECE)
         for c0, w in PAIRED_CHUNKS + SCALAR_CHUNKS:
             for piece in range(1 if c0 == vector_cols.stop else 0, w // PIECE):
                 quantize_out(c0, piece)
-            store_codes(VECTOR_START if c0 == vector_cols.stop else c0, c0 + w)
+            store_codes(c0 + PIECE if c0 == vector_cols.stop else c0, c0 + w)
         scale_rows = out_2[0].bitcast(I32).rearrange("(q r) (k c) -> q k r c", r=4, k=T // SCALE_COLS)
         for q in range(4):
             (nc.scalar, nc.sync)[q % 2].dma_start(out=scale_rows[q], in_=y_s[32 * q : 32 * q + 16, :].bitcast(I32))

@@ -36,16 +36,17 @@ SCALE_COLS = 512
 EARLY_TARGET_PARTED_AT = 0
 WB_RAW_AT = 1984
 WC_SCALES_AT = 2560
-WS_RAW_AT = 58368
-PAGE1_AT = 58368
+WS_RAW_AT = 66560
+PAGE1_AT = 66560
 WC_RAW_AT = (12288, 22464)
 LATE_PICK_AT = (3968, 29632)
 LATE_SOURCE_PARTED_AT = 20480
 LATE_PAGES_AT = (22528, 30720)
 FIRST_ROWS_AT = (38912, 39936)
 PAIRS_AT = (41984, 54144)
-LATE_ROWS_AT = 46016
-LOW_S_AT, LOW_V_AT, HIGH_V_AT = 46080, 50688, 51712
+LATE_ROWS_AT = 54144
+OTHER_ROWS_AT = (46016, 58240)
+LOW_S_AT, LOW_V_AT, HIGH_V_AT = 46080, 50688, 58240
 
 
 def tile_list_rgg_noneP_kernel(
@@ -276,7 +277,7 @@ def tile_list_rgg_noneP_kernel(
                 for e in range(2):
                     weigh(rows[:, 2 * q + e, :], acc[:, e * QUARTER : (e + 1) * QUARTER], b0 + 2 * q + e)
 
-        late_rows = at("late_rows", [P, 4, QUARTER], F32, LATE_ROWS_AT)
+        late_rows = at("late_rows", [P, 5, QUARTER], F32, LATE_ROWS_AT)
         message_rows(late_rows, 4, 0, (0, 4))
         for t in range(2):
             eta = sb("eta%d_2" % t, [P, HALF], F32)
@@ -284,19 +285,30 @@ def tile_list_rgg_noneP_kernel(
             gate(eta[:], t, HALF, HALF, 2 + t)
             turn(msg[:], [late_rows[:, b, t * P : (t + 1) * P] for b in range(4)], "turn_ps%d_2" % t, 6 + t)
             scatter(t, HALF, J, eta[:], msg[:])
-        other_rows = at("other_rows", [P, 8, QUARTER], F32, LATE_ROWS_AT)
-        message_rows(other_rows, 0, QUARTER, (5, 1, 0, 4))
-        operands = {}
-        for t, gate_banks, turn_banks in ((2, (2, 3), (6, 7)), (3, (5, 1), (0, 4))):
+        sums = [bank("msg_ps_other%d" % q, number) for q, number in enumerate((5, 1, 0, 4))]
+        for q in range(4):
+            for a in range(PASSES):
+                message_pair(sums[q], a, 2 * q, QUARTER)
+
+        def weigh_page(t):
+            rows = at("other_rows%d" % t, [P, 8 * (4 - t), P], F32, OTHER_ROWS_AT[t - 2])
+            for b in range(8):
+                first = (b % 2) * QUARTER + (t - 2) * P
+                weigh(rows[:, b, :], sums[b // 2][:, first : first + P], b)
+            return rows
+
+        def whole_page(t, rows, turn_banks):
             eta = sb("eta%d" % t, [P, J], F32)
             msg = sb("msg%d" % t, [P, J], F32)
-            operands[t] = (eta, msg)
             for h in range(2):
-                gate(eta[:, h * HALF : (h + 1) * HALF], t, h * HALF, HALF, gate_banks[h])
+                gate(eta[:, h * HALF : (h + 1) * HALF], t, h * HALF, HALF, 2 + h)
             for h in range(2):
-                rows = [other_rows[:, 4 * h + b, (t - 2) * P : (t - 1) * P] for b in range(4)]
-                turn(msg[:, h * HALF : (h + 1) * HALF], rows, "turn_ps%d_%d" % (t, h), turn_banks[h])
+                blocks = [rows[:, 4 * h + b, :] for b in range(4)]
+                turn(msg[:, h * HALF : (h + 1) * HALF], blocks, "turn_ps%d_%d" % (t, h), turn_banks[h])
+            return eta, msg
 
+        operands = [whole_page(2, weigh_page(2), (6, 7))]
+        last_rows = weigh_page(3)
         out_rows = out_0.rearrange("(p t) c -> p t c", t=PACK)
         y16 = {c0: sb("y16_%d" % c0, [P, w, PACK], BF16) for c0, w in ((VECTOR_START, VECTOR_COLS),) + PAIRED_CHUNKS + SCALAR_CHUNKS}
         y_q = sb("y_q", [P, T], U32)
@@ -304,15 +316,12 @@ def tile_list_rgg_noneP_kernel(
         vector_cols = slice(VECTOR_START, VECTOR_START + VECTOR_COLS)
         low_v = at("low_v", [P, 2, VECTOR_COLS], BF16, LOW_V_AT)
         low_s = at("low_s", [P, 3, SCALAR_COLS], BF16, LOW_S_AT)
-        high_v = at("high_v", [P, 2, VECTOR_COLS], BF16, HIGH_V_AT)
         pairs = {c0: at("pairs%d" % c0, [P, 2, w, 2], BF16, offset) for (c0, w), offset in zip(PAIRED_CHUNKS, PAIRS_AT)}
 
         def round_into_pairs(t, c0, w):
             nc.scalar.copy(out=pairs[c0][:, t // 2, :, t % 2], in_=pages[t][:, c0 : c0 + w])
 
-        for t in range(PACK):
-            if t > 1:
-                scatter(t, 0, J, operands[t][0][:], operands[t][1][:])
+        def finish_page(t):
             nc.sync.dma_start(out=out_rows[:, t, :], in_=pages[t][:])
             if t < 2:
                 nc.scalar.copy(out=low_v[:, t, :], in_=pages[t][:, vector_cols])
@@ -333,6 +342,14 @@ def tile_list_rgg_noneP_kernel(
                         out=y16[c0][:, :, 0:3].rearrange("p (c e) t -> p c t e", e=4),
                         in_=low_s[:, :, c0 : c0 + w].rearrange("p t (c e) -> p c t e", e=4),
                     )
+
+        finish_page(0)
+        operands.append(whole_page(3, last_rows, (5, 1)))
+        finish_page(1)
+        high_v = at("high_v", [P, 2, VECTOR_COLS], BF16, HIGH_V_AT)
+        for t, (eta, msg) in zip((2, 3), operands):
+            scatter(t, 0, J, eta[:], msg[:])
+            finish_page(t)
 
         codes_out = out_1[0].rearrange("p t b -> p (t b)").bitcast(I32)
 

@@ -266,7 +266,7 @@ def tile_list_rgg_noneP_kernel(
         for t in range(2):
             eta = sb("eta%d_1" % t, [P, QUARTER], F32)
             msg = sb("msg%d_1" % t, [P, QUARTER], F32)
-            gate(eta[:], t, QUARTER, QUARTER, 2 + t)
+            gate(eta[:], t, QUARTER, QUARTER, (2, 4)[t])
             turn(msg[:], [rows[:, b, t * P : (t + 1) * P] for b in range(2)], "turn_ps%d_1" % t, 6 + t)
             scatter(t, QUARTER, HALF, eta[:], msg[:])
         def message_rows(rows, b0, n0, numbers):
@@ -278,14 +278,14 @@ def tile_list_rgg_noneP_kernel(
                     weigh(rows[:, 2 * q + e, :], acc[:, e * QUARTER : (e + 1) * QUARTER], b0 + 2 * q + e)
 
         late_rows = at("late_rows", [P, 5, QUARTER], F32, LATE_ROWS_AT)
-        message_rows(late_rows, 4, 0, (0, 4))
+        message_rows(late_rows, 4, 0, (0, 3))
         for t in range(2):
             eta = sb("eta%d_2" % t, [P, HALF], F32)
             msg = sb("msg%d_2" % t, [P, HALF], F32)
-            gate(eta[:], t, HALF, HALF, 2 + t)
-            turn(msg[:], [late_rows[:, b, t * P : (t + 1) * P] for b in range(4)], "turn_ps%d_2" % t, 6 + t)
+            gate(eta[:], t, HALF, HALF, (5, 1)[t])
+            turn(msg[:], [late_rows[:, b, t * P : (t + 1) * P] for b in range(4)], "turn_ps%d_2" % t, (2, 4)[t])
             scatter(t, HALF, J, eta[:], msg[:])
-        sums = [bank("msg_ps_other%d" % q, number) for q, number in enumerate((5, 1, 0, 4))]
+        sums = [bank("msg_ps_other%d" % q, number) for q, number in enumerate((6, 7, 5, 2))]
         for q in range(4):
             for a in range(PASSES):
                 message_pair(sums[q], a, 2 * q, QUARTER)
@@ -301,13 +301,13 @@ def tile_list_rgg_noneP_kernel(
             eta = sb("eta%d" % t, [P, J], F32)
             msg = sb("msg%d" % t, [P, J], F32)
             for h in range(2):
-                gate(eta[:, h * HALF : (h + 1) * HALF], t, h * HALF, HALF, 2 + h)
+                gate(eta[:, h * HALF : (h + 1) * HALF], t, h * HALF, HALF, (1, 4)[h])
             for h in range(2):
                 blocks = [rows[:, 4 * h + b, :] for b in range(4)]
                 turn(msg[:, h * HALF : (h + 1) * HALF], blocks, "turn_ps%d_%d" % (t, h), turn_banks[h])
             return eta, msg
 
-        operands = [whole_page(2, weigh_page(2), (6, 7))]
+        operands = [whole_page(2, weigh_page(2), (0, 3))]
         last_rows = weigh_page(3)
         out_rows = out_0.rearrange("(p t) c -> p t c", t=PACK)
         y16 = {c0: sb("y16_%d" % c0, [P, w, PACK], BF16) for c0, w in ((VECTOR_START, VECTOR_COLS),) + PAIRED_CHUNKS + SCALAR_CHUNKS}
@@ -344,7 +344,7 @@ def tile_list_rgg_noneP_kernel(
                     )
 
         finish_page(0)
-        operands.append(whole_page(3, last_rows, (5, 1)))
+        operands.append(whole_page(3, last_rows, (6, 7)))
         finish_page(1)
         high_v = at("high_v", [P, 2, VECTOR_COLS], BF16, HIGH_V_AT)
         for t, (eta, msg) in zip((2, 3), operands):

from contextlib import ExitStack

import concourse.mybir as mybir
from concourse.masks import make_identity

K, N, T, J = 1024, 512, 2048, 1024
FLOPS = 3 * 2 * K * N * J

F32 = mybir.dt.float32
BF16 = mybir.dt.bfloat16
I32 = mybir.dt.int32
U32 = mybir.dt.uint32
U16 = mybir.dt.uint16
U8 = mybir.dt.uint8
FP8X4 = mybir.dt.float8_e4m3fn_x4
FP4X4 = mybir.dt.float4_e2m1fn_x4
MULT = mybir.AluOpType.mult
COPY = mybir.ActivationFunctionType.Copy
SIGMOID = mybir.ActivationFunctionType.Sigmoid

P = 128
PACK = 4
PASSES = K // (P * PACK)
HALF = 512
QUARTER = 256
SOURCE, TARGET = 0, 1
WA, WB = 0, 1

SCALAR_CHUNKS = ((0, 512), (512, 256))
SCALAR_COLS = 768
VECTOR_START, VECTOR_COLS = 768, 256
PAIRED_CHUNKS = ((1024, 512), (1536, 512))
PIECE = 256
SCALE_COLS = 512

EARLY_TARGET_PARTED_AT = 0
WB_RAW_AT = 1984
WC_SCALES_AT = 2560
WS_RAW_AT = 66560
PAGE1_AT = 66560
WC_RAW_AT = (12288, 22464)
LATE_PICK_AT = (3968, 29632)
LATE_SOURCE_PARTED_AT = 20480
LATE_PAGES_AT = (22528, 30720)
FIRST_ROWS_AT = (38912, 39936)
PAIRS_AT = (41984, 54144)
LATE_ROWS_AT = 54144
OTHER_ROWS_AT = (46016, 58240)
LOW_S_AT, LOW_V_AT, HIGH_V_AT = 46080, 50688, 58240


def tile_list_rgg_noneP_kernel(
    tc, tab_words, tab_scales, wa_words, wa_scales, wb_words, wb_scales, wc, wgo, offs, offs2, out_0, out_1, out_2
):
    nc = tc.nc
    with ExitStack() as ctx:
        keep = ctx.enter_context(tc.tile_pool(name="keep", bufs=1))
        psum = ctx.enter_context(tc.psum_pool(name="psum", bufs=1))
        arena = ctx.enter_context(tc.tile_pool(name="arena", bufs=1))

        def bank(name, number):
            return psum.tile([P, HALF], F32, name=name, tag=name, offset=2048 * number)

        def sb(name, shape, dtype):
            return keep.tile(shape, dtype, name=name, tag=name, align_bytes=64)

        def at(name, shape, dtype, offset):
            return arena.tile(shape, dtype, name=name, tag=name, align_bytes=64, offset=offset)

        lists = [sb("offs_sb", [P, J // 16], U16), sb("offs2_sb", [P, J // 16], U16)]
        tab_s = sb("tab_s", [P, T], U8)
        tab_w = sb("tab_w", [P, T], U32)
        wa_raw = sb("wa_raw", [P, PASSES, N], U32)
        wb_raw = at("wb_raw", [P, PASSES, 2 * N], U8, WB_RAW_AT)
        ws_raw = at("ws_raw", [P, N], U8, WS_RAW_AT)
        w_s = sb("w_s", [P, PASSES, 2, N], U8)
        moved_s = sb("moved_s", [P, 2, J], U8)
        wc_raw = [at("wc_raw%d" % a, [P, PACK, N], F32, WC_RAW_AT[a]) for a in range(PASSES)]
        wgo_rows = sb("wgo_rows", [P, P], F32)
        wgo_col = sb("wgo_col", [P, J // P], F32)
        pages = [sb("page0", [P, T], F32), None, None, None]

        nc.vector.memset(tab_s[:].bitcast(I32), 0)
        nc.vector.memset(pages[0][:], 0.0)
        nc.gpsimd.memset(wgo_rows[:], 0.0)
        nc.gpsimd.memset(ws_raw[64:P].bitcast(I32), 0)
        warm = sb("warm", [P, 8], F32)
        nc.scalar.activation(out=warm[:, 0:1], in_=wgo_rows[:, 0:1], func=SIGMOID)
        ident = sb("ident", [P, P], F32)
        make_identity(nc, ident[:])
        nc.gpsimd.memset(w_s[:].rearrange("p a w n -> p (a w n)").bitcast(I32), 0)
        nc.gpsimd.memset(moved_s[96:P].rearrange("p l j -> p (l j)").bitcast(I32), 0)

        def load_wc(a):
            nc.sync.dma_start(out=wc_raw[a][:], in_=wc[512 * a : 512 * (a + 1), :].rearrange("(p i) n -> p i n", i=PACK))

        nc.sync.dma_start(lists[SOURCE][:], offs)
        for w, src in ((WA, wa_scales), (WB, wb_scales)):
            nc.sync.dma_start(out=ws_raw[w:64:2].bitcast(I32), in_=src.rearrange("a g n -> g a n").bitcast(I32))
        by_row = tab_scales.rearrange("a (q r) t -> r q a t", r=4)
        for r in range(4):
            nc.sync.dma_start(out=tab_s[r:P:16, :].bitcast(I32), in_=by_row[r].bitcast(I32))
        load_wc(0)
        nc.sync.dma_start(lists[TARGET][:], offs2)
        nc.sync.dma_start(out=tab_w[:].bitcast(I32), in_=tab_words[0].rearrange("p t b -> p (t b)").bitcast(I32))
        nc.sync.dma_start(out=wb_raw[:].bitcast(I32), in_=wb_words.rearrange("a p c -> p a c").bitcast(I32))
        nc.sync.dma_start(out=wgo_rows[0 : J // P, :], in_=wgo[0].rearrange("(c m) -> c m", m=P))
        load_wc(1)
        nc.sync.dma_start(out=wa_raw[:].bitcast(I32), in_=wa_words.rearrange("a p n i -> p a (n i)").bitcast(I32))

        ws_dealt = sb("ws_dealt", [P, N], U8)
        nc.vector.tensor_copy(
            out=ws_dealt[:].rearrange("p (t m) -> p t m", t=PACK), in_=ws_raw[:].rearrange("p (m t) -> p t m", t=PACK)
        )
        for q in range(4):
            nc.sync.dma_start(
                out=w_s[32 * q : 32 * q + 4].rearrange("p a w n -> p (a w) n").bitcast(I32),
                in_=ws_dealt[16 * q : 16 * q + 16].bitcast(I32),
            )
        pages[1] = at("page1", [P, T], F32, PAGE1_AT)
        nc.gpsimd.memset(pages[1][:], 0.0)

        wb_q = sb("wb_q", [P, PASSES, 2 * N], U8)
        nc.scalar.copy(
            out=wb_q[:].bitcast(U16).rearrange("p a (t m) -> p a m t", t=PACK),
            in_=wb_raw[:].bitcast(U16).rearrange("p a (m t) -> p a m t", t=PACK),
        )
        wgo_ps = bank("wgo_ps", 7)
        nc.tensor.transpose(wgo_ps[:, 0:P], wgo_rows[:], ident[:])
        nc.scalar.copy(out=wgo_col[:], in_=wgo_ps[:, 0 : J // P])
        wc16 = [sb("wc16_%d" % a, [P, N * PACK], BF16) for a in range(PASSES)]
        for a, t0, t1 in ((0, 0, 4), (1, 0, 2), (1, 2, 4)):
            nc.scalar.copy(
                out=wc16[a][:].rearrange("p (t m i) -> p m i t", t=PACK, i=PACK)[:, :, :, t0:t1],
                in_=wc_raw[a][:].rearrange("p i (m t) -> p m i t", t=PACK)[:, :, :, t0:t1],
            )
        wa_q = sb("wa_q", [P, PASSES, N], U32)
        nc.scalar.copy(
            out=wa_q[:].rearrange("p a (t m) -> p a m t", t=PACK), in_=wa_raw[:].rearrange("p a (m t) -> p a m t", t=PACK)
        )

        picked_s = sb("picked_s", [P, 2, J], U8)
        v_s = [picked_s, moved_s]
        wc_q = [sb("wc_q%d" % a, [P, N], U32) for a in range(PASSES)]
        wc_s = [at("wc_s0", [P, N], U8, WC_SCALES_AT), sb("wc_s1", [P, N], U8)]
        v_w = [[None, None], [None, None]]

        def gather_scales(l):
            nc.vector.tensor_copy(picked_s[:, l, :], tab_s[:].indirect(lists[l][:]))

        def gather_words(l, h, picked):
            nc.vector.tensor_copy(picked[:], tab_w[:].indirect(lists[l][:, h * HALF // 16 : (h + 1) * HALF // 16]))

        def part_words(l, h, picked, parted):
            v_w[l][h] = parted
            nc.vector.tensor_copy(
                out=parted[:].bitcast(U16), in_=picked[:].bitcast(U16).rearrange("p (j d) -> p d j", d=PASSES)
            )

        def quantize_wc(a, n0, n1):
            nc.vector.quantize_mx(
                out=wc_q[a][:, n0:n1].bitcast(FP8X4), scales=wc_s[a][:, n0:n1], in_=wc16[a][:, PACK * n0 : PACK * n1]
            )

        picks = [sb("early_pick%d" % l, [P, HALF], U32) for l in (SOURCE, TARGET)]
        for l in (SOURCE, TARGET):
            gather_scales(l)
        for l in (SOURCE, TARGET):
            gather_words(l, 0, picks[l])
        nc.sync.dma_start(
            out=moved_s[0 : P - 16].rearrange("p l j -> p (l j)").bitcast(I32),
            in_=picked_s[16:P].rearrange("p l j -> p (l j)").bitcast(I32),
        )
        part_words(SOURCE, 0, picks[SOURCE], sb("early_parted0", [P, PASSES, 2 * HALF], U8))
        quantize_wc(0, 0, N)
        part_words(TARGET, 0, picks[TARGET], at("early_parted1", [P, PASSES, 2 * HALF], U8, EARLY_TARGET_PARTED_AT))
        picks = [at("late_pick%d" % l, [P, HALF], U32, LATE_PICK_AT[l]) for l in (SOURCE, TARGET)]
        gather_words(SOURCE, 1, picks[SOURCE])
        quantize_wc(1, 0, N // 2)
        gather_words(TARGET, 1, picks[TARGET])
        quantize_wc(1, N // 2, N)
        part_words(SOURCE, 1, picks[SOURCE], at("late_parted0", [P, PASSES, 2 * HALF], U8, LATE_SOURCE_PARTED_AT))
        part_words(TARGET, 1, picks[TARGET], sb("late_parted1", [P, PASSES, 2 * HALF], U8))
        for t, offset in zip((2, 3), LATE_PAGES_AT):
            pages[t] = at("page%d" % t, [P, T], F32, offset)
            nc.gpsimd.memset(pages[t][:], 0.0)

        def words(l, a, j0, w):
            h, first = divmod(j0, HALF)
            return v_w[l][h][:, a, 2 * first : 2 * (first + w)].bitcast(FP4X4)

        def message_pass(out, a, b, n0, n1, start, stop):
            nc.tensor.matmul_mx(
                out=out,
                lhsT=words(SOURCE, a, b * P, P),
                lhsT_scale=v_s[a][:, SOURCE, b * P : (b + 1) * P],
                rhs=wc_q[a][:, n0:n1].bitcast(FP8X4),
                rhs_scale=wc_s[a][:, n0:n1],
                start=start,
                stop=stop,
            )

        def message_pair(acc, a, b0, n0):
            for e in range(2):
                message_pass(
                    acc[:, e * QUARTER : (e + 1) * QUARTER], a, b0 + e, n0, n0 + QUARTER, a == 0 and e == 0, a == 1 and e == 1
                )

        def weigh(out, in_, b):
            nc.scalar.activation(out=out, in_=in_, func=COPY, scale=wgo_col[:, b : b + 1])

        def gate_passes(acc, w, t, j0, width):
            l = (TARGET, SOURCE)[w]
            for a in range(PASSES):
                if w == WB:
                    stationary = wb_q[:, a, 2 * t * P : 2 * (t + 1) * P].bitcast(FP4X4)
                else:
                    stationary = wa_q[:, a, t * P : (t + 1) * P].bitcast(FP8X4)
                nc.tensor.matmul_mx(
                    out=acc[:, 0:width],
                    lhsT=stationary,
                    lhsT_scale=w_s[:, a, w, t * P : (t + 1) * P],
                    rhs=words(l, a, j0, width),
                    rhs_scale=v_s[a][:, l, j0 : j0 + width],
                    start=(w == WB and a == 0),
                    stop=(w == WA and a == PASSES - 1),
                )

        def gate(out, t, j0, width, number):
            acc = bank("gate_ps%d_%d" % (t, j0), number)
            for w in (WB, WA):
                gate_passes(acc, w, t, j0, width)
            nc.scalar.activation(out=out, in_=acc[:, 0:width], func=SIGMOID)

        def turn(out, rows, name, number):
            turned = bank(name, number)
            for e, block in enumerate(rows):
                nc.tensor.transpose(turned[:, e * P : (e + 1) * P], block, ident[:])
            nc.scalar.copy(out=out, in_=turned[:, 0 : len(rows) * P])

        def scatter(t, j0, j1, eta, msg):
            nc.vector.tensor_tensor(pages[t][:].indirect(lists[TARGET][:, j0 // 16 : j1 // 16]), eta, msg, MULT)

        sums = [bank("msg_ps_a", 0), bank("msg_ps_b", 1)]
        gates = [bank("gate_ps0_0", 2), bank("gate_ps1_0", 3)]
        for q in range(2):
            message_pair(sums[q], 0, 2 * q, 0)
        for t in range(2):
            gate_passes(gates[t], WB, t, 0, QUARTER)
        for q in range(2):
            message_pair(sums[q], 1, 2 * q, 0)
        for t in range(2):
            gate_passes(gates[t], WA, t, 0, QUARTER)
        for t in range(2):
            rows = at("first_rows%d" % t, [P, 2, P], F32, FIRST_ROWS_AT[t])
            eta = sb("eta0_0", [P, QUARTER], F32) if t == 0 else at("eta1_0", [P, QUARTER], F32, FIRST_ROWS_AT[0])
            msg = sb("msg%d_0" % t, [P, QUARTER], F32)
            for b in range(2):
                weigh(rows[:, b, :], sums[0][:, b * QUARTER + t * P : b * QUARTER + (t + 1) * P], b)
            nc.scalar.activation(out=eta[:], in_=gates[t][:, 0:QUARTER], func=SIGMOID)
            turn(msg[:], [rows[:, b, :] for b in range(2)], "turn_ps%d_0" % t, 4 + t)
            scatter(t, 0, QUARTER, eta[:], msg[:])
        rows = at("second_rows", [P, 2, QUARTER], F32, FIRST_ROWS_AT[1])
        for b in range(2):
            weigh(rows[:, b, :], sums[1][:, b * QUARTER : (b + 1) * QUARTER], 2 + b)
        for t in range(2):
            eta = sb("eta%d_1" % t, [P, QUARTER], F32)
            msg = sb("msg%d_1" % t, [P, QUARTER], F32)
            gate(eta[:], t, QUARTER, QUARTER, (2, 4)[t])
            turn(msg[:], [rows[:, b, t * P : (t + 1) * P] for b in range(2)], "turn_ps%d_1" % t, 6 + t)
            scatter(t, QUARTER, HALF, eta[:], msg[:])
        def message_rows(rows, b0, n0, numbers):
            for q, number in enumerate(numbers):
                acc = bank("msg_ps%d_%d" % (b0 + 2 * q, n0), number)
                for a in range(PASSES):
                    message_pair(acc, a, b0 + 2 * q, n0)
                for e in range(2):
                    weigh(rows[:, 2 * q + e, :], acc[:, e * QUARTER : (e + 1) * QUARTER], b0 + 2 * q + e)

        late_rows = at("late_rows", [P, 5, QUARTER], F32, LATE_ROWS_AT)
        message_rows(late_rows, 4, 0, (0, 3))
        for t in range(2):
            eta = sb("eta%d_2" % t, [P, HALF], F32)
            msg = sb("msg%d_2" % t, [P, HALF], F32)
            gate(eta[:], t, HALF, HALF, (5, 1)[t])
            turn(msg[:], [late_rows[:, b, t * P : (t + 1) * P] for b in range(4)], "turn_ps%d_2" % t, (2, 4)[t])
            scatter(t, HALF, J, eta[:], msg[:])
        sums = [bank("msg_ps_other%d" % q, number) for q, number in enumerate((6, 7, 5, 2))]
        for q in range(4):
            for a in range(PASSES):
                message_pair(sums[q], a, 2 * q, QUARTER)

        def weigh_page(t):
            rows = at("other_rows%d" % t, [P, 8 * (4 - t), P], F32, OTHER_ROWS_AT[t - 2])
            for b in range(8):
                first = (b % 2) * QUARTER + (t - 2) * P
                weigh(rows[:, b, :], sums[b // 2][:, first : first + P], b)
            return rows

        def whole_page(t, rows, turn_banks):
            eta = sb("eta%d" % t, [P, J], F32)
            msg = sb("msg%d" % t, [P, J], F32)
            for h in range(2):
                gate(eta[:, h * HALF : (h + 1) * HALF], t, h * HALF, HALF, (1, 4)[h])
            for h in range(2):
                blocks = [rows[:, 4 * h + b, :] for b in range(4)]
                turn(msg[:, h * HALF : (h + 1) * HALF], blocks, "turn_ps%d_%d" % (t, h), turn_banks[h])
            return eta, msg

        operands = [whole_page(2, weigh_page(2), (0, 3))]
        last_rows = weigh_page(3)
        out_rows = out_0.rearrange("(p t) c -> p t c", t=PACK)
        y16 = {c0: sb("y16_%d" % c0, [P, w, PACK], BF16) for c0, w in ((VECTOR_START, VECTOR_COLS),) + PAIRED_CHUNKS + SCALAR_CHUNKS}
        y_q = sb("y_q", [P, T], U32)
        y_s = sb("y_s", [P, SCALE_COLS], U8)
        vector_cols = slice(VECTOR_START, VECTOR_START + VECTOR_COLS)
        low_v = at("low_v", [P, 2, VECTOR_COLS], BF16, LOW_V_AT)
        low_s = at("low_s", [P, 3, SCALAR_COLS], BF16, LOW_S_AT)
        pairs = {c0: at("pairs%d" % c0, [P, 2, w, 2], BF16, offset) for (c0, w), offset in zip(PAIRED_CHUNKS, PAIRS_AT)}

        def round_into_pairs(t, c0, w):
            nc.scalar.copy(out=pairs[c0][:, t // 2, :, t % 2], in_=pages[t][:, c0 : c0 + w])

        def finish_page(t):
            nc.sync.dma_start(out=out_rows[:, t, :], in_=pages[t][:])
            if t < 2:
                nc.scalar.copy(out=low_v[:, t, :], in_=pages[t][:, vector_cols])
            if t == 1:
                nc.scalar.copy(
                    out=y16[VECTOR_START][:, :, 0:2].rearrange("p (c e) t -> p c t e", e=4),
                    in_=low_v[:].rearrange("p t (c e) -> p c t e", e=4),
                )
            if t == 2:
                nc.scalar.copy(out=high_v[:, 0, :], in_=pages[2][:, vector_cols])
            if t < 3:
                nc.scalar.copy(out=low_s[:, t, :], in_=pages[t][:, 0:SCALAR_COLS])
                for c0, w in PAIRED_CHUNKS:
                    round_into_pairs(t, c0, w)
            if t == 2:
                for c0, w in SCALAR_CHUNKS:
                    nc.scalar.copy(
                        out=y16[c0][:, :, 0:3].rearrange("p (c e) t -> p c t e", e=4),
                        in_=low_s[:, :, c0 : c0 + w].rearrange("p t (c e) -> p c t e", e=4),
                    )

        finish_page(0)
        operands.append(whole_page(3, last_rows, (6, 7)))
        finish_page(1)
        high_v = at("high_v", [P, 2, VECTOR_COLS], BF16, HIGH_V_AT)
        for t, (eta, msg) in zip((2, 3), operands):
            scatter(t, 0, J, eta[:], msg[:])
            finish_page(t)

        codes_out = out_1[0].rearrange("p t b -> p (t b)").bitcast(I32)

        def quantize_out(c0, piece):
            col = c0 + piece * PIECE
            k, first = divmod(col, SCALE_COLS)
            nc.vector.quantize_mx(
                out=y_q[:, col : col + PIECE].bitcast(FP8X4),
                scales=y_s[4 * k : P, first : first + PIECE],
                in_=y16[c0][:, piece * PIECE : (piece + 1) * PIECE, :].rearrange("p c t -> p (c t)"),
            )

        def store_codes(c0, c1):
            nc.sync.dma_start(out=codes_out[:, c0:c1], in_=y_q[:, c0:c1].bitcast(I32))

        for c0, w in PAIRED_CHUNKS:
            round_into_pairs(3, c0, w)
        for c0, w in SCALAR_CHUNKS:
            nc.scalar.copy(out=y16[c0][:, :, 3], in_=pages[3][:, c0 : c0 + w])
        nc.vector.tensor_copy(out=high_v[:, 1, :], in_=pages[3][:, vector_cols])
        nc.vector.tensor_copy(out=y16[VECTOR_START][:, :, 2:4], in_=high_v[:].rearrange("p t c -> p c t"))
        for c0, w in PAIRED_CHUNKS:
            nc.vector.tensor_copy(
                out=y16[c0][:].rearrange("p c t -> p (c t)").bitcast(I32).rearrange("p (c r) -> p c r", r=2),
                in_=pairs[c0][:].rearrange("p r c e -> p (r c e)").bitcast(I32).rearrange("p (r c) -> p c r", r=2),
            )
            if c0 == vector_cols.stop:
                quantize_out(VECTOR_START, 0)
                quantize_out(c0, 0)
                store_codes(VECTOR_START, c0 + PIECE)
        for c0, w in PAIRED_CHUNKS + SCALAR_CHUNKS:
            for piece in range(1 if c0 == vector_cols.stop else 0, w // PIECE):
                quantize_out(c0, piece)
            store_codes(c0 + PIECE if c0 == vector_cols.stop else c0, c0 + w)
        scale_rows = out_2[0].bitcast(I32).rearrange("(q r) (k c) -> q k r c", r=4, k=T // SCALE_COLS)
        for q in range(4):
            (nc.scalar, nc.sync)[q % 2].dma_start(out=scale_rows[q], in_=y_s[32 * q : 32 * q + 16, :].bitcast(I32))
